import numpy as np
import ml_dtypes


def mxq(x, axis, fmt="e4m3"):
    dtype, down = {"e4m3": (ml_dtypes.float8_e4m3fn, 7), "e5m2": (ml_dtypes.float8_e5m2, 14)}[fmt]
    v = np.moveaxis(np.asarray(x, np.float32).astype(ml_dtypes.bfloat16).astype(np.float64), axis, -1)
    blocks = v.reshape(v.shape[:-1] + (-1, 32))
    amax = np.abs(blocks).max(-1, keepdims=True)
    byte = np.maximum(np.where(amax > 0, np.frexp(amax)[1] - 1 + 127, 0) - down, 1)
    scale = np.exp2(byte - 127.0)
    codes = (blocks / scale).astype(np.float32).astype(dtype).astype(np.float64)
    return np.moveaxis((codes * scale).reshape(v.shape), -1, axis)


WIDE = False


def mx_kscale(k):
    if not WIDE:
        return np.ones(k)
    levels = np.array([24, -24, 12, -12, 0])
    if k % 512:
        return np.exp2(np.random.permutation(np.resize(levels, k // 32))).repeat(32)
    a = np.empty((k // 512, 16))
    for p in range(k // 512):
        a[p, :8] = np.random.permutation(np.resize(levels, 8))
        for g in range(8):
            far = levels[np.abs(levels - a[p, g]) >= 10]
            a[p, g + 8] = far[np.random.randint(len(far))]
    return np.exp2(a.ravel()).repeat(32)


def f64(x):
    return np.asarray(x).astype(np.float64)


def striped(idx):
    return np.tile(idx.reshape(-1, 16).T, (8, 1)).astype(np.uint16)


def unstriped(offs):
    return offs[:16].T.reshape(-1).astype(np.int64)


E2M1 = np.array([0.0, 0.5, 1.0, 1.5, 2.0, 3.0, 4.0, 6.0, -0.0, -0.5, -1.0, -1.5, -2.0, -3.0, -4.0, -6.0])


def pack_weight(w, fmt):
    k, n = w.shape
    w = f64(np.asarray(w, np.float32).astype(ml_dtypes.bfloat16)).reshape(k // 32, 32, n)
    amax = np.abs(w).max(1)
    if fmt == "e4m3":
        byte = np.frexp(amax)[1] - 1 + 127 - 7
    else:
        mant, ex = np.frexp(amax / 6.0)
        byte = np.where(mant > 0.5, ex, ex - 1) + 127
    byte = np.clip(np.where(amax > 0, byte, 1), 1, 254)
    scaled = (w * np.exp2(127.0 - byte)[:, None, :]).reshape(k, n).astype(np.float32)
    by_word = np.ascontiguousarray(scaled.reshape(k // 512, 128, 4, n).transpose(0, 1, 3, 2))
    if fmt == "e4m3":
        words = by_word.astype(ml_dtypes.float8_e4m3fn).view(np.uint8)
    else:
        c = by_word.astype(ml_dtypes.float4_e2m1fn).view(np.uint8) & 0xF
        words = (c[..., 0::2] | (c[..., 1::2] << 4)).reshape(k // 512, 128, 2 * n)
    return np.ascontiguousarray(words), np.ascontiguousarray(byte.astype(np.uint8).reshape(k // 512, 16, n))


def unpack_weight(words, scales, fmt):
    g, _, n = scales.shape
    words = np.ascontiguousarray(words).reshape(g, 128, n, -1)
    if fmt == "e4m3":
        vals = words.view(ml_dtypes.float8_e4m3fn).astype(np.float64)
    else:
        nib = np.empty((g, 128, n, 4), np.uint8)
        nib[..., 0::2] = words & 0xF
        nib[..., 1::2] = words >> 4
        vals = E2M1[nib]
    vals = vals * np.repeat(np.exp2(scales.astype(np.float64) - 127.0), 8, axis=1)[..., None]
    return vals.transpose(0, 1, 3, 2).reshape(g * 512, n)


def planes(y):
    n, m = y.shape
    v = y.astype(np.float32).astype(ml_dtypes.bfloat16).astype(np.float64).reshape(n // 32, 32, m)
    top = np.abs(v).max(1)
    byte = np.clip(np.where(top > 0, np.frexp(top)[1] - 1 + 127 - 7, 1), 1, 254)
    codes = (v * np.exp2(127.0 - byte)[:, None, :]).reshape(n, m).astype(np.float32).astype(ml_dtypes.float8_e4m3fn).view(np.uint8)
    words = codes.reshape(n // 512, 128, 4, m).transpose(0, 1, 3, 2)
    return np.ascontiguousarray(words), np.ascontiguousarray(byte.astype(np.uint8).reshape(n // 512, 16, m))


def sigm(f):
    return 1.0 / (1.0 + np.exp(-np.maximum(f, -700.0)))


K, M, N, T, J = 1024, 512, 512, 2048, 1024


def setup_inputs():
    n = np.random.standard_normal
    s = mx_kscale(K)[:, None]
    s2 = mx_kscale(M)[:, None]
    h = np.tanh(n((N, T)))
    p_tab = pack_weight(h * s2, "e4m3")
    p_wz = pack_weight(n((K, N)) / np.sqrt(K) / s, "e2m1")
    p_wn = pack_weight(n((K, N)) / np.sqrt(K) / s, "e2m1")
    return {
        "x": (n((K, J)) * s).astype(np.float32),
        "tab_words": p_tab[0],
        "tab_scales": p_tab[1],
        "wz_words": p_wz[0],
        "wz_scales": p_wz[1],
        "uz": (n((M, N)) / np.sqrt(M) / s2).astype(np.float32),
        "wn_words": p_wn[0],
        "wn_scales": p_wn[1],
        "un": (n((M, N)) / np.sqrt(M) / s2).astype(np.float32),
        "bz": (0.3 * n(N)).astype(np.float32),
        "bn": (0.3 * n(N)).astype(np.float32),
        "hT": (h).astype(np.float32),
        "wgo": np.tile(np.random.uniform(0.5, 2.0, J), (128, 1)).astype(np.float32),
        "offs": striped(np.random.permutation(T)[:J]),
    }


def reference(x, tab_words, tab_scales, wz_words, wz_scales, uz, wn_words, wn_scales, un, bz, bn, hT, wgo, offs):
    idx = unstriped(offs)
    x_ = mxq(f64(x), 0, "e4m3")
    tab_ = unpack_weight(tab_words, tab_scales, "e4m3")[:, idx]
    wz_ = unpack_weight(wz_words, wz_scales, "e2m1")
    uz_ = mxq(f64(uz), 0, "e4m3")
    wn_ = unpack_weight(wn_words, wn_scales, "e2m1")
    un_ = mxq(f64(un), 0, "e4m3")
    sz = wz_.T @ x_ + uz_.T @ tab_
    z = sigm(sz + f64(bz)[:, None])
    sn = wn_.T @ x_ + un_.T @ tab_
    cd = np.tanh(sn + f64(bn)[:, None])
    out = np.zeros((N, T))
    out[:, idx] = f64(wgo)[0] * (f64(hT)[:, idx] + z * (cd - f64(hT)[:, idx]))
    return (out,) + planes(out)

@@ -1,0 +1,266 @@
+from contextlib import ExitStack
+
+import concourse.mybir as mybir
+
+K, M, N, T, J = 1024, 512, 512, 2048, 1024
+FLOPS = 2 * 2 * (K + M) * N * J
+
+F32 = mybir.dt.float32
+BF16 = mybir.dt.bfloat16
+I32 = mybir.dt.int32
+U32 = mybir.dt.uint32
+U16 = mybir.dt.uint16
+U8 = mybir.dt.uint8
+FP8X4 = mybir.dt.float8_e4m3fn_x4
+FP4X4 = mybir.dt.float4_e2m1fn_x4
+ACT = mybir.ActivationFunctionType
+ALU = mybir.AluOpType
+
+P = 128
+PACK = 4
+KP = P * PACK
+HALF = 512
+STEPS = [(0, 0), (1, 0), (2, 0), (0, 1), (1, 1), (2, 1), (3, 0), (3, 1)]
+ON_VECTOR = (0,)
+
+
+def tile_list_tgn_emaP_kernel(
+    tc, x, tab_words, tab_scales, wz_words, wz_scales, uz, wn_words, wn_scales, un, bz, bn, hT, wgo, offs,
+    out_0, out_1, out_2,
+):
+    nc = tc.nc
+    with ExitStack() as ctx:
+        keep = ctx.enter_context(tc.tile_pool(name="keep", bufs=1))
+        ring = ctx.enter_context(tc.tile_pool(name="ring", bufs=2))
+        psum = ctx.enter_context(tc.psum_pool(name="psum", bufs=8))
+
+        offsets = keep.tile([P, J // 16], U16, name="offsets")
+        tab_s = keep.tile([P, T], U8, name="tab_s", align_bytes=64)
+        w_s_raw = keep.tile([P, 2, 2, N], U8, name="w_s_raw", align_bytes=64)
+        w_raw = [keep.tile([P, 2, 2 * N], U8, name="w_raw%d" % w, tag="late%d" % w) for w in range(2)]
+        tab_w = keep.tile([P, T], U32, name="tab_w", align_bytes=64)
+        bias_n = keep.tile([P, PACK], F32, name="bias_n")
+        bias_z = [keep.tile([P, 1], F32, name="bias_z%d" % t) for t in range(PACK)]
+        neg_bz = [keep.tile([P, 1], F32, name="neg_bz%d" % t) for t in range(PACK)]
+        weight = [keep.tile([P, HALF], F32, name="weight%d" % h) for h in range(2)]
+        state = [keep.tile([P, T], F32, name="state%d" % t, tag="state%d" % t, align_bytes=64) for t in range(PACK)]
+        page = [keep.tile([P, T], F32, name="page%d" % t) for t in range(2)]
+
+        nc.vector.memset(tab_s[:].bitcast(I32), 0)
+        nc.vector.memset(w_s_raw[:].rearrange("p w a n -> p (w a n)").bitcast(I32), 0)
+        for t in range(2):
+            nc.vector.memset(page[t][:], 0.0)
+
+        def load_rows(tag, rows):
+            raw = keep.tile([P, PACK, HALF], F32, name=tag, tag=tag)
+            nc.sync.dma_start(raw[:], rows.rearrange("(p i) c -> p i c", i=PACK))
+            return raw
+
+        def load_state(t):
+            nc.sync.dma_start(state[t][:], hT.rearrange("(p t) c -> t p c", t=PACK)[t])
+
+        def load_bias_z(t):
+            nc.sync.dma_start(bias_z[t][:], bz.rearrange("(p t) -> p t", t=PACK)[:, t : t + 1])
+
+        def x_rows(a, half):
+            return x[a * KP : (a + 1) * KP, half * HALF : (half + 1) * HALF]
+
+        nc.sync.dma_start(offsets[:], offs)
+        for w, words in enumerate((wz_words, wn_words)):
+            nc.sync.dma_start(w_raw[w][:].bitcast(I32), words.rearrange("a p b -> p a b").bitcast(I32))
+        nc.sync.dma_start(tab_w[:].bitcast(I32), tab_words[0].rearrange("p t i -> p (t i)").bitcast(I32))
+        for q in range(4):
+            nc.sync.dma_start(tab_s[32 * q : 32 * q + 4, :].bitcast(I32), tab_scales[0, 4 * q : 4 * q + 4, :].bitcast(I32))
+        for w, scales in enumerate((wz_scales, wn_scales)):
+            for q in range(4):
+                nc.sync.dma_start(
+                    w_s_raw[32 * q : 32 * q + 4, w].bitcast(I32),
+                    scales[:, 4 * q : 4 * q + 4, :].rearrange("a r n -> r a n").bitcast(I32),
+                )
+        u_raw = [load_rows("raw%d" % w, u) for w, u in enumerate((uz, un))]
+        x_raw = {(a, 0): load_rows("raw%d" % (2 + a), x_rows(a, 0)) for a in range(2)}
+        nc.sync.dma_start(bias_n[:], bn.rearrange("(p t) -> p t", t=PACK))
+        load_bias_z(0)
+        load_state(0)
+        load_state(1)
+        nc.sync.dma_start(weight[0][:], wgo[:, 0:HALF])
+        load_state(2)
+        load_bias_z(1)
+
+        w_q = keep.tile([P, 2, 2, 2 * N], U8, name="w_q", align_bytes=64)
+        w_s = keep.tile([P, 2, 2, N], U8, name="w_s", align_bytes=64)
+        for w in range(2):
+            nc.vector.tensor_copy(
+                w_q[:, w].bitcast(U16).rearrange("p a (t m) -> p a t m", t=PACK),
+                w_raw[w][:].bitcast(U16).rearrange("p a (m t) -> p a t m", t=PACK),
+            )
+
+        for w in range(2):
+            page.append(keep.tile([P, T], F32, name="page%d" % (2 + w), tag="late%d" % w))
+            for c in range(4):
+                nc.gpsimd.memset(page[2 + w][:, c * HALF : (c + 1) * HALF], 0.0)
+
+        picked_w, picked_s = {}, {}
+
+        def pick_table(half):
+            cols = offsets[:, half * (HALF // 16) : (half + 1) * (HALF // 16)]
+            picked_w[half] = keep.tile([P, HALF], U32, name="picked_w%d" % half, align_bytes=64)
+            picked_s[half] = keep.tile([P, HALF], U8, name="picked_s%d" % half, align_bytes=64)
+            nc.vector.tensor_copy(picked_w[half][:], tab_w[:].indirect(cols))
+            nc.vector.tensor_copy(picked_s[half][:], tab_s[:].indirect(cols))
+
+        def quantize(grouped, tag, scale_name):
+            codes = keep.tile([P, HALF], U32, name=tag, tag=tag, align_bytes=64)
+            scales = keep.tile([P, HALF], U8, name=scale_name, align_bytes=64)
+            nc.vector.quantize_mx(codes[:].bitcast(FP8X4), scales[:], grouped[:])
+            return codes, scales
+
+        def round_u(copy, raw):
+            grouped = ring.tile([P, PACK * HALF], BF16, name="grouped", tag="grouped", align_bytes=64, bufs=3)
+            copy(
+                grouped[:].rearrange("p (t m i) -> p m i t", t=PACK, i=PACK),
+                raw[:].rearrange("p i (m t) -> p m i t", t=PACK),
+            )
+            return grouped
+
+        def round_x(copy, raw):
+            grouped = ring.tile([P, PACK * HALF], BF16, name="grouped", tag="grouped", align_bytes=64, bufs=3)
+            copy(
+                grouped[:].rearrange("p (c e i) -> p c i e", e=4, i=PACK),
+                raw[:].rearrange("p i (c e) -> p c i e", e=4),
+            )
+            return grouped
+
+        pick_table(0)
+        g_uz = round_u(nc.scalar.copy, u_raw[0])
+        pick_table(1)
+        u_q = [quantize(g_uz, "uz_q", "uz_s")]
+        g_un = round_u(nc.scalar.copy, u_raw[1])
+        nc.vector.tensor_copy(
+            w_s[:].rearrange("p w a (t m) -> p (w a) t m", t=PACK),
+            w_s_raw[:].rearrange("p w a (m t) -> p (w a) t m", t=PACK),
+        )
+        u_q.append(quantize(g_un, "un_q", "un_s"))
+        g_x0 = round_x(nc.scalar.copy, x_raw[0, 0])
+        g_x1 = round_x(nc.vector.tensor_copy, x_raw[1, 0])
+        x_q = {(0, 0): quantize(g_x0, "xq0", "xs0"), (1, 0): quantize(g_x1, "xq1", "xs1")}
+        QUARTER = HALF // 2
+        late_raw = []
+        for piece in range(4):
+            a, c0 = piece // 2, HALF + (piece % 2) * QUARTER
+            raw = keep.tile([P, PACK, QUARTER], F32, name="late_raw%d" % piece, tag="raw%d" % piece)
+            nc.sync.dma_start(raw[:], x[a * KP : (a + 1) * KP, c0 : c0 + QUARTER].rearrange("(p i) c -> p i c", i=PACK))
+            late_raw.append(raw)
+        load_bias_z(2)
+        load_state(3)
+        load_bias_z(3)
+        nc.sync.dma_start(weight[1][:], wgo[:, HALF:J])
+
+        def gate(w, t, half):
+            bank = psum.tile([P, HALF], F32, name="bank", tag="bank")
+            cols = slice(t * P, (t + 1) * P)
+            nc.tensor.matmul_mx(
+                bank[:], lhsT=u_q[w][0][:, cols].bitcast(FP8X4), lhsT_scale=u_q[w][1][:, cols],
+                rhs=picked_w[half][:].bitcast(FP8X4), rhs_scale=picked_s[half][:], start=True, stop=False,
+            )
+            for a in range(2):
+                nc.tensor.matmul_mx(
+                    bank[:], lhsT=w_q[:, w, a, 2 * t * P : 2 * (t + 1) * P].bitcast(FP4X4),
+                    lhsT_scale=w_s[:, w, a, cols],
+                    rhs=x_q[a, half][0][:].bitcast(FP8X4), rhs_scale=x_q[a, half][1][:], start=False, stop=(a == 1),
+                )
+            if w == 1:
+                res = ring.tile([P, HALF], F32, name="cand", tag="cand", bufs=8)
+                nc.scalar.activation(res[:], bank[:], ACT.Tanh, bias=bias_n[:, t : t + 1])
+            else:
+                if half == 0:
+                    nc.scalar.mul(neg_bz[t][:], bias_z[t][:], -1.0)
+                res = ring.tile([P, HALF], F32, name="hold", tag="hold", bufs=8)
+                nc.scalar.activation(res[:], bank[:], ACT.Sigmoid, bias=neg_bz[t][:], scale=-1.0)
+            return res
+
+        cands, holds = {}, {}
+        for step, (t, half) in enumerate(STEPS):
+            if half == 1 and (0, 1) not in x_q:
+                for a in range(2):
+                    codes = keep.tile([P, HALF], U32, name="xq_late", tag="xq%d" % (2 + a), align_bytes=64)
+                    scales = keep.tile([P, HALF], U8, name="xs%d" % (2 + a), align_bytes=64)
+                    x_q[a, 1] = codes, scales
+                    for part in range(2):
+                        grouped = ring.tile([P, PACK * QUARTER], BF16, name="grouped", tag="grouped", align_bytes=64, bufs=3)
+                        nc.scalar.copy(
+                            grouped[:].rearrange("p (c e i) -> p c i e", e=4, i=PACK),
+                            late_raw[2 * a + part][:].rearrange("p i (c e) -> p c i e", e=4),
+                        )
+                        cols = slice(part * QUARTER, (part + 1) * QUARTER)
+                        nc.vector.quantize_mx(codes[:, cols].bitcast(FP8X4), scales[:, cols], grouped[:])
+            cands[step] = gate(1, t, half)
+            if step > 1:
+                holds[step - 1] = gate(0, *STEPS[step - 1])
+            if step in (0, len(STEPS) - 1):
+                holds[step] = gate(0, t, half)
+
+        def blend(step):
+            t, half = STEPS[step]
+            cand, hold = cands[step], holds[step]
+            cols = offsets[:, half * (HALF // 16) : (half + 1) * (HALF // 16)]
+            mix = ring.tile([P, HALF], F32, name="mix", tag="mix")
+            engine = nc.vector if step in ON_VECTOR else nc.gpsimd
+            nc.vector.tensor_tensor(mix[:], state[t][:].indirect(cols), cand[:], ALU.subtract)
+            engine.tensor_tensor(mix[:], mix[:], hold[:], ALU.mult)
+            engine.tensor_tensor(mix[:], mix[:], cand[:], ALU.add)
+            engine.tensor_tensor(mix[:], mix[:], weight[half][:], ALU.mult)
+            return mix
+
+        SPLIT = 1280
+        planes_s = keep.tile([P, PACK - 1, SPLIT], BF16, name="planes_s", tag="xq2", align_bytes=64)
+        planes_v = keep.tile([P, PACK, T - SPLIT], BF16, name="planes_v", tag="xq3", align_bytes=64)
+        PARTS = [(0, 512, "state0"), (512, 1024, "state1"), (1024, SPLIT, "part2"), (1536, T, "state2"), (SPLIT, 1536, "part4")]
+        rounded = {}
+
+        def weave(copy, part, planes, first, slots):
+            lo, hi, tag = part
+            rounded[part] = keep.tile([P, hi - lo, PACK], BF16, name="rounded", tag=tag, align_bytes=64)
+            copy(
+                rounded[part][:, :, 0:slots].rearrange("p (c e) t -> p c t e", e=4),
+                planes[:, 0:slots, lo - first : hi - first].rearrange("p t (c e) -> p c t e", e=4),
+            )
+
+        y_s = keep.tile([P, T], U8, name="y_s", align_bytes=64)
+        words_out = out_1[0].rearrange("p t i -> p (t i)").bitcast(I32)
+
+        def emit(part):
+            lo, hi, tag = part
+            y_w = keep.tile([P, hi - lo], U32, name="y_w%d" % lo, align_bytes=64)
+            nc.vector.quantize_mx(y_w[:].bitcast(FP8X4), y_s[:, lo:hi], rounded[part][:].rearrange("p c t -> p (c t)"))
+            nc.sync.dma_start(words_out[:, lo:hi], y_w[:].bitcast(I32))
+
+        def place(step, mix):
+            t, half = STEPS[step]
+            cols = offsets[:, half * (HALF // 16) : (half + 1) * (HALF // 16)]
+            nc.vector.tensor_copy(page[t][:].indirect(cols), mix[:])
+            if half == 1:
+                nc.sync.dma_start(out_0.rearrange("(p t) c -> t p c", t=PACK)[t], page[t][:])
+                if t < PACK - 1:
+                    nc.scalar.copy(planes_s[:, t, :], page[t][:, 0:SPLIT])
+                    nc.scalar.copy(planes_v[:, t, :], page[t][:, SPLIT:T])
+                if t == PACK - 2:
+                    for part in PARTS[:3]:
+                        weave(nc.scalar.copy, part, planes_s, 0, PACK - 1)
+                if t == PACK - 1:
+                    for part in PARTS[:3]:
+                        nc.scalar.copy(rounded[part][:, :, t], page[t][:, part[0] : part[1]])
+                    nc.vector.tensor_copy(planes_v[:, t, :], page[t][:, SPLIT:T])
+                    for part in PARTS[3:]:
+                        weave(nc.vector.tensor_copy, part, planes_v, SPLIT, PACK)
+                    for part in PARTS[3:] + PARTS[:3]:
+                        emit(part)
+
+        mix = blend(0)
+        for step in range(len(STEPS)):
+            ahead = blend(step + 1) if step + 1 < len(STEPS) else None
+            place(step, mix)
+            mix = ahead
+
+        for q in range(4):
+            nc.sync.dma_start(out_2[0, 4 * q : 4 * q + 4, :].bitcast(I32), y_s[32 * q : 32 * q + 4, :].bitcast(I32))

@@ -20,8 +20,8 @@ P = 128
 PACK = 4
 KP = P * PACK
 HALF = 512
-STEPS = [(0, 0), (1, 0), (2, 0), (0, 1), (1, 1), (2, 1), (3, 0), (3, 1)]
-ON_VECTOR = (0,)
+QUARTER = HALF // 2
+STEPS = [(0, 0, QUARTER), (1, 0, QUARTER), (0, QUARTER, HALF), (1, QUARTER, HALF), (2, 0, HALF), (0, HALF, J), (1, HALF, J), (2, HALF, J), (3, 0, HALF), (3, HALF, J)]
 
 
 def tile_list_tgn_emaP_kernel(
@@ -40,8 +40,8 @@ def tile_list_tgn_emaP_kernel(
         w_raw = [keep.tile([P, 2, 2 * N], U8, name="w_raw%d" % w, tag="late%d" % w) for w in range(2)]
         tab_w = keep.tile([P, T], U32, name="tab_w", align_bytes=64)
         bias_n = keep.tile([P, PACK], F32, name="bias_n")
-        bias_z = [keep.tile([P, 1], F32, name="bias_z%d" % t) for t in range(PACK)]
-        neg_bz = [keep.tile([P, 1], F32, name="neg_bz%d" % t) for t in range(PACK)]
+        bias_z = keep.tile([P, PACK], F32, name="bias_z")
+        neg_bz = keep.tile([P, PACK], F32, name="neg_bz")
         weight = [keep.tile([P, HALF], F32, name="weight%d" % h) for h in range(2)]
         state = [keep.tile([P, T], F32, name="state%d" % t, tag="state%d" % t, align_bytes=64) for t in range(PACK)]
         page = [keep.tile([P, T], F32, name="page%d" % t) for t in range(2)]
@@ -52,40 +52,49 @@ def tile_list_tgn_emaP_kernel(
             nc.vector.memset(page[t][:], 0.0)
 
         def load_rows(tag, rows):
-            raw = keep.tile([P, PACK, HALF], F32, name=tag, tag=tag)
+            raw = keep.tile([P, PACK, rows.shape[1]], F32, name=tag, tag=tag)
             nc.sync.dma_start(raw[:], rows.rearrange("(p i) c -> p i c", i=PACK))
             return raw
 
         def load_state(t):
             nc.sync.dma_start(state[t][:], hT.rearrange("(p t) c -> t p c", t=PACK)[t])
 
-        def load_bias_z(t):
-            nc.sync.dma_start(bias_z[t][:], bz.rearrange("(p t) -> p t", t=PACK)[:, t : t + 1])
+        x_raw = {}
 
-        def x_rows(a, half):
-            return x[a * KP : (a + 1) * KP, half * HALF : (half + 1) * HALF]
+        def load_x(tag, a, lo, hi):
+            x_raw[a, lo] = load_rows(tag, x[a * KP : (a + 1) * KP, lo:hi])
+
+        def load_tab_scales(q):
+            nc.sync.dma_start(tab_s[32 * q : 32 * q + 4, :].bitcast(I32), tab_scales[0, 4 * q : 4 * q + 4, :].bitcast(I32))
+
+        def load_w_scales(k):
+            w, q = divmod(k, 4)
+            (nc.sync, nc.gpsimd)[w].dma_start(
+                w_s_raw[32 * q : 32 * q + 4, w].bitcast(I32),
+                (wz_scales, wn_scales)[w][:, 4 * q : 4 * q + 4, :].rearrange("a r n -> r a n").bitcast(I32),
+            )
 
         nc.sync.dma_start(offsets[:], offs)
-        for w, words in enumerate((wz_words, wn_words)):
-            nc.sync.dma_start(w_raw[w][:].bitcast(I32), words.rearrange("a p b -> p a b").bitcast(I32))
         nc.sync.dma_start(tab_w[:].bitcast(I32), tab_words[0].rearrange("p t i -> p (t i)").bitcast(I32))
         for q in range(4):
-            nc.sync.dma_start(tab_s[32 * q : 32 * q + 4, :].bitcast(I32), tab_scales[0, 4 * q : 4 * q + 4, :].bitcast(I32))
-        for w, scales in enumerate((wz_scales, wn_scales)):
-            for q in range(4):
-                nc.sync.dma_start(
-                    w_s_raw[32 * q : 32 * q + 4, w].bitcast(I32),
-                    scales[:, 4 * q : 4 * q + 4, :].rearrange("a r n -> r a n").bitcast(I32),
-                )
-        u_raw = [load_rows("raw%d" % w, u) for w, u in enumerate((uz, un))]
-        x_raw = {(a, 0): load_rows("raw%d" % (2 + a), x_rows(a, 0)) for a in range(2)}
-        nc.sync.dma_start(bias_n[:], bn.rearrange("(p t) -> p t", t=PACK))
-        load_bias_z(0)
+            load_tab_scales(q)
+        for k in range(4, 8):
+            load_w_scales(k)
+        u_raw = {1: load_rows("raw1", un), 0: load_rows("raw0", uz)}
+        for w, words in enumerate((wz_words, wn_words)):
+            nc.sync.dma_start(w_raw[w][:].bitcast(I32), words.rearrange("a p b -> p a b").bitcast(I32))
+        load_x("raw2", 0, 0, QUARTER)
+        load_x("raw3", 1, 0, QUARTER)
+        for k in range(4):
+            load_w_scales(k)
         load_state(0)
-        load_state(1)
+        nc.sync.dma_start(bias_n[:], bn.rearrange("(p t) -> p t", t=PACK))
+        nc.sync.dma_start(bias_z[:], bz.rearrange("(p t) -> p t", t=PACK))
         nc.sync.dma_start(weight[0][:], wgo[:, 0:HALF])
-        load_state(2)
-        load_bias_z(1)
+        load_x("raw4", 0, QUARTER, HALF)
+        load_x("raw5", 1, QUARTER, HALF)
+        load_state(1)
+        nc.scalar.mul(neg_bz[:], bias_z[:], -1.0)
 
         w_q = keep.tile([P, 2, 2, 2 * N], U8, name="w_q", align_bytes=64)
         w_s = keep.tile([P, 2, 2, N], U8, name="w_s", align_bytes=64)
@@ -123,94 +132,84 @@ def tile_list_tgn_emaP_kernel(
             )
             return grouped
 
-        def round_x(copy, raw):
-            grouped = ring.tile([P, PACK * HALF], BF16, name="grouped", tag="grouped", align_bytes=64, bufs=3)
+        x_q = {}
+
+        def quantize_x(copy, a, lo):
+            raw = x_raw[a, lo]
+            width = raw.shape[2]
+            half, first = divmod(lo, HALF)
+            if first == 0:
+                x_q[a, half] = (
+                    keep.tile([P, HALF], U32, name="x_codes", tag="xq%d" % (2 * half + a), align_bytes=64),
+                    keep.tile([P, HALF], U8, name="x_scales%d" % (2 * half + a), align_bytes=64),
+                )
+            grouped = ring.tile([P, PACK * width], BF16, name="grouped", tag="grouped", align_bytes=64, bufs=3)
             copy(
                 grouped[:].rearrange("p (c e i) -> p c i e", e=4, i=PACK),
                 raw[:].rearrange("p i (c e) -> p c i e", e=4),
             )
-            return grouped
+            codes, scales = x_q[a, half]
+            cols = slice(first, first + width)
+            nc.vector.quantize_mx(codes[:, cols].bitcast(FP8X4), scales[:, cols], grouped[:])
 
         pick_table(0)
-        g_uz = round_u(nc.scalar.copy, u_raw[0])
         pick_table(1)
-        u_q = [quantize(g_uz, "uz_q", "uz_s")]
-        g_un = round_u(nc.scalar.copy, u_raw[1])
+        u_q = {1: quantize(round_u(nc.scalar.copy, u_raw[1]), "un_q", "un_s")}
         nc.vector.tensor_copy(
             w_s[:].rearrange("p w a (t m) -> p (w a) t m", t=PACK),
             w_s_raw[:].rearrange("p w a (m t) -> p (w a) t m", t=PACK),
         )
-        u_q.append(quantize(g_un, "un_q", "un_s"))
-        g_x0 = round_x(nc.scalar.copy, x_raw[0, 0])
-        g_x1 = round_x(nc.vector.tensor_copy, x_raw[1, 0])
-        x_q = {(0, 0): quantize(g_x0, "xq0", "xs0"), (1, 0): quantize(g_x1, "xq1", "xs1")}
-        QUARTER = HALF // 2
-        late_raw = []
-        for piece in range(4):
-            a, c0 = piece // 2, HALF + (piece % 2) * QUARTER
-            raw = keep.tile([P, PACK, QUARTER], F32, name="late_raw%d" % piece, tag="raw%d" % piece)
-            nc.sync.dma_start(raw[:], x[a * KP : (a + 1) * KP, c0 : c0 + QUARTER].rearrange("(p i) c -> p i c", i=PACK))
-            late_raw.append(raw)
-        load_bias_z(2)
-        load_state(3)
-        load_bias_z(3)
+        u_q[0] = quantize(round_u(nc.scalar.copy, u_raw[0]), "uz_q", "uz_s")
+        quantize_x(nc.scalar.copy, 0, 0)
+        quantize_x(nc.vector.tensor_copy, 1, 0)
+        load_x("raw1", 0, HALF, J)
+        load_x("raw0", 1, HALF, J)
+        load_state(2)
         nc.sync.dma_start(weight[1][:], wgo[:, HALF:J])
+        load_state(3)
 
-        def gate(w, t, half):
-            bank = psum.tile([P, HALF], F32, name="bank", tag="bank")
+        def gate(w, t, lo, hi):
+            half, first = divmod(lo, HALF)
+            width = hi - lo
+            bank = psum.tile([P, width], F32, name="bank", tag="bank")
             cols = slice(t * P, (t + 1) * P)
             nc.tensor.matmul_mx(
                 bank[:], lhsT=u_q[w][0][:, cols].bitcast(FP8X4), lhsT_scale=u_q[w][1][:, cols],
-                rhs=picked_w[half][:].bitcast(FP8X4), rhs_scale=picked_s[half][:], start=True, stop=False,
+                rhs=picked_w[half][:, first : first + width].bitcast(FP8X4), rhs_scale=picked_s[half][:, first : first + width],
+                start=True, stop=False,
             )
+            n = HALF if width == HALF else P
             for a in range(2):
-                nc.tensor.matmul_mx(
-                    bank[:], lhsT=w_q[:, w, a, 2 * t * P : 2 * (t + 1) * P].bitcast(FP4X4),
-                    lhsT_scale=w_s[:, w, a, cols],
-                    rhs=x_q[a, half][0][:].bitcast(FP8X4), rhs_scale=x_q[a, half][1][:], start=False, stop=(a == 1),
-                )
+                codes, scales = x_q[a, half]
+                for c in range(0, width, n):
+                    nc.tensor.matmul_mx(
+                        bank[:, c : c + n], lhsT=w_q[:, w, a, 2 * t * P : 2 * (t + 1) * P].bitcast(FP4X4),
+                        lhsT_scale=w_s[:, w, a, cols],
+                        rhs=codes[:, first + c : first + c + n].bitcast(FP8X4), rhs_scale=scales[:, first + c : first + c + n],
+                        start=False, stop=(a == 1 and c + n == width),
+                    )
             if w == 1:
-                res = ring.tile([P, HALF], F32, name="cand", tag="cand", bufs=8)
+                res = ring.tile([P, width], F32, name="cand", tag="cand", bufs=10)
                 nc.scalar.activation(res[:], bank[:], ACT.Tanh, bias=bias_n[:, t : t + 1])
             else:
-                if half == 0:
-                    nc.scalar.mul(neg_bz[t][:], bias_z[t][:], -1.0)
-                res = ring.tile([P, HALF], F32, name="hold", tag="hold", bufs=8)
-                nc.scalar.activation(res[:], bank[:], ACT.Sigmoid, bias=neg_bz[t][:], scale=-1.0)
+                res = ring.tile([P, width], F32, name="hold", tag="hold", bufs=10)
+                nc.scalar.activation(res[:], bank[:], ACT.Sigmoid, bias=neg_bz[:, t : t + 1], scale=-1.0)
             return res
 
         cands, holds = {}, {}
-        for step, (t, half) in enumerate(STEPS):
-            if half == 1 and (0, 1) not in x_q:
+        for step, (t, lo, hi) in enumerate(STEPS):
+            if t == 0 and lo > 0:
                 for a in range(2):
-                    codes = keep.tile([P, HALF], U32, name="xq_late", tag="xq%d" % (2 + a), align_bytes=64)
-                    scales = keep.tile([P, HALF], U8, name="xs%d" % (2 + a), align_bytes=64)
-                    x_q[a, 1] = codes, scales
-                    for part in range(2):
-                        grouped = ring.tile([P, PACK * QUARTER], BF16, name="grouped", tag="grouped", align_bytes=64, bufs=3)
-                        nc.scalar.copy(
-                            grouped[:].rearrange("p (c e i) -> p c i e", e=4, i=PACK),
-                            late_raw[2 * a + part][:].rearrange("p i (c e) -> p c i e", e=4),
-                        )
-                        cols = slice(part * QUARTER, (part + 1) * QUARTER)
-                        nc.vector.quantize_mx(codes[:, cols].bitcast(FP8X4), scales[:, cols], grouped[:])
-            cands[step] = gate(1, t, half)
-            if step > 1:
-                holds[step - 1] = gate(0, *STEPS[step - 1])
-            if step in (0, len(STEPS) - 1):
-                holds[step] = gate(0, t, half)
+                    quantize_x(nc.scalar.copy, a, lo)
+            cands[step] = gate(1, t, lo, hi)
+            holds[step] = gate(0, t, lo, hi)
 
-        def blend(step):
-            t, half = STEPS[step]
-            cand, hold = cands[step], holds[step]
-            cols = offsets[:, half * (HALF // 16) : (half + 1) * (HALF // 16)]
-            mix = ring.tile([P, HALF], F32, name="mix", tag="mix")
-            engine = nc.vector if step in ON_VECTOR else nc.gpsimd
-            nc.vector.tensor_tensor(mix[:], state[t][:].indirect(cols), cand[:], ALU.subtract)
-            engine.tensor_tensor(mix[:], mix[:], hold[:], ALU.mult)
-            engine.tensor_tensor(mix[:], mix[:], cand[:], ALU.add)
-            engine.tensor_tensor(mix[:], mix[:], weight[half][:], ALU.mult)
-            return mix
+        mixes = {}
+
+        def fetch(step):
+            t, lo, hi = STEPS[step]
+            mixes[step] = ring.tile([P, hi - lo], F32, name="mix", tag="mix", bufs=3)
+            nc.vector.tensor_tensor(mixes[step][:], state[t][:].indirect(offsets[:, lo // 16 : hi // 16]), cands[step][:], ALU.subtract)
 
         SPLIT = 1280
         planes_s = keep.tile([P, PACK - 1, SPLIT], BF16, name="planes_s", tag="xq2", align_bytes=64)
@@ -236,10 +235,12 @@ def tile_list_tgn_emaP_kernel(
             nc.sync.dma_start(words_out[:, lo:hi], y_w[:].bitcast(I32))
 
         def place(step, mix):
-            t, half = STEPS[step]
-            cols = offsets[:, half * (HALF // 16) : (half + 1) * (HALF // 16)]
-            nc.vector.tensor_copy(page[t][:].indirect(cols), mix[:])
-            if half == 1:
+            t, lo, hi = STEPS[step]
+            half, first = divmod(lo, HALF)
+            nc.vector.tensor_tensor(
+                page[t][:].indirect(offsets[:, lo // 16 : hi // 16]), mix[:], weight[half][:, first : first + hi - lo], ALU.mult
+            )
+            if hi == J:
                 nc.sync.dma_start(out_0.rearrange("(p t) c -> t p c", t=PACK)[t], page[t][:])
                 if t < PACK - 1:
                     nc.scalar.copy(planes_s[:, t, :], page[t][:, 0:SPLIT])
@@ -256,11 +257,16 @@ def tile_list_tgn_emaP_kernel(
                     for part in PARTS[3:] + PARTS[:3]:
                         emit(part)
 
-        mix = blend(0)
+        fetch(0)
+        fetch(1)
         for step in range(len(STEPS)):
-            ahead = blend(step + 1) if step + 1 < len(STEPS) else None
-            place(step, mix)
-            mix = ahead
+            nc.vector.tensor_tensor(mixes[step][:], mixes[step][:], holds[step][:], ALU.mult)
+            if step > 0:
+                place(step - 1, mixes[step - 1])
+            nc.vector.tensor_tensor(mixes[step][:], mixes[step][:], cands[step][:], ALU.add)
+            if step + 2 < len(STEPS):
+                fetch(step + 2)
+        place(len(STEPS) - 1, mixes[len(STEPS) - 1])
 
         for q in range(4):
             nc.sync.dma_start(out_2[0, 4 * q : 4 * q + 4, :].bitcast(I32), y_s[32 * q : 32 * q + 4, :].bitcast(I32))

@@ -21,7 +21,7 @@ PACK = 4
 KP = P * PACK
 HALF = 512
 QUARTER = HALF // 2
-STEPS = [(0, 0, QUARTER), (1, 0, QUARTER), (0, QUARTER, HALF), (1, QUARTER, HALF), (2, 0, HALF), (0, HALF, J), (1, HALF, J), (2, HALF, J), (3, 0, HALF), (3, HALF, J)]
+STEPS = [(0, 0, HALF), (1, 0, HALF), (0, HALF, J), (1, HALF, J), (2, 0, HALF), (2, HALF, J), (3, 0, HALF), (3, HALF, J)]
 
 
 def tile_list_tgn_emaP_kernel(
@@ -32,23 +32,23 @@ def tile_list_tgn_emaP_kernel(
     with ExitStack() as ctx:
         keep = ctx.enter_context(tc.tile_pool(name="keep", bufs=1))
         ring = ctx.enter_context(tc.tile_pool(name="ring", bufs=2))
-        psum = ctx.enter_context(tc.psum_pool(name="psum", bufs=8))
+        psum = ctx.enter_context(tc.psum_pool(name="psum", bufs=2))
 
         offsets = keep.tile([P, J // 16], U16, name="offsets")
         tab_s = keep.tile([P, T], U8, name="tab_s", align_bytes=64)
         w_s_raw = keep.tile([P, 2, 2, N], U8, name="w_s_raw", align_bytes=64)
-        w_raw = [keep.tile([P, 2, 2 * N], U8, name="w_raw%d" % w, tag="late%d" % w) for w in range(2)]
+        w_raw = [keep.tile([P, 2, 2 * N], U8, name="w_raw%d" % w) for w in range(2)]
         tab_w = keep.tile([P, T], U32, name="tab_w", align_bytes=64)
         bias_n = keep.tile([P, PACK], F32, name="bias_n")
         bias_z = keep.tile([P, PACK], F32, name="bias_z")
         neg_bz = keep.tile([P, PACK], F32, name="neg_bz")
         weight = [keep.tile([P, HALF], F32, name="weight%d" % h) for h in range(2)]
         state = [keep.tile([P, T], F32, name="state%d" % t, tag="state%d" % t, align_bytes=64) for t in range(PACK)]
-        page = [keep.tile([P, T], F32, name="page%d" % t) for t in range(2)]
+        page = [keep.tile([P, T], F32, name="page%d" % t) for t in range(3)]
 
         nc.vector.memset(tab_s[:].bitcast(I32), 0)
         nc.vector.memset(w_s_raw[:].rearrange("p w a n -> p (w a n)").bitcast(I32), 0)
-        for t in range(2):
+        for t in range(3):
             nc.vector.memset(page[t][:], 0.0)
 
         def load_rows(tag, rows):
@@ -83,17 +83,22 @@ def tile_list_tgn_emaP_kernel(
         u_raw = {1: load_rows("raw1", un), 0: load_rows("raw0", uz)}
         for w, words in enumerate((wz_words, wn_words)):
             nc.sync.dma_start(w_raw[w][:].bitcast(I32), words.rearrange("a p b -> p a b").bitcast(I32))
-        load_x("raw2", 0, 0, QUARTER)
-        load_x("raw3", 1, 0, QUARTER)
         for k in range(4):
             load_w_scales(k)
+        load_x("raw2", 0, 0, QUARTER)
+        load_x("raw3", 0, QUARTER, HALF)
+        load_x("raw4", 1, 0, QUARTER)
+        load_x("raw5", 1, QUARTER, HALF)
         load_state(0)
         nc.sync.dma_start(bias_n[:], bn.rearrange("(p t) -> p t", t=PACK))
         nc.sync.dma_start(bias_z[:], bz.rearrange("(p t) -> p t", t=PACK))
         nc.sync.dma_start(weight[0][:], wgo[:, 0:HALF])
-        load_x("raw4", 0, QUARTER, HALF)
-        load_x("raw5", 1, QUARTER, HALF)
+        load_x("raw6", 0, HALF, J)
+        load_x("raw8", 1, HALF, J)
         load_state(1)
+        nc.sync.dma_start(weight[1][:], wgo[:, HALF:J])
+        load_state(2)
+        load_state(3)
         nc.scalar.mul(neg_bz[:], bias_z[:], -1.0)
 
         w_q = keep.tile([P, 2, 2, 2 * N], U8, name="w_q", align_bytes=64)
@@ -103,11 +108,6 @@ def tile_list_tgn_emaP_kernel(
                 w_q[:, w].bitcast(U16).rearrange("p a (t m) -> p a t m", t=PACK),
                 w_raw[w][:].bitcast(U16).rearrange("p a (m t) -> p a t m", t=PACK),
             )
-
-        for w in range(2):
-            page.append(keep.tile([P, T], F32, name="page%d" % (2 + w), tag="late%d" % w))
-            for c in range(4):
-                nc.gpsimd.memset(page[2 + w][:, c * HALF : (c + 1) * HALF], 0.0)
 
         picked_w, picked_s = {}, {}
 
@@ -127,14 +127,14 @@ def tile_list_tgn_emaP_kernel(
         def round_u(copy, raw):
             grouped = ring.tile([P, PACK * HALF], BF16, name="grouped", tag="grouped", align_bytes=64, bufs=3)
             copy(
-                grouped[:].rearrange("p (t m i) -> p m i t", t=PACK, i=PACK),
-                raw[:].rearrange("p i (m t) -> p m i t", t=PACK),
+                grouped[:].rearrange("p (t m i) -> p m t i", t=PACK, i=PACK),
+                raw[:].rearrange("p i (m t) -> p m t i", t=PACK),
             )
             return grouped
 
         x_q = {}
 
-        def quantize_x(copy, a, lo):
+        def quantize_x(copy, a, lo, pool=ring, tag="grouped", bufs=3):
             raw = x_raw[a, lo]
             width = raw.shape[2]
             half, first = divmod(lo, HALF)
@@ -143,7 +143,7 @@ def tile_list_tgn_emaP_kernel(
                     keep.tile([P, HALF], U32, name="x_codes", tag="xq%d" % (2 * half + a), align_bytes=64),
                     keep.tile([P, HALF], U8, name="x_scales%d" % (2 * half + a), align_bytes=64),
                 )
-            grouped = ring.tile([P, PACK * width], BF16, name="grouped", tag="grouped", align_bytes=64, bufs=3)
+            grouped = pool.tile([P, PACK * width], BF16, name="grouped", tag=tag, align_bytes=64, bufs=bufs)
             copy(
                 grouped[:].rearrange("p (c e i) -> p c i e", e=4, i=PACK),
                 raw[:].rearrange("p i (c e) -> p c i e", e=4),
@@ -161,12 +161,14 @@ def tile_list_tgn_emaP_kernel(
         )
         u_q[0] = quantize(round_u(nc.scalar.copy, u_raw[0]), "uz_q", "uz_s")
         quantize_x(nc.scalar.copy, 0, 0)
-        quantize_x(nc.vector.tensor_copy, 1, 0)
-        load_x("raw1", 0, HALF, J)
-        load_x("raw0", 1, HALF, J)
-        load_state(2)
-        nc.sync.dma_start(weight[1][:], wgo[:, HALF:J])
-        load_state(3)
+        quantize_x(nc.scalar.copy, 0, QUARTER)
+        quantize_x(nc.scalar.copy, 1, 0)
+        quantize_x(nc.vector.tensor_copy, 1, QUARTER, keep, "last_page", 1)
+        page.append(keep.tile([P, T], F32, name="page3", tag="last_page", align_bytes=64, bufs=1))
+        for c in range(4):
+            nc.gpsimd.memset(page[3][:, c * HALF : (c + 1) * HALF], 0.0)
+        for a in range(2):
+            quantize_x(nc.scalar.copy, a, HALF)
 
         def gate(w, t, lo, hi):
             half, first = divmod(lo, HALF)
@@ -189,84 +191,78 @@ def tile_list_tgn_emaP_kernel(
                         start=False, stop=(a == 1 and c + n == width),
                     )
             if w == 1:
-                res = ring.tile([P, width], F32, name="cand", tag="cand", bufs=10)
+                res = ring.tile([P, width], F32, name="cand", tag="cand", bufs=3)
                 nc.scalar.activation(res[:], bank[:], ACT.Tanh, bias=bias_n[:, t : t + 1])
             else:
-                res = ring.tile([P, width], F32, name="hold", tag="hold", bufs=10)
+                res = ring.tile([P, width], F32, name="hold", tag="hold", bufs=3)
                 nc.scalar.activation(res[:], bank[:], ACT.Sigmoid, bias=neg_bz[:, t : t + 1], scale=-1.0)
             return res
 
         cands, holds = {}, {}
         for step, (t, lo, hi) in enumerate(STEPS):
-            if t == 0 and lo > 0:
-                for a in range(2):
-                    quantize_x(nc.scalar.copy, a, lo)
             cands[step] = gate(1, t, lo, hi)
             holds[step] = gate(0, t, lo, hi)
 
-        mixes = {}
+        diffs, mixes = {}, {}
 
         def fetch(step):
             t, lo, hi = STEPS[step]
-            mixes[step] = ring.tile([P, hi - lo], F32, name="mix", tag="mix", bufs=3)
-            nc.vector.tensor_tensor(mixes[step][:], state[t][:].indirect(offsets[:, lo // 16 : hi // 16]), cands[step][:], ALU.subtract)
+            diffs[step] = keep.tile([P, hi - lo], F32, name="diff", tag="diff")
+            nc.vector.tensor_tensor(diffs[step][:], state[t][:].indirect(offsets[:, lo // 16 : hi // 16]), cands[step][:], ALU.subtract)
 
-        SPLIT = 1280
-        planes_s = keep.tile([P, PACK - 1, SPLIT], BF16, name="planes_s", tag="xq2", align_bytes=64)
-        planes_v = keep.tile([P, PACK, T - SPLIT], BF16, name="planes_v", tag="xq3", align_bytes=64)
-        PARTS = [(0, 512, "state0"), (512, 1024, "state1"), (1024, SPLIT, "part2"), (1536, T, "state2"), (SPLIT, 1536, "part4")]
-        rounded = {}
+        def blend(step):
+            t, lo, hi = STEPS[step]
+            half, first = divmod(lo, HALF)
+            diff = diffs[step]
+            engine = nc.vector if step < 2 else nc.gpsimd
+            engine.tensor_tensor(diff[:], diff[:], holds[step][:], ALU.mult)
+            engine.tensor_tensor(diff[:], diff[:], cands[step][:], ALU.add)
+            if step == 0:
+                return
+            mixes[step] = ring.tile([P, hi - lo], F32, name="mix", tag="mix")
+            nc.vector.tensor_tensor(mixes[step][:], diff[:], weight[half][:, first : first + hi - lo], ALU.mult)
 
-        def weave(copy, part, planes, first, slots):
-            lo, hi, tag = part
-            rounded[part] = keep.tile([P, hi - lo, PACK], BF16, name="rounded", tag=tag, align_bytes=64)
-            copy(
-                rounded[part][:, :, 0:slots].rearrange("p (c e) t -> p c t e", e=4),
-                planes[:, 0:slots, lo - first : hi - first].rearrange("p t (c e) -> p c t e", e=4),
-            )
+        rounded = [keep.tile([P, HALF, PACK], BF16, name="rounded%d" % c, align_bytes=64) for c in range(4)]
 
         y_s = keep.tile([P, T], U8, name="y_s", align_bytes=64)
         words_out = out_1[0].rearrange("p t i -> p (t i)").bitcast(I32)
 
-        def emit(part):
-            lo, hi, tag = part
+        def emit(c):
+            lo, hi = c * HALF, (c + 1) * HALF
             y_w = keep.tile([P, hi - lo], U32, name="y_w%d" % lo, align_bytes=64)
-            nc.vector.quantize_mx(y_w[:].bitcast(FP8X4), y_s[:, lo:hi], rounded[part][:].rearrange("p c t -> p (c t)"))
+            nc.vector.quantize_mx(y_w[:].bitcast(FP8X4), y_s[:, lo:hi], rounded[c][:].rearrange("p c t -> p (c t)"))
             nc.sync.dma_start(words_out[:, lo:hi], y_w[:].bitcast(I32))
 
-        def place(step, mix):
+        def place(step):
             t, lo, hi = STEPS[step]
-            half, first = divmod(lo, HALF)
-            nc.vector.tensor_tensor(
-                page[t][:].indirect(offsets[:, lo // 16 : hi // 16]), mix[:], weight[half][:, first : first + hi - lo], ALU.mult
-            )
+            window = page[t][:].indirect(offsets[:, lo // 16 : hi // 16])
+            if step == 0:
+                nc.vector.tensor_tensor(window, diffs[step][:], weight[0][:], ALU.mult)
+            else:
+                nc.vector.tensor_copy(window, mixes[step][:])
             if hi == J:
                 nc.sync.dma_start(out_0.rearrange("(p t) c -> t p c", t=PACK)[t], page[t][:])
-                if t < PACK - 1:
-                    nc.scalar.copy(planes_s[:, t, :], page[t][:, 0:SPLIT])
-                    nc.scalar.copy(planes_v[:, t, :], page[t][:, SPLIT:T])
-                if t == PACK - 2:
-                    for part in PARTS[:3]:
-                        weave(nc.scalar.copy, part, planes_s, 0, PACK - 1)
+                for c in (2, 3, 0, 1):
+                    src = page[t][:, c * HALF : (c + 1) * HALF]
+                    if t == 2 and c >= 2:
+                        nc.scalar.copy(rounded[c][:, :, 2:4], src.unsqueeze(2).to_broadcast([P, HALF, 2]))
+                    elif t == 3 and c >= 2:
+                        nc.vector.tensor_copy(rounded[c][:, :, t], src)
+                    else:
+                        nc.scalar.copy(rounded[c][:, :, t], src)
                 if t == PACK - 1:
-                    for part in PARTS[:3]:
-                        nc.scalar.copy(rounded[part][:, :, t], page[t][:, part[0] : part[1]])
-                    nc.vector.tensor_copy(planes_v[:, t, :], page[t][:, SPLIT:T])
-                    for part in PARTS[3:]:
-                        weave(nc.vector.tensor_copy, part, planes_v, SPLIT, PACK)
-                    for part in PARTS[3:] + PARTS[:3]:
-                        emit(part)
+                    for c in (2, 3, 0, 1):
+                        emit(c)
 
         fetch(0)
-        fetch(1)
         for step in range(len(STEPS)):
-            nc.vector.tensor_tensor(mixes[step][:], mixes[step][:], holds[step][:], ALU.mult)
+            blend(step)
+            if step == 0:
+                place(step)
+            if step + 1 < len(STEPS):
+                fetch(step + 1)
             if step > 0:
-                place(step - 1, mixes[step - 1])
-            nc.vector.tensor_tensor(mixes[step][:], mixes[step][:], cands[step][:], ALU.add)
-            if step + 2 < len(STEPS):
-                fetch(step + 2)
-        place(len(STEPS) - 1, mixes[len(STEPS) - 1])
+                place(step)
 
         for q in range(4):
             nc.sync.dma_start(out_2[0, 4 * q : 4 * q + 4, :].bitcast(I32), y_s[32 * q : 32 * q + 4, :].bitcast(I32))

@@ -1,6 +1,7 @@
 from contextlib import ExitStack
 
 import concourse.mybir as mybir
+from concourse.masks import make_identity
 
 K, M, N, T, J = 1024, 512, 512, 2048, 1024
 FLOPS = 2 * 2 * (K + M) * N * J
@@ -21,7 +22,7 @@ PACK = 4
 KP = P * PACK
 HALF = 512
 QUARTER = HALF // 2
-STEPS = [(0, 0, HALF), (1, 0, HALF), (0, HALF, J), (1, HALF, J), (2, 0, HALF), (2, HALF, J), (3, 0, HALF), (3, HALF, J)]
+STEPS = [(0, 0, HALF), (1, 0, HALF), (2, 0, HALF), (0, HALF, J), (1, HALF, J), (2, HALF, J), (3, 0, HALF), (3, HALF, J)]
 
 
 def tile_list_tgn_emaP_kernel(
@@ -42,17 +43,18 @@ def tile_list_tgn_emaP_kernel(
         bias_n = keep.tile([P, PACK], F32, name="bias_n")
         bias_z = keep.tile([P, PACK], F32, name="bias_z")
         neg_bz = keep.tile([P, PACK], F32, name="neg_bz")
-        weight = [keep.tile([P, HALF], F32, name="weight%d" % h) for h in range(2)]
+        weight_t = keep.tile([P, J // P], F32, name="weight_t")
+        ident = keep.tile([P, P], F32, name="ident")
         state = [keep.tile([P, T], F32, name="state%d" % t, tag="state%d" % t, align_bytes=64) for t in range(PACK)]
-        page = [keep.tile([P, T], F32, name="page%d" % t) for t in range(3)]
+        page = [keep.tile([P, T], F32, name="page%d" % t) for t in range(PACK)]
 
         nc.vector.memset(tab_s[:].bitcast(I32), 0)
         nc.vector.memset(w_s_raw[:].rearrange("p w a n -> p (w a n)").bitcast(I32), 0)
-        for t in range(3):
-            nc.vector.memset(page[t][:], 0.0)
+        for t in range(2):
+            nc.vector.memset(page[t][:].bitcast(I32), 0)
 
         def load_rows(tag, rows):
-            raw = keep.tile([P, PACK, rows.shape[1]], F32, name=tag, tag=tag)
+            raw = keep.tile([P, PACK, rows.shape[1]], F32, name=tag, tag=tag, align_bytes=64)
             nc.sync.dma_start(raw[:], rows.rearrange("(p i) c -> p i c", i=PACK))
             return raw
 
@@ -69,37 +71,42 @@ def tile_list_tgn_emaP_kernel(
 
         def load_w_scales(k):
             w, q = divmod(k, 4)
-            (nc.sync, nc.gpsimd)[w].dma_start(
+            (nc.sync, nc.scalar)[w].dma_start(
                 w_s_raw[32 * q : 32 * q + 4, w].bitcast(I32),
                 (wz_scales, wn_scales)[w][:, 4 * q : 4 * q + 4, :].rearrange("a r n -> r a n").bitcast(I32),
             )
 
         nc.sync.dma_start(offsets[:], offs)
         nc.sync.dma_start(tab_w[:].bitcast(I32), tab_words[0].rearrange("p t i -> p (t i)").bitcast(I32))
+        u_raw = {1: load_rows("raw1", un)}
         for q in range(4):
             load_tab_scales(q)
         for k in range(4, 8):
             load_w_scales(k)
-        u_raw = {1: load_rows("raw1", un), 0: load_rows("raw0", uz)}
+        u_raw[0] = load_rows("raw0", uz)
         for w, words in enumerate((wz_words, wn_words)):
             nc.sync.dma_start(w_raw[w][:].bitcast(I32), words.rearrange("a p b -> p a b").bitcast(I32))
         for k in range(4):
             load_w_scales(k)
         load_x("raw2", 0, 0, QUARTER)
         load_x("raw3", 0, QUARTER, HALF)
+        nc.sync.dma_start(bias_n[:], bn.rearrange("(p t) -> p t", t=PACK))
+        nc.sync.dma_start(bias_z[:], bz.rearrange("(p t) -> p t", t=PACK))
         load_x("raw4", 1, 0, QUARTER)
         load_x("raw5", 1, QUARTER, HALF)
         load_state(0)
-        nc.sync.dma_start(bias_n[:], bn.rearrange("(p t) -> p t", t=PACK))
-        nc.sync.dma_start(bias_z[:], bz.rearrange("(p t) -> p t", t=PACK))
-        nc.sync.dma_start(weight[0][:], wgo[:, 0:HALF])
+        with nc.allow_non_contiguous_dma(reason="one weight a partition"):
+            nc.sync.dma_start(weight_t[:], wgo[0].rearrange("(b p) -> p b", p=P))
+        load_state(1)
+        load_state(2)
         load_x("raw6", 0, HALF, J)
         load_x("raw8", 1, HALF, J)
-        load_state(1)
-        nc.sync.dma_start(weight[1][:], wgo[:, HALF:J])
-        load_state(2)
         load_state(3)
         nc.scalar.mul(neg_bz[:], bias_z[:], -1.0)
+        for t in range(2, PACK):
+            for c in range(4):
+                nc.gpsimd.memset(page[t][:, c * HALF : (c + 1) * HALF], 0.0)
+        make_identity(nc, ident[:])
 
         w_q = keep.tile([P, 2, 2, 2 * N], U8, name="w_q", align_bytes=64)
         w_s = keep.tile([P, 2, 2, N], U8, name="w_s", align_bytes=64)
@@ -135,8 +142,9 @@ def tile_list_tgn_emaP_kernel(
         x_q = {}
 
         def quantize_x(copy, a, lo, pool=ring, tag="grouped", bufs=3):
-            raw = x_raw[a, lo]
-            width = raw.shape[2]
+            width = QUARTER
+            raw = x_raw[a, lo] if (a, lo) in x_raw else x_raw[a, lo - QUARTER]
+            raw = raw[:, :, lo % raw.shape[2] : lo % raw.shape[2] + width]
             half, first = divmod(lo, HALF)
             if first == 0:
                 x_q[a, half] = (
@@ -146,11 +154,15 @@ def tile_list_tgn_emaP_kernel(
             grouped = pool.tile([P, PACK * width], BF16, name="grouped", tag=tag, align_bytes=64, bufs=bufs)
             copy(
                 grouped[:].rearrange("p (c e i) -> p c i e", e=4, i=PACK),
-                raw[:].rearrange("p i (c e) -> p c i e", e=4),
+                raw.rearrange("p i (c e) -> p c i e", e=4),
             )
             codes, scales = x_q[a, half]
             cols = slice(first, first + width)
             nc.vector.quantize_mx(codes[:, cols].bitcast(FP8X4), scales[:, cols], grouped[:])
+
+        def pool_copy(dst, src):
+            order = "p c i e -> p (c e) i"
+            nc.gpsimd.tensor_scalar(dst.rearrange(order), src.rearrange(order), 1.0, 0.0, ALU.mult, ALU.add)
 
         pick_table(0)
         pick_table(1)
@@ -163,14 +175,14 @@ def tile_list_tgn_emaP_kernel(
         quantize_x(nc.scalar.copy, 0, 0)
         quantize_x(nc.scalar.copy, 0, QUARTER)
         quantize_x(nc.scalar.copy, 1, 0)
-        quantize_x(nc.vector.tensor_copy, 1, QUARTER, keep, "last_page", 1)
-        page.append(keep.tile([P, T], F32, name="page3", tag="last_page", align_bytes=64, bufs=1))
-        for c in range(4):
-            nc.gpsimd.memset(page[3][:, c * HALF : (c + 1) * HALF], 0.0)
-        for a in range(2):
-            quantize_x(nc.scalar.copy, a, HALF)
+        quantize_x(nc.vector.tensor_copy, 1, QUARTER)
+        quantize_x(nc.scalar.copy, 0, HALF)
+        quantize_x(pool_copy, 0, HALF + QUARTER)
+        quantize_x(nc.scalar.copy, 1, HALF, keep, "second_mix", 1)
+        quantize_x(pool_copy, 1, HALF + QUARTER)
 
-        def gate(w, t, lo, hi):
+        def gate(w, step):
+            t, lo, hi = STEPS[step]
             half, first = divmod(lo, HALF)
             width = hi - lo
             bank = psum.tile([P, width], F32, name="bank", tag="bank")
@@ -191,38 +203,56 @@ def tile_list_tgn_emaP_kernel(
                         start=False, stop=(a == 1 and c + n == width),
                     )
             if w == 1:
-                res = ring.tile([P, width], F32, name="cand", tag="cand", bufs=3)
+                res = ring.tile([P, width], F32, name="cand", tag="cand", bufs=4)
                 nc.scalar.activation(res[:], bank[:], ACT.Tanh, bias=bias_n[:, t : t + 1])
             else:
-                res = ring.tile([P, width], F32, name="hold", tag="hold", bufs=3)
+                if step == last:
+                    res = keep.tile([P, width], F32, name="hold", tag="last_hold", align_bytes=64)
+                else:
+                    res = ring.tile([P, width], F32, name="hold", tag="hold", bufs=4)
                 nc.scalar.activation(res[:], bank[:], ACT.Sigmoid, bias=neg_bz[:, t : t + 1], scale=-1.0)
             return res
 
         cands, holds = {}, {}
-        for step, (t, lo, hi) in enumerate(STEPS):
-            cands[step] = gate(1, t, lo, hi)
-            holds[step] = gate(0, t, lo, hi)
+        last = len(STEPS) - 1
 
         diffs, mixes = {}, {}
 
         def fetch(step):
             t, lo, hi = STEPS[step]
-            diffs[step] = keep.tile([P, hi - lo], F32, name="diff", tag="diff")
-            nc.vector.tensor_tensor(diffs[step][:], state[t][:].indirect(offsets[:, lo // 16 : hi // 16]), cands[step][:], ALU.subtract)
+            diffs[step] = keep.tile([P, hi - lo], F32, name="diff%d" % step)
+            listed = state[t][:].indirect(offsets[:, lo // 16 : hi // 16])
+            nc.vector.tensor_copy(diffs[step][:], listed)
 
         def blend(step):
             t, lo, hi = STEPS[step]
-            half, first = divmod(lo, HALF)
-            diff = diffs[step]
-            engine = nc.vector if step < 2 else nc.gpsimd
-            engine.tensor_tensor(diff[:], diff[:], holds[step][:], ALU.mult)
-            engine.tensor_tensor(diff[:], diff[:], cands[step][:], ALU.add)
-            if step == 0:
-                return
-            mixes[step] = ring.tile([P, hi - lo], F32, name="mix", tag="mix")
-            nc.vector.tensor_tensor(mixes[step][:], diff[:], weight[half][:, first : first + hi - lo], ALU.mult)
+            diff, cand = diffs[step], cands[step]
+            mix = mixes[step] = diff
+            if step == 1:
+                mix = mixes[step] = keep.tile([P, hi - lo], F32, name="mix", tag="second_mix", align_bytes=64, bufs=1)
+            nc.gpsimd.tensor_tensor(diff[:], diff[:], cand[:], ALU.subtract)
+            nc.gpsimd.tensor_tensor(diff[:], diff[:], holds[step][:], ALU.mult)
+            blocks = [slice(b, b + P) for b in range(0, hi - lo, P)]
+            turned = psum.tile([P, hi - lo], F32, name="turned", tag="turned")
+            for term, src in enumerate((cand, diff)):
+                for b, cols in enumerate(blocks):
+                    nc.tensor.matmul(
+                        turned[:, cols], lhsT=src[:, cols], rhs=ident[:], is_transpose=True,
+                        start=(term == 0 and b == 0), stop=(term == 1 and b == len(blocks) - 1),
+                    )
+            if step == last:
+                weighted = keep.tile([P, hi - lo], F32, name="weighted", tag="last_weighted", align_bytes=64)
+            else:
+                weighted = ring.tile([P, hi - lo], F32, name="weighted", tag="weighted")
+            for b, cols in enumerate(blocks):
+                block = lo // P + b
+                nc.scalar.activation(weighted[:, cols], turned[:, cols], ACT.Copy, scale=weight_t[:, block : block + 1])
+            back = psum.tile([P, hi - lo], F32, name="back", tag="back")
+            for cols in blocks:
+                nc.tensor.transpose(back[:, cols], weighted[:, cols], ident[:])
+            nc.scalar.copy(mix[:], back[:])
 
-        rounded = [keep.tile([P, HALF, PACK], BF16, name="rounded%d" % c, align_bytes=64) for c in range(4)]
+        rounded = [keep.tile([P, HALF, PACK], BF16, name="rounded", tag="raw%d" % (2 + c), align_bytes=64) for c in range(4)]
 
         y_s = keep.tile([P, T], U8, name="y_s", align_bytes=64)
         words_out = out_1[0].rearrange("p t i -> p (t i)").bitcast(I32)
@@ -236,33 +266,46 @@ def tile_list_tgn_emaP_kernel(
         def place(step):
             t, lo, hi = STEPS[step]
             window = page[t][:].indirect(offsets[:, lo // 16 : hi // 16])
-            if step == 0:
-                nc.vector.tensor_tensor(window, diffs[step][:], weight[0][:], ALU.mult)
-            else:
-                nc.vector.tensor_copy(window, mixes[step][:])
+            nc.vector.tensor_copy(window, mixes[step][:])
             if hi == J:
                 nc.sync.dma_start(out_0.rearrange("(p t) c -> t p c", t=PACK)[t], page[t][:])
-                for c in (2, 3, 0, 1):
-                    src = page[t][:, c * HALF : (c + 1) * HALF]
-                    if t == 2 and c >= 2:
-                        nc.scalar.copy(rounded[c][:, :, 2:4], src.unsqueeze(2).to_broadcast([P, HALF, 2]))
-                    elif t == 3 and c >= 2:
-                        nc.vector.tensor_copy(rounded[c][:, :, t], src)
-                    else:
-                        nc.scalar.copy(rounded[c][:, :, t], src)
-                if t == PACK - 1:
-                    for c in (2, 3, 0, 1):
-                        emit(c)
 
-        fetch(0)
-        for step in range(len(STEPS)):
-            blend(step)
+        def round_page(t):
+            u, e = divmod(t, 2)
+            for c in (2, 3, 0, 1):
+                src = page[t][:, c * HALF : (c + 1) * HALF]
+                dst = pairs[c // 2][:, c % 2, u]
+                if c < 2:
+                    nc.scalar.copy(dst[:, :, e], src)
+                elif t == 3:
+                    nc.vector.tensor_copy(dst[:, :, e], src)
+                elif t == 2:
+                    nc.gpsimd.tensor_scalar(dst, src.unsqueeze(2).to_broadcast([P, HALF, 2]), 1.0, 0.0, ALU.mult, ALU.add)
+                else:
+                    nc.gpsimd.tensor_scalar(dst[:, :, e], src, 1.0, 0.0, ALU.mult, ALU.add)
+                if t == 3:
+                    copy, word = (nc.scalar.copy, U32) if c < 2 else (nc.vector.tensor_copy, I32)
+                    copy(
+                        rounded[c][:].bitcast(word),
+                        pairs[c // 2][:, c % 2].rearrange("p u c e -> p u (c e)").bitcast(word).rearrange("p u c -> p c u"),
+                    )
+
+        for step in range(len(STEPS) + 1):
+            if step < len(STEPS):
+                cands[step] = gate(1, step)
+                holds[step] = gate(0, step)
             if step == 0:
-                place(step)
-            if step + 1 < len(STEPS):
-                fetch(step + 1)
-            if step > 0:
-                place(step)
+                for later in range(len(STEPS)):
+                    fetch(later)
+            else:
+                blend(step - 1)
+        for step in range(len(STEPS)):
+            place(step)
+        pairs = [keep.tile([P, 2, 2, HALF, 2], BF16, name="pairs", tag=tag, align_bytes=64) for tag in ("last_weighted", "last_hold")]
+        for t in range(PACK):
+            round_page(t)
+        for c in (2, 3, 0, 1):
+            emit(c)
 
         for q in range(4):
             nc.sync.dma_start(out_2[0, 4 * q : 4 * q + 4, :].bitcast(I32), y_s[32 * q : 32 * q + 4, :].bitcast(I32))

@@ -44,13 +44,15 @@ def tile_list_tgn_emaP_kernel(
         bias_z = keep.tile([P, PACK], F32, name="bias_z")
         neg_bz = keep.tile([P, PACK], F32, name="neg_bz")
         weight_t = keep.tile([P, J // P], F32, name="weight_t")
+        weight_rows = keep.tile([P, P], F32, name="weight_rows")
         ident = keep.tile([P, P], F32, name="ident")
         state = [keep.tile([P, T], F32, name="state%d" % t, tag="state%d" % t, align_bytes=64) for t in range(PACK)]
         page = [keep.tile([P, T], F32, name="page%d" % t) for t in range(PACK)]
 
         nc.vector.memset(tab_s[:].bitcast(I32), 0)
         nc.vector.memset(w_s_raw[:].rearrange("p w a n -> p (w a n)").bitcast(I32), 0)
-        for t in range(2):
+        nc.vector.memset(weight_rows[:], 0.0)
+        for t in range(3):
             nc.vector.memset(page[t][:].bitcast(I32), 0)
 
         def load_rows(tag, rows):
@@ -69,44 +71,42 @@ def tile_list_tgn_emaP_kernel(
         def load_tab_scales(q):
             nc.sync.dma_start(tab_s[32 * q : 32 * q + 4, :].bitcast(I32), tab_scales[0, 4 * q : 4 * q + 4, :].bitcast(I32))
 
-        def load_w_scales(k):
-            w, q = divmod(k, 4)
-            (nc.sync, nc.scalar)[w].dma_start(
-                w_s_raw[32 * q : 32 * q + 4, w].bitcast(I32),
-                (wz_scales, wn_scales)[w][:, 4 * q : 4 * q + 4, :].rearrange("a r n -> r a n").bitcast(I32),
-            )
+        def load_w_scales(w):
+            for q in range(4):
+                nc.sync.dma_start(
+                    w_s_raw[32 * q : 32 * q + 4, w].bitcast(I32),
+                    (wz_scales, wn_scales)[w][:, 4 * q : 4 * q + 4, :].rearrange("a r n -> r a n").bitcast(I32),
+                )
 
         nc.sync.dma_start(offsets[:], offs)
         nc.sync.dma_start(tab_w[:].bitcast(I32), tab_words[0].rearrange("p t i -> p (t i)").bitcast(I32))
-        u_raw = {1: load_rows("raw1", un)}
         for q in range(4):
             load_tab_scales(q)
-        for k in range(4, 8):
-            load_w_scales(k)
-        u_raw[0] = load_rows("raw0", uz)
+        u_raw = {1: load_rows("raw1", un), 0: load_rows("raw0", uz)}
+        load_w_scales(1)
         for w, words in enumerate((wz_words, wn_words)):
             nc.sync.dma_start(w_raw[w][:].bitcast(I32), words.rearrange("a p b -> p a b").bitcast(I32))
-        for k in range(4):
-            load_w_scales(k)
         load_x("raw2", 0, 0, QUARTER)
+        load_w_scales(0)
         load_x("raw3", 0, QUARTER, HALF)
         nc.sync.dma_start(bias_n[:], bn.rearrange("(p t) -> p t", t=PACK))
         nc.sync.dma_start(bias_z[:], bz.rearrange("(p t) -> p t", t=PACK))
         load_x("raw4", 1, 0, QUARTER)
         load_x("raw5", 1, QUARTER, HALF)
         load_state(0)
-        with nc.allow_non_contiguous_dma(reason="one weight a partition"):
-            nc.sync.dma_start(weight_t[:], wgo[0].rearrange("(b p) -> p b", p=P))
+        nc.sync.dma_start(weight_rows[0 : J // P, :], wgo[0].rearrange("(b p) -> b p", p=P))
         load_state(1)
         load_state(2)
         load_x("raw6", 0, HALF, J)
         load_x("raw8", 1, HALF, J)
         load_state(3)
         nc.scalar.mul(neg_bz[:], bias_z[:], -1.0)
-        for t in range(2, PACK):
-            for c in range(4):
-                nc.gpsimd.memset(page[t][:, c * HALF : (c + 1) * HALF], 0.0)
         make_identity(nc, ident[:])
+        for c in range(4):
+            nc.gpsimd.memset(page[3][:, c * HALF : (c + 1) * HALF], 0.0)
+        weight_bank = psum.tile([P, P], F32, name="weight_bank", tag="back")
+        nc.tensor.transpose(weight_bank[:], weight_rows[:], ident[:])
+        nc.scalar.copy(weight_t[:], weight_bank[:, 0 : J // P])
 
         w_q = keep.tile([P, 2, 2, 2 * N], U8, name="w_q", align_bytes=64)
         w_s = keep.tile([P, 2, 2, N], U8, name="w_s", align_bytes=64)

@@ -78,25 +78,27 @@ def tile_list_tgn_emaP_kernel(
                     (wz_scales, wn_scales)[w][:, 4 * q : 4 * q + 4, :].rearrange("a r n -> r a n").bitcast(I32),
                 )
 
+        u_raw = {}
         nc.sync.dma_start(offsets[:], offs)
         nc.sync.dma_start(tab_w[:].bitcast(I32), tab_words[0].rearrange("p t i -> p (t i)").bitcast(I32))
         for q in range(4):
             load_tab_scales(q)
-        u_raw = {1: load_rows("raw1", un), 0: load_rows("raw0", uz)}
+        load_state(0)
+        u_raw[1] = load_rows("raw1", un)
+        u_raw[0] = load_rows("raw0", uz)
         load_w_scales(1)
+        load_state(1)
         for w, words in enumerate((wz_words, wn_words)):
             nc.sync.dma_start(w_raw[w][:].bitcast(I32), words.rearrange("a p b -> p a b").bitcast(I32))
-        load_x("raw2", 0, 0, QUARTER)
         load_w_scales(0)
-        load_x("raw3", 0, QUARTER, HALF)
+        load_state(2)
         nc.sync.dma_start(bias_n[:], bn.rearrange("(p t) -> p t", t=PACK))
         nc.sync.dma_start(bias_z[:], bz.rearrange("(p t) -> p t", t=PACK))
+        nc.sync.dma_start(weight_rows[0 : J // P, :], wgo[0].rearrange("(b p) -> b p", p=P))
+        load_x("raw2", 0, 0, QUARTER)
+        load_x("raw3", 0, QUARTER, HALF)
         load_x("raw4", 1, 0, QUARTER)
         load_x("raw5", 1, QUARTER, HALF)
-        load_state(0)
-        nc.sync.dma_start(weight_rows[0 : J // P, :], wgo[0].rearrange("(b p) -> b p", p=P))
-        load_state(1)
-        load_state(2)
         load_x("raw6", 0, HALF, J)
         load_x("raw8", 1, HALF, J)
         load_state(3)
@@ -160,10 +162,6 @@ def tile_list_tgn_emaP_kernel(
             cols = slice(first, first + width)
             nc.vector.quantize_mx(codes[:, cols].bitcast(FP8X4), scales[:, cols], grouped[:])
 
-        def pool_copy(dst, src):
-            order = "p c i e -> p (c e) i"
-            nc.gpsimd.tensor_scalar(dst.rearrange(order), src.rearrange(order), 1.0, 0.0, ALU.mult, ALU.add)
-
         pick_table(0)
         pick_table(1)
         u_q = {1: quantize(round_u(nc.scalar.copy, u_raw[1]), "un_q", "un_s")}
@@ -176,10 +174,6 @@ def tile_list_tgn_emaP_kernel(
         quantize_x(nc.scalar.copy, 0, QUARTER)
         quantize_x(nc.scalar.copy, 1, 0)
         quantize_x(nc.vector.tensor_copy, 1, QUARTER)
-        quantize_x(nc.scalar.copy, 0, HALF)
-        quantize_x(pool_copy, 0, HALF + QUARTER)
-        quantize_x(nc.scalar.copy, 1, HALF, keep, "second_mix", 1)
-        quantize_x(pool_copy, 1, HALF + QUARTER)
 
         def gate(w, step):
             t, lo, hi = STEPS[step]
@@ -228,10 +222,9 @@ def tile_list_tgn_emaP_kernel(
             t, lo, hi = STEPS[step]
             diff, cand = diffs[step], cands[step]
             mix = mixes[step] = diff
-            if step == 1:
-                mix = mixes[step] = keep.tile([P, hi - lo], F32, name="mix", tag="second_mix", align_bytes=64, bufs=1)
-            nc.gpsimd.tensor_tensor(diff[:], diff[:], cand[:], ALU.subtract)
-            nc.gpsimd.tensor_tensor(diff[:], diff[:], holds[step][:], ALU.mult)
+            engine = nc.vector if step < 2 else nc.gpsimd
+            engine.tensor_tensor(diff[:], diff[:], cand[:], ALU.subtract)
+            engine.tensor_tensor(diff[:], diff[:], holds[step][:], ALU.mult)
             blocks = [slice(b, b + P) for b in range(0, hi - lo, P)]
             turned = psum.tile([P, hi - lo], F32, name="turned", tag="turned")
             for term, src in enumerate((cand, diff)):
@@ -299,6 +292,10 @@ def tile_list_tgn_emaP_kernel(
                     fetch(later)
             else:
                 blend(step - 1)
+            if step == 2:
+                for a in range(2):
+                    quantize_x(nc.vector.tensor_copy, a, HALF)
+                    quantize_x(nc.vector.tensor_copy, a, HALF + QUARTER)
         for step in range(len(STEPS)):
             place(step)
         pairs = [keep.tile([P, 2, 2, HALF, 2], BF16, name="pairs", tag=tag, align_bytes=64) for tag in ("last_weighted", "last_hold")]

@@ -22,7 +22,7 @@ PACK = 4
 KP = P * PACK
 HALF = 512
 QUARTER = HALF // 2
-STEPS = [(0, 0, HALF), (1, 0, HALF), (2, 0, HALF), (0, HALF, J), (1, HALF, J), (2, HALF, J), (3, 0, HALF), (3, HALF, J)]
+STEPS = [(0, 0, HALF), (1, 0, HALF), (2, 0, HALF), (0, HALF, J), (1, HALF, J), (3, 0, HALF), (2, HALF, J), (3, HALF, J)]
 
 
 def tile_list_tgn_emaP_kernel(
@@ -52,7 +52,7 @@ def tile_list_tgn_emaP_kernel(
         nc.vector.memset(tab_s[:].bitcast(I32), 0)
         nc.vector.memset(w_s_raw[:].rearrange("p w a n -> p (w a n)").bitcast(I32), 0)
         nc.vector.memset(weight_rows[:], 0.0)
-        for t in range(3):
+        for t in range(PACK):
             nc.vector.memset(page[t][:].bitcast(I32), 0)
 
         def load_rows(tag, rows):
@@ -69,13 +69,13 @@ def tile_list_tgn_emaP_kernel(
             x_raw[a, lo] = load_rows(tag, x[a * KP : (a + 1) * KP, lo:hi])
 
         def load_tab_scales(q):
-            nc.sync.dma_start(tab_s[32 * q : 32 * q + 4, :].bitcast(I32), tab_scales[0, 4 * q : 4 * q + 4, :].bitcast(I32))
+            nc.sync.dma_start(tab_s[q:P:32, :].bitcast(I32), tab_scales[0, q:16:4, :].bitcast(I32))
 
         def load_w_scales(w):
             for q in range(4):
                 nc.sync.dma_start(
-                    w_s_raw[32 * q : 32 * q + 4, w].bitcast(I32),
-                    (wz_scales, wn_scales)[w][:, 4 * q : 4 * q + 4, :].rearrange("a r n -> r a n").bitcast(I32),
+                    w_s_raw[q:P:32, w].bitcast(I32),
+                    (wz_scales, wn_scales)[w][:, q:16:4, :].rearrange("a r n -> r a n").bitcast(I32),
                 )
 
         u_raw = {}
@@ -104,8 +104,6 @@ def tile_list_tgn_emaP_kernel(
         load_state(3)
         nc.scalar.mul(neg_bz[:], bias_z[:], -1.0)
         make_identity(nc, ident[:])
-        for c in range(4):
-            nc.gpsimd.memset(page[3][:, c * HALF : (c + 1) * HALF], 0.0)
         weight_bank = psum.tile([P, P], F32, name="weight_bank", tag="back")
         nc.tensor.transpose(weight_bank[:], weight_rows[:], ident[:])
         nc.scalar.copy(weight_t[:], weight_bank[:, 0 : J // P])
@@ -179,7 +177,7 @@ def tile_list_tgn_emaP_kernel(
             t, lo, hi = STEPS[step]
             half, first = divmod(lo, HALF)
             width = hi - lo
-            bank = psum.tile([P, width], F32, name="bank", tag="bank")
+            bank = psum.tile([P, width], F32, name="bank", tag="bank", bufs=4)
             cols = slice(t * P, (t + 1) * P)
             nc.tensor.matmul_mx(
                 bank[:], lhsT=u_q[w][0][:, cols].bitcast(FP8X4), lhsT_scale=u_q[w][1][:, cols],
@@ -223,15 +221,18 @@ def tile_list_tgn_emaP_kernel(
             diff, cand = diffs[step], cands[step]
             mix = mixes[step] = diff
             engine = nc.vector if step < 2 else nc.gpsimd
-            engine.tensor_tensor(diff[:], diff[:], cand[:], ALU.subtract)
-            engine.tensor_tensor(diff[:], diff[:], holds[step][:], ALU.mult)
+            term = diff
+            if step == 2:
+                term = keep.tile([P, hi - lo], F32, name="term", tag="first_pool_term", align_bytes=64, bufs=1)
+            engine.tensor_tensor(term[:], diff[:], cand[:], ALU.subtract)
+            engine.tensor_tensor(term[:], term[:], holds[step][:], ALU.mult)
             blocks = [slice(b, b + P) for b in range(0, hi - lo, P)]
             turned = psum.tile([P, hi - lo], F32, name="turned", tag="turned")
-            for term, src in enumerate((cand, diff)):
+            for second, src in enumerate((cand, term)):
                 for b, cols in enumerate(blocks):
                     nc.tensor.matmul(
                         turned[:, cols], lhsT=src[:, cols], rhs=ident[:], is_transpose=True,
-                        start=(term == 0 and b == 0), stop=(term == 1 and b == len(blocks) - 1),
+                        start=(second == 0 and b == 0), stop=(second == 1 and b == len(blocks) - 1),
                     )
             if step == last:
                 weighted = keep.tile([P, hi - lo], F32, name="weighted", tag="last_weighted", align_bytes=64)
@@ -245,15 +246,20 @@ def tile_list_tgn_emaP_kernel(
                 nc.tensor.transpose(back[:, cols], weighted[:, cols], ident[:])
             nc.scalar.copy(mix[:], back[:])
 
-        rounded = [keep.tile([P, HALF, PACK], BF16, name="rounded", tag="raw%d" % (2 + c), align_bytes=64) for c in range(4)]
+        spare = ["raw2", "raw3", "raw4", "raw5", "raw6", "raw8"]
 
         y_s = keep.tile([P, T], U8, name="y_s", align_bytes=64)
         words_out = out_1[0].rearrange("p t i -> p (t i)").bitcast(I32)
 
-        def emit(c):
-            lo, hi = c * HALF, (c + 1) * HALF
+        def emit(lo, hi):
+            c, first = divmod(lo, HALF)
+            cols = slice(first, first + hi - lo)
+            copy, word = (nc.scalar.copy, U32) if c < 2 else (nc.vector.tensor_copy, I32)
+            both = pairs[c // 2][:, c % 2].rearrange("p u c e -> p u (c e)").bitcast(word).rearrange("p u c -> p c u")
+            rounded = keep.tile([P, hi - lo, PACK], BF16, name="rounded%d" % lo, tag=spare.pop(), align_bytes=64)
+            copy(rounded[:].bitcast(word), both[:, cols])
             y_w = keep.tile([P, hi - lo], U32, name="y_w%d" % lo, align_bytes=64)
-            nc.vector.quantize_mx(y_w[:].bitcast(FP8X4), y_s[:, lo:hi], rounded[c][:].rearrange("p c t -> p (c t)"))
+            nc.vector.quantize_mx(y_w[:].bitcast(FP8X4), y_s[:, lo:hi], rounded[:].rearrange("p c t -> p (c t)"))
             nc.sync.dma_start(words_out[:, lo:hi], y_w[:].bitcast(I32))
 
         def place(step):
@@ -276,33 +282,31 @@ def tile_list_tgn_emaP_kernel(
                     nc.gpsimd.tensor_scalar(dst, src.unsqueeze(2).to_broadcast([P, HALF, 2]), 1.0, 0.0, ALU.mult, ALU.add)
                 else:
                     nc.gpsimd.tensor_scalar(dst[:, :, e], src, 1.0, 0.0, ALU.mult, ALU.add)
-                if t == 3:
-                    copy, word = (nc.scalar.copy, U32) if c < 2 else (nc.vector.tensor_copy, I32)
-                    copy(
-                        rounded[c][:].bitcast(word),
-                        pairs[c // 2][:, c % 2].rearrange("p u c e -> p u (c e)").bitcast(word).rearrange("p u c -> p c u"),
-                    )
 
         for step in range(len(STEPS) + 1):
             if step < len(STEPS):
                 cands[step] = gate(1, step)
                 holds[step] = gate(0, step)
             if step == 0:
-                for later in range(len(STEPS)):
-                    fetch(later)
+                for later in range(last):
+                    if STEPS[later][0] < PACK - 1:
+                        fetch(later)
             else:
                 blend(step - 1)
             if step == 2:
-                for a in range(2):
-                    quantize_x(nc.vector.tensor_copy, a, HALF)
-                    quantize_x(nc.vector.tensor_copy, a, HALF + QUARTER)
+                quantize_x(nc.vector.tensor_copy, 0, HALF)
+                quantize_x(nc.scalar.copy, 0, HALF + QUARTER)
+                quantize_x(nc.vector.tensor_copy, 1, HALF)
+                quantize_x(nc.scalar.copy, 1, HALF + QUARTER, keep, "first_pool_term", 1)
+                fetch(last - 2)
+                fetch(last)
         for step in range(len(STEPS)):
             place(step)
         pairs = [keep.tile([P, 2, 2, HALF, 2], BF16, name="pairs", tag=tag, align_bytes=64) for tag in ("last_weighted", "last_hold")]
         for t in range(PACK):
             round_page(t)
-        for c in (2, 3, 0, 1):
-            emit(c)
+        for lo, hi in ((J, J + QUARTER), (J + QUARTER, J + HALF), (J + HALF, T), (0, HALF), (HALF, HALF + QUARTER), (HALF + QUARTER, 2 * HALF)):
+            emit(lo, hi)
 
-        for q in range(4):
-            nc.sync.dma_start(out_2[0, 4 * q : 4 * q + 4, :].bitcast(I32), y_s[32 * q : 32 * q + 4, :].bitcast(I32))
+        for r in range(4):
+            nc.scalar.dma_start(out_2[0, r:16:4, :].bitcast(I32), y_s[r:P:32, :].bitcast(I32))

@@ -22,7 +22,7 @@ PACK = 4
 KP = P * PACK
 HALF = 512
 QUARTER = HALF // 2
-STEPS = [(0, 0, HALF), (1, 0, HALF), (2, 0, HALF), (0, HALF, J), (1, HALF, J), (3, 0, HALF), (2, HALF, J), (3, HALF, J)]
+STEPS = [(t, lo, lo + HALF) for lo in (0, HALF) for t in range(PACK)]
 
 
 def tile_list_tgn_emaP_kernel(
@@ -37,7 +37,7 @@ def tile_list_tgn_emaP_kernel(
 
         offsets = keep.tile([P, J // 16], U16, name="offsets")
         tab_s = keep.tile([P, T], U8, name="tab_s", align_bytes=64)
-        w_s_raw = keep.tile([P, 2, 2, N], U8, name="w_s_raw", align_bytes=64)
+        w_s_raw = [keep.tile([P, 2, N], U8, name="w_s_raw%d" % w, align_bytes=64) for w in range(2)]
         w_raw = [keep.tile([P, 2, 2 * N], U8, name="w_raw%d" % w) for w in range(2)]
         tab_w = keep.tile([P, T], U32, name="tab_w", align_bytes=64)
         bias_n = keep.tile([P, PACK], F32, name="bias_n")
@@ -50,7 +50,8 @@ def tile_list_tgn_emaP_kernel(
         page = [keep.tile([P, T], F32, name="page%d" % t) for t in range(PACK)]
 
         nc.vector.memset(tab_s[:].bitcast(I32), 0)
-        nc.vector.memset(w_s_raw[:].rearrange("p w a n -> p (w a n)").bitcast(I32), 0)
+        for w in (1, 0):
+            nc.vector.memset(w_s_raw[w][:].rearrange("p a n -> p (a n)").bitcast(I32), 0)
         nc.vector.memset(weight_rows[:], 0.0)
         for t in range(PACK):
             nc.vector.memset(page[t][:].bitcast(I32), 0)
@@ -74,46 +75,47 @@ def tile_list_tgn_emaP_kernel(
         def load_w_scales(w):
             for q in range(4):
                 nc.sync.dma_start(
-                    w_s_raw[q:P:32, w].bitcast(I32),
+                    w_s_raw[w][q:P:32].bitcast(I32),
                     (wz_scales, wn_scales)[w][:, q:16:4, :].rearrange("a r n -> r a n").bitcast(I32),
                 )
 
         u_raw = {}
         nc.sync.dma_start(offsets[:], offs)
-        nc.sync.dma_start(tab_w[:].bitcast(I32), tab_words[0].rearrange("p t i -> p (t i)").bitcast(I32))
         for q in range(4):
             load_tab_scales(q)
-        load_state(0)
+        nc.sync.dma_start(tab_w[:].bitcast(I32), tab_words[0].rearrange("p t i -> p (t i)").bitcast(I32))
         u_raw[1] = load_rows("raw1", un)
         u_raw[0] = load_rows("raw0", uz)
         load_w_scales(1)
-        load_state(1)
-        for w, words in enumerate((wz_words, wn_words)):
-            nc.sync.dma_start(w_raw[w][:].bitcast(I32), words.rearrange("a p b -> p a b").bitcast(I32))
+        for w in (1, 0):
+            nc.sync.dma_start(w_raw[w][:].bitcast(I32), (wz_words, wn_words)[w].rearrange("a p b -> p a b").bitcast(I32))
+        load_x("raw2", 0, 0, HALF)
         load_w_scales(0)
-        load_state(2)
+        load_x("raw3", 1, 0, HALF)
         nc.sync.dma_start(bias_n[:], bn.rearrange("(p t) -> p t", t=PACK))
         nc.sync.dma_start(bias_z[:], bz.rearrange("(p t) -> p t", t=PACK))
+        load_state(0)
+        load_state(1)
         nc.sync.dma_start(weight_rows[0 : J // P, :], wgo[0].rearrange("(b p) -> b p", p=P))
-        load_x("raw2", 0, 0, QUARTER)
-        load_x("raw3", 0, QUARTER, HALF)
-        load_x("raw4", 1, 0, QUARTER)
-        load_x("raw5", 1, QUARTER, HALF)
-        load_x("raw6", 0, HALF, J)
-        load_x("raw8", 1, HALF, J)
+        load_state(2)
         load_state(3)
         nc.scalar.mul(neg_bz[:], bias_z[:], -1.0)
         make_identity(nc, ident[:])
-        weight_bank = psum.tile([P, P], F32, name="weight_bank", tag="back")
+        weight_bank = psum.tile([P, P], F32, name="weight_bank", tag="back", bufs=1)
         nc.tensor.transpose(weight_bank[:], weight_rows[:], ident[:])
         nc.scalar.copy(weight_t[:], weight_bank[:, 0 : J // P])
 
-        w_q = keep.tile([P, 2, 2, 2 * N], U8, name="w_q", align_bytes=64)
-        w_s = keep.tile([P, 2, 2, N], U8, name="w_s", align_bytes=64)
-        for w in range(2):
+        w_q = [keep.tile([P, 2, 2 * N], U8, name="w_q%d" % w, align_bytes=64) for w in range(2)]
+        w_s = [keep.tile([P, 2, N], U8, name="w_s%d" % w, align_bytes=64) for w in range(2)]
+
+        def deal(w):
             nc.vector.tensor_copy(
-                w_q[:, w].bitcast(U16).rearrange("p a (t m) -> p a t m", t=PACK),
+                w_q[w][:].bitcast(U16).rearrange("p a (t m) -> p a t m", t=PACK),
                 w_raw[w][:].bitcast(U16).rearrange("p a (m t) -> p a t m", t=PACK),
+            )
+            nc.vector.tensor_copy(
+                w_s[w][:].rearrange("p a (t m) -> p a t m", t=PACK),
+                w_s_raw[w][:].rearrange("p a (m t) -> p a t m", t=PACK),
             )
 
         picked_w, picked_s = {}, {}
@@ -141,37 +143,28 @@ def tile_list_tgn_emaP_kernel(
 
         x_q = {}
 
-        def quantize_x(copy, a, lo, pool=ring, tag="grouped", bufs=3):
-            width = QUARTER
-            raw = x_raw[a, lo] if (a, lo) in x_raw else x_raw[a, lo - QUARTER]
-            raw = raw[:, :, lo % raw.shape[2] : lo % raw.shape[2] + width]
-            half, first = divmod(lo, HALF)
-            if first == 0:
-                x_q[a, half] = (
-                    keep.tile([P, HALF], U32, name="x_codes", tag="xq%d" % (2 * half + a), align_bytes=64),
-                    keep.tile([P, HALF], U8, name="x_scales%d" % (2 * half + a), align_bytes=64),
+        def quantize_x(copies, a, lo, pool=ring, tag="grouped", bufs=3):
+            raw = x_raw[a, lo]
+            grouped = pool.tile([P, PACK * HALF], BF16, name="grouped", tag=tag, align_bytes=64, bufs=bufs)
+            width = HALF // len(copies)
+            for k, copy in enumerate(copies):
+                copy(
+                    grouped[:, PACK * k * width : PACK * (k + 1) * width].rearrange("p (c e i) -> p c i e", e=4, i=PACK),
+                    raw[:, :, k * width : (k + 1) * width].rearrange("p i (c e) -> p c i e", e=4),
                 )
-            grouped = pool.tile([P, PACK * width], BF16, name="grouped", tag=tag, align_bytes=64, bufs=bufs)
-            copy(
-                grouped[:].rearrange("p (c e i) -> p c i e", e=4, i=PACK),
-                raw.rearrange("p i (c e) -> p c i e", e=4),
-            )
-            codes, scales = x_q[a, half]
-            cols = slice(first, first + width)
-            nc.vector.quantize_mx(codes[:, cols].bitcast(FP8X4), scales[:, cols], grouped[:])
+            half = lo // HALF
+            x_q[a, half] = quantize(grouped, "xq%d" % (2 * half + a), "x_scales%d" % (2 * half + a))
 
         pick_table(0)
         pick_table(1)
         u_q = {1: quantize(round_u(nc.scalar.copy, u_raw[1]), "un_q", "un_s")}
-        nc.vector.tensor_copy(
-            w_s[:].rearrange("p w a (t m) -> p (w a) t m", t=PACK),
-            w_s_raw[:].rearrange("p w a (m t) -> p (w a) t m", t=PACK),
-        )
+        deal(1)
         u_q[0] = quantize(round_u(nc.scalar.copy, u_raw[0]), "uz_q", "uz_s")
-        quantize_x(nc.scalar.copy, 0, 0)
-        quantize_x(nc.scalar.copy, 0, QUARTER)
-        quantize_x(nc.scalar.copy, 1, 0)
-        quantize_x(nc.vector.tensor_copy, 1, QUARTER)
+        load_x("raw1", 0, HALF, J)
+        load_x("raw0", 1, HALF, J)
+        quantize_x((nc.scalar.copy, nc.vector.tensor_copy), 0, 0)
+        deal(0)
+        quantize_x((nc.scalar.copy, nc.vector.tensor_copy), 1, 0)
 
         def gate(w, step):
             t, lo, hi = STEPS[step]
@@ -189,8 +182,8 @@ def tile_list_tgn_emaP_kernel(
                 codes, scales = x_q[a, half]
                 for c in range(0, width, n):
                     nc.tensor.matmul_mx(
-                        bank[:, c : c + n], lhsT=w_q[:, w, a, 2 * t * P : 2 * (t + 1) * P].bitcast(FP4X4),
-                        lhsT_scale=w_s[:, w, a, cols],
+                        bank[:, c : c + n], lhsT=w_q[w][:, a, 2 * t * P : 2 * (t + 1) * P].bitcast(FP4X4),
+                        lhsT_scale=w_s[w][:, a, cols],
                         rhs=codes[:, first + c : first + c + n].bitcast(FP8X4), rhs_scale=scales[:, first + c : first + c + n],
                         start=False, stop=(a == 1 and c + n == width),
                     )
@@ -198,34 +191,38 @@ def tile_list_tgn_emaP_kernel(
                 res = ring.tile([P, width], F32, name="cand", tag="cand", bufs=4)
                 nc.scalar.activation(res[:], bank[:], ACT.Tanh, bias=bias_n[:, t : t + 1])
             else:
-                if step == last:
-                    res = keep.tile([P, width], F32, name="hold", tag="last_hold", align_bytes=64)
+                if step in hold_tags:
+                    res = keep.tile([P, width], F32, name="hold", tag=hold_tags[step], align_bytes=64)
                 else:
-                    res = ring.tile([P, width], F32, name="hold", tag="hold", bufs=4)
+                    res = ring.tile([P, width], F32, name="hold", tag="hold", bufs=3)
                 nc.scalar.activation(res[:], bank[:], ACT.Sigmoid, bias=neg_bz[:, t : t + 1], scale=-1.0)
             return res
 
         cands, holds = {}, {}
         last = len(STEPS) - 1
 
-        diffs, mixes = {}, {}
+        hold_tags = {1: "hold1", 2: "hold2", last: "last_hold"}
+        term_tags = {2: "hold1", 3: "late1"}
+        weighted_tags = {2: "raw0", last: "last_weighted"}
+        picked_h, mixes = {}, {}
 
-        def fetch(step):
-            t, lo, hi = STEPS[step]
-            diffs[step] = keep.tile([P, hi - lo], F32, name="diff%d" % step)
-            listed = state[t][:].indirect(offsets[:, lo // 16 : hi // 16])
-            nc.vector.tensor_copy(diffs[step][:], listed)
+        def fetch(t):
+            picked_h[t] = keep.tile([P, J], F32, name="picked_h%d" % t, tag="hold2" if t == PACK - 1 else "picked_h%d" % t, align_bytes=64)
+            nc.vector.tensor_copy(picked_h[t][:], state[t][:].indirect(offsets[:]))
 
         def blend(step):
             t, lo, hi = STEPS[step]
-            diff, cand = diffs[step], cands[step]
-            mix = mixes[step] = diff
+            diff, cand = picked_h[t][:, lo:hi], cands[step]
+            mix = diff
+            if step == 1:
+                mix = keep.tile([P, hi - lo], F32, name="mix", tag="late0", align_bytes=64)[:]
+            mixes[step] = mix
             engine = nc.vector if step < 2 else nc.gpsimd
             term = diff
-            if step == 2:
-                term = keep.tile([P, hi - lo], F32, name="term", tag="first_pool_term", align_bytes=64, bufs=1)
-            engine.tensor_tensor(term[:], diff[:], cand[:], ALU.subtract)
-            engine.tensor_tensor(term[:], term[:], holds[step][:], ALU.mult)
+            if step in term_tags:
+                term = keep.tile([P, hi - lo], F32, name="term", tag=term_tags[step], align_bytes=64)[:]
+            engine.tensor_tensor(term, diff, cand[:], ALU.subtract)
+            engine.tensor_tensor(term, term, holds[step][:], ALU.mult)
             blocks = [slice(b, b + P) for b in range(0, hi - lo, P)]
             turned = psum.tile([P, hi - lo], F32, name="turned", tag="turned")
             for second, src in enumerate((cand, term)):
@@ -234,19 +231,19 @@ def tile_list_tgn_emaP_kernel(
                         turned[:, cols], lhsT=src[:, cols], rhs=ident[:], is_transpose=True,
                         start=(second == 0 and b == 0), stop=(second == 1 and b == len(blocks) - 1),
                     )
-            if step == last:
-                weighted = keep.tile([P, hi - lo], F32, name="weighted", tag="last_weighted", align_bytes=64)
+            if step in weighted_tags:
+                weighted = keep.tile([P, hi - lo], F32, name="weighted", tag=weighted_tags[step], align_bytes=64)
             else:
                 weighted = ring.tile([P, hi - lo], F32, name="weighted", tag="weighted")
             for b, cols in enumerate(blocks):
                 block = lo // P + b
                 nc.scalar.activation(weighted[:, cols], turned[:, cols], ACT.Copy, scale=weight_t[:, block : block + 1])
-            back = psum.tile([P, hi - lo], F32, name="back", tag="back")
+            back = psum.tile([P, hi - lo], F32, name="back", tag="back", bufs=1)
             for cols in blocks:
                 nc.tensor.transpose(back[:, cols], weighted[:, cols], ident[:])
-            nc.scalar.copy(mix[:], back[:])
+            nc.scalar.copy(mix, back[:])
 
-        spare = ["raw2", "raw3", "raw4", "raw5", "raw6", "raw8"]
+        spare = ["raw2", "raw3", "state0", "state1", "state2", "state3"]
 
         y_s = keep.tile([P, T], U8, name="y_s", align_bytes=64)
         words_out = out_1[0].rearrange("p t i -> p (t i)").bitcast(I32)
@@ -265,7 +262,7 @@ def tile_list_tgn_emaP_kernel(
         def place(step):
             t, lo, hi = STEPS[step]
             window = page[t][:].indirect(offsets[:, lo // 16 : hi // 16])
-            nc.vector.tensor_copy(window, mixes[step][:])
+            nc.vector.tensor_copy(window, mixes[step])
             if hi == J:
                 nc.sync.dma_start(out_0.rearrange("(p t) c -> t p c", t=PACK)[t], page[t][:])
 
@@ -283,23 +280,27 @@ def tile_list_tgn_emaP_kernel(
                 else:
                     nc.gpsimd.tensor_scalar(dst[:, :, e], src, 1.0, 0.0, ALU.mult, ALU.add)
 
-        for step in range(len(STEPS) + 1):
-            if step < len(STEPS):
-                cands[step] = gate(1, step)
-                holds[step] = gate(0, step)
-            if step == 0:
-                for later in range(last):
-                    if STEPS[later][0] < PACK - 1:
-                        fetch(later)
-            else:
-                blend(step - 1)
-            if step == 2:
-                quantize_x(nc.vector.tensor_copy, 0, HALF)
-                quantize_x(nc.scalar.copy, 0, HALF + QUARTER)
-                quantize_x(nc.vector.tensor_copy, 1, HALF)
-                quantize_x(nc.scalar.copy, 1, HALF + QUARTER, keep, "first_pool_term", 1)
-                fetch(last - 2)
-                fetch(last)
+        def gates(step):
+            cands[step] = gate(1, step)
+            holds[step] = gate(0, step)
+
+        gates(0)
+        fetch(0)
+        gates(1)
+        blend(0)
+        fetch(1)
+        gates(2)
+        quantize_x((nc.scalar.copy, nc.scalar.copy), 0, HALF, keep, "late0", 1)
+        quantize_x((nc.scalar.copy, nc.scalar.copy), 1, HALF, keep, "late1", 1)
+        blend(1)
+        fetch(2)
+        gates(3)
+        blend(2)
+        fetch(3)
+        for step in range(3, len(STEPS)):
+            if step < last:
+                gates(step + 1)
+            blend(step)
         for step in range(len(STEPS)):
             place(step)
         pairs = [keep.tile([P, 2, 2, HALF, 2], BF16, name="pairs", tag=tag, align_bytes=64) for tag in ("last_weighted", "last_hold")]

@@ -56,6 +56,10 @@ def tile_list_tgn_emaP_kernel(
         for t in range(PACK):
             nc.vector.memset(page[t][:].bitcast(I32), 0)
 
+        make_identity(nc, ident[:])
+        warm = keep.tile([P, 1], F32, name="warm")
+        nc.scalar.activation(warm[:], ident[:, 0:1], ACT.Sigmoid)
+
         def load_rows(tag, rows):
             raw = keep.tile([P, PACK, rows.shape[1]], F32, name=tag, tag=tag, align_bytes=64)
             nc.sync.dma_start(raw[:], rows.rearrange("(p i) c -> p i c", i=PACK))
@@ -83,8 +87,8 @@ def tile_list_tgn_emaP_kernel(
         nc.sync.dma_start(offsets[:], offs)
         for q in range(4):
             load_tab_scales(q)
-        nc.sync.dma_start(tab_w[:].bitcast(I32), tab_words[0].rearrange("p t i -> p (t i)").bitcast(I32))
         u_raw[1] = load_rows("raw1", un)
+        nc.sync.dma_start(tab_w[:].bitcast(I32), tab_words[0].rearrange("p t i -> p (t i)").bitcast(I32))
         u_raw[0] = load_rows("raw0", uz)
         load_w_scales(1)
         for w in (1, 0):
@@ -100,7 +104,6 @@ def tile_list_tgn_emaP_kernel(
         load_state(2)
         load_state(3)
         nc.scalar.mul(neg_bz[:], bias_z[:], -1.0)
-        make_identity(nc, ident[:])
         weight_bank = psum.tile([P, P], F32, name="weight_bank", tag="back", bufs=1)
         nc.tensor.transpose(weight_bank[:], weight_rows[:], ident[:])
         nc.scalar.copy(weight_t[:], weight_bank[:, 0 : J // P])
@@ -118,14 +121,8 @@ def tile_list_tgn_emaP_kernel(
                 w_s_raw[w][:].rearrange("p a (m t) -> p a t m", t=PACK),
             )
 
-        picked_w, picked_s = {}, {}
-
-        def pick_table(half):
-            cols = offsets[:, half * (HALF // 16) : (half + 1) * (HALF // 16)]
-            picked_w[half] = keep.tile([P, HALF], U32, name="picked_w%d" % half, align_bytes=64)
-            picked_s[half] = keep.tile([P, HALF], U8, name="picked_s%d" % half, align_bytes=64)
-            nc.vector.tensor_copy(picked_w[half][:], tab_w[:].indirect(cols))
-            nc.vector.tensor_copy(picked_s[half][:], tab_s[:].indirect(cols))
+        picked_w = keep.tile([P, J], U32, name="picked_w", align_bytes=64)
+        picked_s = keep.tile([P, J], U8, name="picked_s", align_bytes=64)
 
         def quantize(grouped, tag, scale_name):
             codes = keep.tile([P, HALF], U32, name=tag, tag=tag, align_bytes=64)
@@ -143,7 +140,7 @@ def tile_list_tgn_emaP_kernel(
 
         x_q = {}
 
-        def quantize_x(copies, a, lo, pool=ring, tag="grouped", bufs=3):
+        def quantize_x(copies, a, lo, pool=ring, tag="grouped", bufs=3, code_tag=None):
             raw = x_raw[a, lo]
             grouped = pool.tile([P, PACK * HALF], BF16, name="grouped", tag=tag, align_bytes=64, bufs=bufs)
             width = HALF // len(copies)
@@ -153,10 +150,10 @@ def tile_list_tgn_emaP_kernel(
                     raw[:, :, k * width : (k + 1) * width].rearrange("p i (c e) -> p c i e", e=4),
                 )
             half = lo // HALF
-            x_q[a, half] = quantize(grouped, "xq%d" % (2 * half + a), "x_scales%d" % (2 * half + a))
+            x_q[a, half] = quantize(grouped, code_tag or "xq%d" % (2 * half + a), "x_scales%d" % (2 * half + a))
 
-        pick_table(0)
-        pick_table(1)
+        nc.vector.tensor_copy(picked_s[:], tab_s[:].indirect(offsets[:]))
+        nc.vector.tensor_copy(picked_w[:], tab_w[:].indirect(offsets[:]))
         u_q = {1: quantize(round_u(nc.scalar.copy, u_raw[1]), "un_q", "un_s")}
         deal(1)
         u_q[0] = quantize(round_u(nc.scalar.copy, u_raw[0]), "uz_q", "uz_s")
@@ -174,7 +171,7 @@ def tile_list_tgn_emaP_kernel(
             cols = slice(t * P, (t + 1) * P)
             nc.tensor.matmul_mx(
                 bank[:], lhsT=u_q[w][0][:, cols].bitcast(FP8X4), lhsT_scale=u_q[w][1][:, cols],
-                rhs=picked_w[half][:, first : first + width].bitcast(FP8X4), rhs_scale=picked_s[half][:, first : first + width],
+                rhs=picked_w[:, lo:hi].bitcast(FP8X4), rhs_scale=picked_s[:, lo:hi],
                 start=True, stop=False,
             )
             n = HALF if width == HALF else P
@@ -188,7 +185,10 @@ def tile_list_tgn_emaP_kernel(
                         start=False, stop=(a == 1 and c + n == width),
                     )
             if w == 1:
-                res = ring.tile([P, width], F32, name="cand", tag="cand", bufs=4)
+                if step == last:
+                    res = keep.tile([P, width], F32, name="cand", tag="last_cand", align_bytes=64)
+                else:
+                    res = ring.tile([P, width], F32, name="cand", tag="cand", bufs=4)
                 nc.scalar.activation(res[:], bank[:], ACT.Tanh, bias=bias_n[:, t : t + 1])
             else:
                 if step in hold_tags:
@@ -204,25 +204,36 @@ def tile_list_tgn_emaP_kernel(
         hold_tags = {1: "hold1", 2: "hold2", last: "last_hold"}
         term_tags = {2: "hold1", 3: "late1"}
         weighted_tags = {2: "raw0", last: "last_weighted"}
-        picked_h, mixes = {}, {}
+        diffs, terms, mixes = {}, {}, {}
 
-        def fetch(t):
-            picked_h[t] = keep.tile([P, J], F32, name="picked_h%d" % t, tag="hold2" if t == PACK - 1 else "picked_h%d" % t, align_bytes=64)
-            nc.vector.tensor_copy(picked_h[t][:], state[t][:].indirect(offsets[:]))
-
-        def blend(step):
+        def window(step):
             t, lo, hi = STEPS[step]
-            diff, cand = picked_h[t][:, lo:hi], cands[step]
-            mix = diff
+            return state[t][:].indirect(offsets[:, lo // 16 : hi // 16])
+
+        def own(tag, width=HALF):
+            return keep.tile([P, width], F32, name="diff", tag=tag, align_bytes=64)
+
+        def fetch_diff(step, diff):
+            diffs[step] = diff
+            nc.vector.tensor_tensor(diff, window(step), cands[step][:], ALU.subtract)
+
+        def fetch(step, diff):
+            diffs[step] = diff
+            nc.vector.tensor_copy(diff, window(step))
+
+        def product(step, engine):
+            term = diffs[step]
+            if step in term_tags:
+                term = keep.tile([P, HALF], F32, name="term", tag=term_tags[step], align_bytes=64)[:]
+            engine.tensor_tensor(term, diffs[step], holds[step][:], ALU.mult)
+            terms[step] = term
+
+        def turn(step):
+            t, lo, hi = STEPS[step]
+            cand, term, mix = cands[step], terms[step], diffs[step]
             if step == 1:
                 mix = keep.tile([P, hi - lo], F32, name="mix", tag="late0", align_bytes=64)[:]
             mixes[step] = mix
-            engine = nc.vector if step < 2 else nc.gpsimd
-            term = diff
-            if step in term_tags:
-                term = keep.tile([P, hi - lo], F32, name="term", tag=term_tags[step], align_bytes=64)[:]
-            engine.tensor_tensor(term, diff, cand[:], ALU.subtract)
-            engine.tensor_tensor(term, term, holds[step][:], ALU.mult)
             blocks = [slice(b, b + P) for b in range(0, hi - lo, P)]
             turned = psum.tile([P, hi - lo], F32, name="turned", tag="turned")
             for second, src in enumerate((cand, term)):
@@ -243,70 +254,88 @@ def tile_list_tgn_emaP_kernel(
                 nc.tensor.transpose(back[:, cols], weighted[:, cols], ident[:])
             nc.scalar.copy(mix, back[:])
 
-        spare = ["raw2", "raw3", "state0", "state1", "state2", "state3"]
-
         y_s = keep.tile([P, T], U8, name="y_s", align_bytes=64)
         words_out = out_1[0].rearrange("p t i -> p (t i)").bitcast(I32)
 
+        def weave(lo, hi, tag):
+            c, first = divmod(lo - J, HALF)
+            both = pairs[:, c].rearrange("p u c e -> p u (c e)").bitcast(U32).rearrange("p u c -> p c u")
+            rounded[lo] = keep.tile([P, hi - lo, PACK], BF16, name="rounded%d" % lo, tag=tag, align_bytes=64)
+            nc.scalar.copy(rounded[lo][:].bitcast(U32), both[:, first : first + hi - lo])
+
         def emit(lo, hi):
-            c, first = divmod(lo, HALF)
-            cols = slice(first, first + hi - lo)
-            copy, word = (nc.scalar.copy, U32) if c < 2 else (nc.vector.tensor_copy, I32)
-            both = pairs[c // 2][:, c % 2].rearrange("p u c e -> p u (c e)").bitcast(word).rearrange("p u c -> p c u")
-            rounded = keep.tile([P, hi - lo, PACK], BF16, name="rounded%d" % lo, tag=spare.pop(), align_bytes=64)
-            copy(rounded[:].bitcast(word), both[:, cols])
             y_w = keep.tile([P, hi - lo], U32, name="y_w%d" % lo, align_bytes=64)
-            nc.vector.quantize_mx(y_w[:].bitcast(FP8X4), y_s[:, lo:hi], rounded[:].rearrange("p c t -> p (c t)"))
+            nc.vector.quantize_mx(y_w[:].bitcast(FP8X4), y_s[:, lo:hi], rounded[lo][:].rearrange("p c t -> p (c t)"))
             nc.sync.dma_start(words_out[:, lo:hi], y_w[:].bitcast(I32))
 
         def place(step):
             t, lo, hi = STEPS[step]
-            window = page[t][:].indirect(offsets[:, lo // 16 : hi // 16])
-            nc.vector.tensor_copy(window, mixes[step])
+            nc.vector.tensor_copy(page[t][:].indirect(offsets[:, lo // 16 : hi // 16]), mixes[step])
             if hi == J:
                 nc.sync.dma_start(out_0.rearrange("(p t) c -> t p c", t=PACK)[t], page[t][:])
 
         def round_page(t):
             u, e = divmod(t, 2)
-            for c in (2, 3, 0, 1):
-                src = page[t][:, c * HALF : (c + 1) * HALF]
-                dst = pairs[c // 2][:, c % 2, u]
-                if c < 2:
-                    nc.scalar.copy(dst[:, :, e], src)
-                elif t == 3:
-                    nc.vector.tensor_copy(dst[:, :, e], src)
+            for lo in (0, HALF):
+                src, dst = page[t][:, lo : lo + HALF], rounded[lo]
+                if t == 3:
+                    nc.vector.tensor_copy(dst[:, :, t], src)
                 elif t == 2:
-                    nc.gpsimd.tensor_scalar(dst, src.unsqueeze(2).to_broadcast([P, HALF, 2]), 1.0, 0.0, ALU.mult, ALU.add)
+                    nc.gpsimd.tensor_scalar(dst[:, :, 2:4], src.unsqueeze(2).to_broadcast([P, HALF, 2]), 1.0, 0.0, ALU.mult, ALU.add)
                 else:
-                    nc.gpsimd.tensor_scalar(dst[:, :, e], src, 1.0, 0.0, ALU.mult, ALU.add)
+                    nc.gpsimd.tensor_scalar(dst[:, :, t], src, 1.0, 0.0, ALU.mult, ALU.add)
+            for c in range(2):
+                nc.scalar.copy(pairs[:, c, u, :, e], page[t][:, J + c * HALF : J + (c + 1) * HALF])
 
         def gates(step):
             cands[step] = gate(1, step)
             holds[step] = gate(0, step)
 
         gates(0)
-        fetch(0)
+        fetch(4, own("diff4")[:])
         gates(1)
-        blend(0)
-        fetch(1)
+        fetch_diff(0, own("diff0")[:])
+        product(0, nc.vector)
+        turn(0)
         gates(2)
+        fetch(5, own("diff5")[:])
+        fetch_diff(1, own("diff1")[:])
+        product(1, nc.vector)
         quantize_x((nc.scalar.copy, nc.scalar.copy), 0, HALF, keep, "late0", 1)
         quantize_x((nc.scalar.copy, nc.scalar.copy), 1, HALF, keep, "late1", 1)
-        blend(1)
-        fetch(2)
+        turn(1)
         gates(3)
-        blend(2)
-        fetch(3)
-        for step in range(3, len(STEPS)):
+        fetch(6, own("diff6")[:])
+        fetch_diff(2, own("diff2")[:])
+        product(2, nc.gpsimd)
+        turn(2)
+        both = own("hold2", J)
+        fetch(7, both[:, HALF:J])
+        fetch_diff(3, both[:, 0:HALF])
+        gates(4)
+        product(3, nc.gpsimd)
+        turn(3)
+        for step in range(PACK, len(STEPS)):
             if step < last:
                 gates(step + 1)
-            blend(step)
+            nc.gpsimd.tensor_tensor(diffs[step], diffs[step], cands[step][:], ALU.subtract)
+            product(step, nc.gpsimd)
+            turn(step)
         for step in range(len(STEPS)):
             place(step)
-        pairs = [keep.tile([P, 2, 2, HALF, 2], BF16, name="pairs", tag=tag, align_bytes=64) for tag in ("last_weighted", "last_hold")]
+        pairs = keep.tile([P, 2, 2, HALF, 2], BF16, name="pairs", tag="last_weighted", align_bytes=64)
+        rounded = {
+            lo: keep.tile([P, HALF, PACK], BF16, name="rounded%d" % lo, tag=tag, align_bytes=64)
+            for lo, tag in ((0, "last_hold"), (HALF, "last_cand"))
+        }
         for t in range(PACK):
             round_page(t)
-        for lo, hi in ((J, J + QUARTER), (J + QUARTER, J + HALF), (J + HALF, T), (0, HALF), (HALF, HALF + QUARTER), (HALF + QUARTER, 2 * HALF)):
+        woven = ((J, J + HALF, "raw2"), (J + HALF, T - QUARTER, "raw3"), (T - QUARTER, T, "state0"))
+        for lo, hi, tag in woven:
+            weave(lo, hi, tag)
+        emit(0, HALF)
+        emit(HALF, J)
+        for lo, hi, tag in woven:
             emit(lo, hi)
 
         for r in range(4):

@@ -185,10 +185,7 @@ def tile_list_tgn_emaP_kernel(
                         start=False, stop=(a == 1 and c + n == width),
                     )
             if w == 1:
-                if step == last:
-                    res = keep.tile([P, width], F32, name="cand", tag="last_cand", align_bytes=64)
-                else:
-                    res = ring.tile([P, width], F32, name="cand", tag="cand", bufs=4)
+                res = ring.tile([P, width], F32, name="cand", tag="cand", bufs=4)
                 nc.scalar.activation(res[:], bank[:], ACT.Tanh, bias=bias_n[:, t : t + 1])
             else:
                 if step in hold_tags:
@@ -254,18 +251,20 @@ def tile_list_tgn_emaP_kernel(
                 nc.tensor.transpose(back[:, cols], weighted[:, cols], ident[:])
             nc.scalar.copy(mix, back[:])
 
+        spare = ["raw2", "raw3", "state0", "state1", "state2", "state3"]
+
         y_s = keep.tile([P, T], U8, name="y_s", align_bytes=64)
         words_out = out_1[0].rearrange("p t i -> p (t i)").bitcast(I32)
 
-        def weave(lo, hi, tag):
-            c, first = divmod(lo - J, HALF)
-            both = pairs[:, c].rearrange("p u c e -> p u (c e)").bitcast(U32).rearrange("p u c -> p c u")
-            rounded[lo] = keep.tile([P, hi - lo, PACK], BF16, name="rounded%d" % lo, tag=tag, align_bytes=64)
-            nc.scalar.copy(rounded[lo][:].bitcast(U32), both[:, first : first + hi - lo])
-
         def emit(lo, hi):
+            c, first = divmod(lo, HALF)
+            cols = slice(first, first + hi - lo)
+            copy, word = (nc.scalar.copy, U32) if c < 2 else (nc.vector.tensor_copy, I32)
+            both = pairs[c // 2][:, c % 2].rearrange("p u c e -> p u (c e)").bitcast(word).rearrange("p u c -> p c u")
+            rounded = keep.tile([P, hi - lo, PACK], BF16, name="rounded%d" % lo, tag=spare.pop(), align_bytes=64)
+            copy(rounded[:].bitcast(word), both[:, cols])
             y_w = keep.tile([P, hi - lo], U32, name="y_w%d" % lo, align_bytes=64)
-            nc.vector.quantize_mx(y_w[:].bitcast(FP8X4), y_s[:, lo:hi], rounded[lo][:].rearrange("p c t -> p (c t)"))
+            nc.vector.quantize_mx(y_w[:].bitcast(FP8X4), y_s[:, lo:hi], rounded[:].rearrange("p c t -> p (c t)"))
             nc.sync.dma_start(words_out[:, lo:hi], y_w[:].bitcast(I32))
 
         def place(step):
@@ -276,16 +275,17 @@ def tile_list_tgn_emaP_kernel(
 
         def round_page(t):
             u, e = divmod(t, 2)
-            for lo in (0, HALF):
-                src, dst = page[t][:, lo : lo + HALF], rounded[lo]
-                if t == 3:
-                    nc.vector.tensor_copy(dst[:, :, t], src)
+            for c in (2, 3, 0, 1):
+                src = page[t][:, c * HALF : (c + 1) * HALF]
+                dst = pairs[c // 2][:, c % 2, u]
+                if c < 2:
+                    nc.scalar.copy(dst[:, :, e], src)
+                elif t == 3:
+                    nc.vector.tensor_copy(dst[:, :, e], src)
                 elif t == 2:
-                    nc.gpsimd.tensor_scalar(dst[:, :, 2:4], src.unsqueeze(2).to_broadcast([P, HALF, 2]), 1.0, 0.0, ALU.mult, ALU.add)
+                    nc.gpsimd.tensor_scalar(dst, src.unsqueeze(2).to_broadcast([P, HALF, 2]), 1.0, 0.0, ALU.mult, ALU.add)
                 else:
-                    nc.gpsimd.tensor_scalar(dst[:, :, t], src, 1.0, 0.0, ALU.mult, ALU.add)
-            for c in range(2):
-                nc.scalar.copy(pairs[:, c, u, :, e], page[t][:, J + c * HALF : J + (c + 1) * HALF])
+                    nc.gpsimd.tensor_scalar(dst[:, :, e], src, 1.0, 0.0, ALU.mult, ALU.add)
 
         def gates(step):
             cands[step] = gate(1, step)
@@ -323,19 +323,10 @@ def tile_list_tgn_emaP_kernel(
             turn(step)
         for step in range(len(STEPS)):
             place(step)
-        pairs = keep.tile([P, 2, 2, HALF, 2], BF16, name="pairs", tag="last_weighted", align_bytes=64)
-        rounded = {
-            lo: keep.tile([P, HALF, PACK], BF16, name="rounded%d" % lo, tag=tag, align_bytes=64)
-            for lo, tag in ((0, "last_hold"), (HALF, "last_cand"))
-        }
+        pairs = [keep.tile([P, 2, 2, HALF, 2], BF16, name="pairs", tag=tag, align_bytes=64) for tag in ("last_weighted", "last_hold")]
         for t in range(PACK):
             round_page(t)
-        woven = ((J, J + HALF, "raw2"), (J + HALF, T - QUARTER, "raw3"), (T - QUARTER, T, "state0"))
-        for lo, hi, tag in woven:
-            weave(lo, hi, tag)
-        emit(0, HALF)
-        emit(HALF, J)
-        for lo, hi, tag in woven:
+        for lo, hi in ((J, J + QUARTER), (J + QUARTER, J + HALF), (J + HALF, T), (0, HALF), (HALF, HALF + QUARTER), (HALF + QUARTER, 2 * HALF)):
             emit(lo, hi)
 
         for r in range(4):

@@ -47,14 +47,17 @@ def tile_list_tgn_emaP_kernel(
         weight_rows = keep.tile([P, P], F32, name="weight_rows")
         ident = keep.tile([P, P], F32, name="ident")
         state = [keep.tile([P, T], F32, name="state%d" % t, tag="state%d" % t, align_bytes=64) for t in range(PACK)]
-        page = [keep.tile([P, T], F32, name="page%d" % t) for t in range(PACK)]
+        page = [keep.tile([P, T], F32, name="page0")]
 
         nc.vector.memset(tab_s[:].bitcast(I32), 0)
         for w in (1, 0):
             nc.vector.memset(w_s_raw[w][:].rearrange("p a n -> p (a n)").bitcast(I32), 0)
         nc.vector.memset(weight_rows[:], 0.0)
-        for t in range(PACK):
-            nc.vector.memset(page[t][:].bitcast(I32), 0)
+        nc.vector.memset(page[0][:].bitcast(I32), 0)
+
+        def clear_page(t):
+            page.append(keep.tile([P, T], F32, name="page%d" % t, tag="page%d" % t, align_bytes=64))
+            nc.gpsimd.memset(page[t][:], 0.0)
 
         make_identity(nc, ident[:])
         warm = keep.tile([P, 1], F32, name="warm")
@@ -161,7 +164,8 @@ def tile_list_tgn_emaP_kernel(
         load_x("raw0", 1, HALF, J)
         quantize_x((nc.scalar.copy, nc.vector.tensor_copy), 0, 0)
         deal(0)
-        quantize_x((nc.scalar.copy, nc.vector.tensor_copy), 1, 0)
+        quantize_x((nc.scalar.copy, nc.vector.tensor_copy), 1, 0, keep, "page1", 1)
+        clear_page(1)
 
         def gate(w, step):
             t, lo, hi = STEPS[step]
@@ -198,8 +202,8 @@ def tile_list_tgn_emaP_kernel(
         cands, holds = {}, {}
         last = len(STEPS) - 1
 
-        hold_tags = {1: "hold1", 2: "hold2", last: "last_hold"}
-        term_tags = {2: "hold1", 3: "late1"}
+        hold_tags = {0: "page2", 1: "page3", 2: "hold2", last: "last_hold"}
+        term_tags = {}
         weighted_tags = {2: "raw0", last: "last_weighted"}
         diffs, terms, mixes = {}, {}, {}
 
@@ -217,6 +221,10 @@ def tile_list_tgn_emaP_kernel(
         def fetch(step, diff):
             diffs[step] = diff
             nc.vector.tensor_copy(diff, window(step))
+
+        def fetch_plane(t, both):
+            diffs[t], diffs[t + PACK] = both[:, 0:HALF], both[:, HALF:J]
+            nc.vector.tensor_copy(both[:], state[t][:].indirect(offsets[:]))
 
         def product(step, engine):
             term = diffs[step]
@@ -296,23 +304,25 @@ def tile_list_tgn_emaP_kernel(
         gates(1)
         fetch_diff(0, own("diff0")[:])
         product(0, nc.vector)
+        clear_page(2)
         turn(0)
         gates(2)
         fetch(5, own("diff5")[:])
         fetch_diff(1, own("diff1")[:])
         product(1, nc.vector)
+        clear_page(3)
         quantize_x((nc.scalar.copy, nc.scalar.copy), 0, HALF, keep, "late0", 1)
         quantize_x((nc.scalar.copy, nc.scalar.copy), 1, HALF, keep, "late1", 1)
         turn(1)
         gates(3)
-        fetch(6, own("diff6")[:])
-        fetch_diff(2, own("diff2")[:])
+        fetch_plane(2, own("diff2", J))
+        nc.gpsimd.tensor_tensor(diffs[2], diffs[2], cands[2][:], ALU.subtract)
         product(2, nc.gpsimd)
         turn(2)
-        both = own("hold2", J)
-        fetch(7, both[:, HALF:J])
-        fetch_diff(3, both[:, 0:HALF])
+        fetch_plane(3, own("hold2", J))
         gates(4)
+        fetched, diffs[3] = diffs[3], own("late1")[:]
+        nc.gpsimd.tensor_tensor(diffs[3], fetched, cands[3][:], ALU.subtract)
         product(3, nc.gpsimd)
         turn(3)
         for step in range(PACK, len(STEPS)):

@@ -22,6 +22,7 @@ PACK = 4
 KP = P * PACK
 HALF = 512
 QUARTER = HALF // 2
+TAB_ROW = 4
 STEPS = [(t, lo, lo + HALF) for lo in (0, HALF) for t in range(PACK)]
 
 
@@ -41,22 +42,24 @@ def tile_list_tgn_emaP_kernel(
         w_raw = [keep.tile([P, 2, 2 * N], U8, name="w_raw%d" % w) for w in range(2)]
         tab_w = keep.tile([P, T], U32, name="tab_w", align_bytes=64)
         bias_n = keep.tile([P, PACK], F32, name="bias_n")
-        bias_z = keep.tile([P, PACK], F32, name="bias_z")
+        bias_rows = keep.tile([P, N], F32, name="bias_rows")
         neg_bz = keep.tile([P, PACK], F32, name="neg_bz")
         weight_t = keep.tile([P, J // P], F32, name="weight_t")
         weight_rows = keep.tile([P, P], F32, name="weight_rows")
         ident = keep.tile([P, P], F32, name="ident")
         state = [keep.tile([P, T], F32, name="state%d" % t, tag="state%d" % t, align_bytes=64) for t in range(PACK)]
-        page = [keep.tile([P, T], F32, name="page0")]
+        page = {t: keep.tile([P, T], F32, name="page%d" % t) for t in (0, 3)}
 
         nc.vector.memset(tab_s[:].bitcast(I32), 0)
         for w in (1, 0):
             nc.vector.memset(w_s_raw[w][:].rearrange("p a n -> p (a n)").bitcast(I32), 0)
+        nc.vector.memset(bias_rows[:], 0.0)
         nc.vector.memset(weight_rows[:], 0.0)
-        nc.vector.memset(page[0][:].bitcast(I32), 0)
+        for t in (0, 3):
+            nc.vector.memset(page[t][:].bitcast(I32), 0)
 
         def clear_page(t):
-            page.append(keep.tile([P, T], F32, name="page%d" % t, tag="page%d" % t, align_bytes=64))
+            page[t] = keep.tile([P, T], F32, name="page%d" % t, tag="page%d" % t, align_bytes=64)
             nc.gpsimd.memset(page[t][:], 0.0)
 
         make_identity(nc, ident[:])
@@ -77,7 +80,7 @@ def tile_list_tgn_emaP_kernel(
             x_raw[a, lo] = load_rows(tag, x[a * KP : (a + 1) * KP, lo:hi])
 
         def load_tab_scales(q):
-            nc.sync.dma_start(tab_s[q:P:32, :].bitcast(I32), tab_scales[0, q:16:4, :].bitcast(I32))
+            nc.sync.dma_start(tab_s[TAB_ROW + q : P : 32, :].bitcast(I32), tab_scales[0, q:16:4, :].bitcast(I32))
 
         def load_w_scales(w):
             for q in range(4):
@@ -88,10 +91,10 @@ def tile_list_tgn_emaP_kernel(
 
         u_raw = {}
         nc.sync.dma_start(offsets[:], offs)
+        nc.sync.dma_start(tab_w[:].bitcast(I32), tab_words[0].rearrange("p t i -> p (t i)").bitcast(I32))
         for q in range(4):
             load_tab_scales(q)
         u_raw[1] = load_rows("raw1", un)
-        nc.sync.dma_start(tab_w[:].bitcast(I32), tab_words[0].rearrange("p t i -> p (t i)").bitcast(I32))
         u_raw[0] = load_rows("raw0", uz)
         load_w_scales(1)
         for w in (1, 0):
@@ -99,14 +102,18 @@ def tile_list_tgn_emaP_kernel(
         load_x("raw2", 0, 0, HALF)
         load_w_scales(0)
         load_x("raw3", 1, 0, HALF)
-        nc.sync.dma_start(bias_n[:], bn.rearrange("(p t) -> p t", t=PACK))
-        nc.sync.dma_start(bias_z[:], bz.rearrange("(p t) -> p t", t=PACK))
+        for row, bias in enumerate((bn, bz)):
+            nc.sync.dma_start(bias_rows[row : row + 1, :], bias.unsqueeze(0))
         load_state(0)
         load_state(1)
         nc.sync.dma_start(weight_rows[0 : J // P, :], wgo[0].rearrange("(b p) -> b p", p=P))
         load_state(2)
         load_state(3)
-        nc.scalar.mul(neg_bz[:], bias_z[:], -1.0)
+        bias_bank = psum.tile([P, PACK, P], F32, name="bias_bank", tag="turned")
+        for t in range(PACK):
+            nc.tensor.transpose(bias_bank[:, t, :], bias_rows[:, t:N:PACK], ident[:])
+        nc.scalar.copy(bias_n[:], bias_bank[:, :, 0])
+        nc.scalar.mul(neg_bz[:], bias_bank[:, :, 1], -1.0)
         weight_bank = psum.tile([P, P], F32, name="weight_bank", tag="back", bufs=1)
         nc.tensor.transpose(weight_bank[:], weight_rows[:], ident[:])
         nc.scalar.copy(weight_t[:], weight_bank[:, 0 : J // P])
@@ -143,20 +150,24 @@ def tile_list_tgn_emaP_kernel(
 
         x_q = {}
 
-        def quantize_x(copies, a, lo, pool=ring, tag="grouped", bufs=3, code_tag=None):
+        def gpsimd_round(dst, src):
+            nc.gpsimd.tensor_scalar(
+                dst.rearrange("p c i e -> p c e i"), src.rearrange("p c i e -> p c e i"), 1.0, 0.0, ALU.mult, ALU.add
+            )
+
+        def quantize_x(copies, a, lo, pool=ring, tag="grouped", bufs=3, code_tag=None, split=HALF // 2):
             raw = x_raw[a, lo]
             grouped = pool.tile([P, PACK * HALF], BF16, name="grouped", tag=tag, align_bytes=64, bufs=bufs)
-            width = HALF // len(copies)
-            for k, copy in enumerate(copies):
+            for copy, (c0, c1) in zip(copies, ((0, split), (split, HALF))):
                 copy(
-                    grouped[:, PACK * k * width : PACK * (k + 1) * width].rearrange("p (c e i) -> p c i e", e=4, i=PACK),
-                    raw[:, :, k * width : (k + 1) * width].rearrange("p i (c e) -> p c i e", e=4),
+                    grouped[:, PACK * c0 : PACK * c1].rearrange("p (c e i) -> p c i e", e=4, i=PACK),
+                    raw[:, :, c0:c1].rearrange("p i (c e) -> p c i e", e=4),
                 )
             half = lo // HALF
             x_q[a, half] = quantize(grouped, code_tag or "xq%d" % (2 * half + a), "x_scales%d" % (2 * half + a))
 
-        nc.vector.tensor_copy(picked_s[:], tab_s[:].indirect(offsets[:]))
         nc.vector.tensor_copy(picked_w[:], tab_w[:].indirect(offsets[:]))
+        nc.vector.tensor_copy(picked_s[:], tab_s[:].indirect(offsets[:]))
         u_q = {1: quantize(round_u(nc.scalar.copy, u_raw[1]), "un_q", "un_s")}
         deal(1)
         u_q[0] = quantize(round_u(nc.scalar.copy, u_raw[0]), "uz_q", "uz_s")
@@ -164,7 +175,7 @@ def tile_list_tgn_emaP_kernel(
         load_x("raw0", 1, HALF, J)
         quantize_x((nc.scalar.copy, nc.vector.tensor_copy), 0, 0)
         deal(0)
-        quantize_x((nc.scalar.copy, nc.vector.tensor_copy), 1, 0, keep, "page1", 1)
+        quantize_x((nc.scalar.copy, nc.vector.tensor_copy), 1, 0, keep, "page1", 1, split=160)
         clear_page(1)
 
         def gate(w, step):
@@ -175,7 +186,7 @@ def tile_list_tgn_emaP_kernel(
             cols = slice(t * P, (t + 1) * P)
             nc.tensor.matmul_mx(
                 bank[:], lhsT=u_q[w][0][:, cols].bitcast(FP8X4), lhsT_scale=u_q[w][1][:, cols],
-                rhs=picked_w[:, lo:hi].bitcast(FP8X4), rhs_scale=picked_s[:, lo:hi],
+                rhs=picked_w[:, lo:hi].bitcast(FP8X4), rhs_scale=picked_s[TAB_ROW:P, lo:hi],
                 start=True, stop=False,
             )
             n = HALF if width == HALF else P
@@ -202,7 +213,7 @@ def tile_list_tgn_emaP_kernel(
         cands, holds = {}, {}
         last = len(STEPS) - 1
 
-        hold_tags = {0: "page2", 1: "page3", 2: "hold2", last: "last_hold"}
+        hold_tags = {0: "page2", 2: "hold2", last: "last_hold"}
         term_tags = {}
         weighted_tags = {2: "raw0", last: "last_weighted"}
         diffs, terms, mixes = {}, {}, {}
@@ -309,10 +320,9 @@ def tile_list_tgn_emaP_kernel(
         gates(2)
         fetch(5, own("diff5")[:])
         fetch_diff(1, own("diff1")[:])
-        product(1, nc.vector)
-        clear_page(3)
+        product(1, nc.gpsimd)
         quantize_x((nc.scalar.copy, nc.scalar.copy), 0, HALF, keep, "late0", 1)
-        quantize_x((nc.scalar.copy, nc.scalar.copy), 1, HALF, keep, "late1", 1)
+        quantize_x((nc.scalar.copy, gpsimd_round), 1, HALF, keep, "late1", 1)
         turn(1)
         gates(3)
         fetch_plane(2, own("diff2", J))

@@ -47,7 +47,7 @@ def tile_list_tgn_emaP_kernel(
         weight_t = keep.tile([P, J // P], F32, name="weight_t")
         weight_rows = keep.tile([P, P], F32, name="weight_rows")
         ident = keep.tile([P, P], F32, name="ident")
-        state = [keep.tile([P, T], F32, name="state%d" % t, tag="state%d" % t, align_bytes=64) for t in range(PACK)]
+        state = [keep.tile([P, T], F32, name="state%d" % t, tag="state%d" % t, align_bytes=64) for t in range(PACK - 1)]
         page = {t: keep.tile([P, T], F32, name="page%d" % t) for t in (0, 3)}
 
         nc.vector.memset(tab_s[:].bitcast(I32), 0)
@@ -84,7 +84,7 @@ def tile_list_tgn_emaP_kernel(
 
         def load_w_scales(w):
             for q in range(4):
-                nc.sync.dma_start(
+                (nc.sync, nc.gpsimd)[w].dma_start(
                     w_s_raw[w][q:P:32].bitcast(I32),
                     (wz_scales, wn_scales)[w][:, q:16:4, :].rearrange("a r n -> r a n").bitcast(I32),
                 )
@@ -99,8 +99,8 @@ def tile_list_tgn_emaP_kernel(
         load_w_scales(1)
         for w in (1, 0):
             nc.sync.dma_start(w_raw[w][:].bitcast(I32), (wz_words, wn_words)[w].rearrange("a p b -> p a b").bitcast(I32))
-        load_x("raw2", 0, 0, HALF)
         load_w_scales(0)
+        load_x("raw2", 0, 0, HALF)
         load_x("raw3", 1, 0, HALF)
         for row, bias in enumerate((bn, bz)):
             nc.sync.dma_start(bias_rows[row : row + 1, :], bias.unsqueeze(0))
@@ -108,7 +108,6 @@ def tile_list_tgn_emaP_kernel(
         load_state(1)
         nc.sync.dma_start(weight_rows[0 : J // P, :], wgo[0].rearrange("(b p) -> b p", p=P))
         load_state(2)
-        load_state(3)
         bias_bank = psum.tile([P, PACK, P], F32, name="bias_bank", tag="turned")
         for t in range(PACK):
             nc.tensor.transpose(bias_bank[:, t, :], bias_rows[:, t:N:PACK], ident[:])
@@ -150,18 +149,14 @@ def tile_list_tgn_emaP_kernel(
 
         x_q = {}
 
-        def gpsimd_round(dst, src):
-            nc.gpsimd.tensor_scalar(
-                dst.rearrange("p c i e -> p c e i"), src.rearrange("p c i e -> p c e i"), 1.0, 0.0, ALU.mult, ALU.add
-            )
-
         def quantize_x(copies, a, lo, pool=ring, tag="grouped", bufs=3, code_tag=None, split=HALF // 2):
             raw = x_raw[a, lo]
             grouped = pool.tile([P, PACK * HALF], BF16, name="grouped", tag=tag, align_bytes=64, bufs=bufs)
-            for copy, (c0, c1) in zip(copies, ((0, split), (split, HALF))):
+            parts = raw if isinstance(raw, list) else [raw[:, :, 0:split], raw[:, :, split:HALF]]
+            for copy, part, (c0, c1) in zip(copies, parts, ((0, split), (split, HALF))):
                 copy(
                     grouped[:, PACK * c0 : PACK * c1].rearrange("p (c e i) -> p c i e", e=4, i=PACK),
-                    raw[:, :, c0:c1].rearrange("p i (c e) -> p c i e", e=4),
+                    part.rearrange("p i (c e) -> p c i e", e=4),
                 )
             half = lo // HALF
             x_q[a, half] = quantize(grouped, code_tag or "xq%d" % (2 * half + a), "x_scales%d" % (2 * half + a))
@@ -172,11 +167,17 @@ def tile_list_tgn_emaP_kernel(
         deal(1)
         u_q[0] = quantize(round_u(nc.scalar.copy, u_raw[0]), "uz_q", "uz_s")
         load_x("raw1", 0, HALF, J)
-        load_x("raw0", 1, HALF, J)
         quantize_x((nc.scalar.copy, nc.vector.tensor_copy), 0, 0)
+        state.append(keep.tile([P, T], F32, name="state3", tag="raw2", align_bytes=64))
+        load_state(3)
         deal(0)
         quantize_x((nc.scalar.copy, nc.vector.tensor_copy), 1, 0, keep, "page1", 1, split=160)
         clear_page(1)
+        last_raw = keep.tile([P, 2, PACK, QUARTER], F32, name="last_raw", tag="raw3", align_bytes=64)
+        x_raw[1, HALF] = [last_raw[:, k] for k in range(2)]
+        for k in range(2):
+            lo = HALF + k * QUARTER
+            nc.sync.dma_start(last_raw[:, k], x[KP : 2 * KP, lo : lo + QUARTER].rearrange("(p i) c -> p i c", i=PACK))
 
         def gate(w, step):
             t, lo, hi = STEPS[step]
@@ -213,9 +214,9 @@ def tile_list_tgn_emaP_kernel(
         cands, holds = {}, {}
         last = len(STEPS) - 1
 
-        hold_tags = {0: "page2", 2: "hold2", last: "last_hold"}
-        term_tags = {}
-        weighted_tags = {2: "raw0", last: "last_weighted"}
+        hold_tags = {0: "page2", 1: "hold1", 2: "hold2", last: "last_hold"}
+        term_tags = {1: "state2", 3: "late1"}
+        weighted_tags = {1: "raw1", last: "last_weighted"}
         diffs, terms, mixes = {}, {}, {}
 
         def window(step):
@@ -233,10 +234,6 @@ def tile_list_tgn_emaP_kernel(
             diffs[step] = diff
             nc.vector.tensor_copy(diff, window(step))
 
-        def fetch_plane(t, both):
-            diffs[t], diffs[t + PACK] = both[:, 0:HALF], both[:, HALF:J]
-            nc.vector.tensor_copy(both[:], state[t][:].indirect(offsets[:]))
-
         def product(step, engine):
             term = diffs[step]
             if step in term_tags:
@@ -248,7 +245,7 @@ def tile_list_tgn_emaP_kernel(
             t, lo, hi = STEPS[step]
             cand, term, mix = cands[step], terms[step], diffs[step]
             if step == 1:
-                mix = keep.tile([P, hi - lo], F32, name="mix", tag="late0", align_bytes=64)[:]
+                mix = behind_rounding[:, 0:HALF]
             mixes[step] = mix
             blocks = [slice(b, b + P) for b in range(0, hi - lo, P)]
             turned = psum.tile([P, hi - lo], F32, name="turned", tag="turned")
@@ -258,7 +255,9 @@ def tile_list_tgn_emaP_kernel(
                         turned[:, cols], lhsT=src[:, cols], rhs=ident[:], is_transpose=True,
                         start=(second == 0 and b == 0), stop=(second == 1 and b == len(blocks) - 1),
                     )
-            if step in weighted_tags:
+            if step == 2:
+                weighted = behind_rounding[:, HALF:J]
+            elif step in weighted_tags:
                 weighted = keep.tile([P, hi - lo], F32, name="weighted", tag=weighted_tags[step], align_bytes=64)
             else:
                 weighted = ring.tile([P, hi - lo], F32, name="weighted", tag="weighted")
@@ -270,7 +269,7 @@ def tile_list_tgn_emaP_kernel(
                 nc.tensor.transpose(back[:, cols], weighted[:, cols], ident[:])
             nc.scalar.copy(mix, back[:])
 
-        spare = ["raw2", "raw3", "state0", "state1", "state2", "state3"]
+        spare = ["raw2", "raw3", "state0", "state1", "state2", "raw0"]
 
         y_s = keep.tile([P, T], U8, name="y_s", align_bytes=64)
         words_out = out_1[0].rearrange("p t i -> p (t i)").bitcast(I32)
@@ -320,19 +319,20 @@ def tile_list_tgn_emaP_kernel(
         gates(2)
         fetch(5, own("diff5")[:])
         fetch_diff(1, own("diff1")[:])
+        gates(3)
+        fetch(6, own("diff6")[:])
+        fetch_diff(2, own("diff2")[:])
         product(1, nc.gpsimd)
         quantize_x((nc.scalar.copy, nc.scalar.copy), 0, HALF, keep, "late0", 1)
-        quantize_x((nc.scalar.copy, gpsimd_round), 1, HALF, keep, "late1", 1)
+        quantize_x((nc.scalar.copy, nc.scalar.copy), 1, HALF, keep, "late1", 1)
+        behind_rounding = own("raw3", J)
         turn(1)
-        gates(3)
-        fetch_plane(2, own("diff2", J))
-        nc.gpsimd.tensor_tensor(diffs[2], diffs[2], cands[2][:], ALU.subtract)
         product(2, nc.gpsimd)
         turn(2)
-        fetch_plane(3, own("hold2", J))
+        both = own("hold2", J)
+        fetch(7, both[:, HALF:J])
+        fetch_diff(3, both[:, 0:HALF])
         gates(4)
-        fetched, diffs[3] = diffs[3], own("late1")[:]
-        nc.gpsimd.tensor_tensor(diffs[3], fetched, cands[3][:], ALU.subtract)
         product(3, nc.gpsimd)
         turn(3)
         for step in range(PACK, len(STEPS)):

@@ -21,9 +21,10 @@ P = 128
 PACK = 4
 KP = P * PACK
 HALF = 512
-QUARTER = HALF // 2
+QUARTER = 256
 TAB_ROW = 4
-STEPS = [(t, lo, lo + HALF) for lo in (0, HALF) for t in range(PACK)]
+CAND, HOLD = 1, 0
+ORDER = (2, 0, 1, 3)
 
 
 def tile_list_tgn_emaP_kernel(
@@ -34,320 +35,334 @@ def tile_list_tgn_emaP_kernel(
     with ExitStack() as ctx:
         keep = ctx.enter_context(tc.tile_pool(name="keep", bufs=1))
         ring = ctx.enter_context(tc.tile_pool(name="ring", bufs=2))
-        psum = ctx.enter_context(tc.psum_pool(name="psum", bufs=2))
+        psum = ctx.enter_context(tc.psum_pool(name="psum", bufs=1))
+
+        def own(tag, shape, dtype=F32):
+            return keep.tile([P] + shape, dtype, name=tag, tag=tag, align_bytes=64)
+
+        def bank(k, shape):
+            return psum.tile([P] + shape, F32, name="bank%d" % k, tag="bank%d" % k)
 
         offsets = keep.tile([P, J // 16], U16, name="offsets")
-        tab_s = keep.tile([P, T], U8, name="tab_s", align_bytes=64)
-        w_s_raw = [keep.tile([P, 2, N], U8, name="w_s_raw%d" % w, align_bytes=64) for w in range(2)]
-        w_raw = [keep.tile([P, 2, 2 * N], U8, name="w_raw%d" % w) for w in range(2)]
-        tab_w = keep.tile([P, T], U32, name="tab_w", align_bytes=64)
-        bias_n = keep.tile([P, PACK], F32, name="bias_n")
-        bias_rows = keep.tile([P, N], F32, name="bias_rows")
-        neg_bz = keep.tile([P, PACK], F32, name="neg_bz")
-        weight_t = keep.tile([P, J // P], F32, name="weight_t")
-        weight_rows = keep.tile([P, P], F32, name="weight_rows")
-        ident = keep.tile([P, P], F32, name="ident")
-        state = [keep.tile([P, T], F32, name="state%d" % t, tag="state%d" % t, align_bytes=64) for t in range(PACK - 1)]
-        page = {t: keep.tile([P, T], F32, name="page%d" % t) for t in (0, 3)}
+        tab_s = own("tab_s", [T], U8)
+        tab_w = own("tab_w", [T], U32)
+        w_s_raw = [own("w_s_raw%d" % w, [2, N], U8) for w in range(2)]
+        w_raw = [own("w_raw%d" % w, [2, 2 * N], U8) for w in range(2)]
+        bias_n = own("bias_n", [PACK])
+        neg_bz = own("neg_bz", [PACK])
+        bias_rows = own("bias_rows", [N])
+        weight_t = own("weight_t", [J // P])
+        weight_rows = own("weight_rows", [P])
+        ident = own("ident", [P])
+        page = {2: own("page2", [T])}
 
-        nc.vector.memset(tab_s[:].bitcast(I32), 0)
-        for w in (1, 0):
+        nc.gpsimd.memset(tab_s[:].bitcast(I32), 0)
+        for w in (CAND, HOLD):
             nc.vector.memset(w_s_raw[w][:].rearrange("p a n -> p (a n)").bitcast(I32), 0)
         nc.vector.memset(bias_rows[:], 0.0)
         nc.vector.memset(weight_rows[:], 0.0)
-        for t in (0, 3):
-            nc.vector.memset(page[t][:].bitcast(I32), 0)
+        nc.vector.memset(page[2][:].bitcast(I32), 0)
 
-        def clear_page(t):
-            page[t] = keep.tile([P, T], F32, name="page%d" % t, tag="page%d" % t, align_bytes=64)
+        def clear_page(t, tag):
+            page[t] = own(tag, [T])
             nc.gpsimd.memset(page[t][:], 0.0)
 
         make_identity(nc, ident[:])
-        warm = keep.tile([P, 1], F32, name="warm")
+        warm = own("warm", [1])
         nc.scalar.activation(warm[:], ident[:, 0:1], ACT.Sigmoid)
 
-        def load_rows(tag, rows):
-            raw = keep.tile([P, PACK, rows.shape[1]], F32, name=tag, tag=tag, align_bytes=64)
-            nc.sync.dma_start(raw[:], rows.rearrange("(p i) c -> p i c", i=PACK))
-            return raw
+        def load_rows(dst, rows):
+            nc.sync.dma_start(dst, rows.rearrange("(p i) c -> p i c", i=PACK))
 
-        def load_state(t):
+        state = {}
+
+        def load_state(t, tag):
+            state[t] = own(tag, [T])
             nc.sync.dma_start(state[t][:], hT.rearrange("(p t) c -> t p c", t=PACK)[t])
 
-        x_raw = {}
-
         def load_x(tag, a, lo, hi):
-            x_raw[a, lo] = load_rows(tag, x[a * KP : (a + 1) * KP, lo:hi])
+            raw = own(tag, [PACK, hi - lo])
+            load_rows(raw[:], x[a * KP : (a + 1) * KP, lo:hi])
+            return raw
 
-        def load_tab_scales(q):
-            nc.sync.dma_start(tab_s[TAB_ROW + q : P : 32, :].bitcast(I32), tab_scales[0, q:16:4, :].bitcast(I32))
-
-        def load_w_scales(w):
+        def load_w_scales(w, queue):
             for q in range(4):
-                (nc.sync, nc.gpsimd)[w].dma_start(
+                queue.dma_start(
                     w_s_raw[w][q:P:32].bitcast(I32),
                     (wz_scales, wn_scales)[w][:, q:16:4, :].rearrange("a r n -> r a n").bitcast(I32),
                 )
 
-        u_raw = {}
         nc.sync.dma_start(offsets[:], offs)
         nc.sync.dma_start(tab_w[:].bitcast(I32), tab_words[0].rearrange("p t i -> p (t i)").bitcast(I32))
         for q in range(4):
-            load_tab_scales(q)
-        u_raw[1] = load_rows("raw1", un)
-        u_raw[0] = load_rows("raw0", uz)
-        load_w_scales(1)
-        for w in (1, 0):
+            nc.sync.dma_start(tab_s[TAB_ROW + q : P : 32, :].bitcast(I32), tab_scales[0, q:16:4, :].bitcast(I32))
+        u_raw = {w: own("u_raw%d" % w, [PACK, N]) for w in (CAND, HOLD)}
+        load_w_scales(CAND, nc.gpsimd)
+        for w in (CAND, HOLD):
+            load_rows(u_raw[w][:], (uz, un)[w])
+            nc.sync.dma_start(bias_rows[1 - w : 2 - w, :], (bz, bn)[w].unsqueeze(0))
             nc.sync.dma_start(w_raw[w][:].bitcast(I32), (wz_words, wn_words)[w].rearrange("a p b -> p a b").bitcast(I32))
-        load_w_scales(0)
-        load_x("raw2", 0, 0, HALF)
-        load_x("raw3", 1, 0, HALF)
-        for row, bias in enumerate((bn, bz)):
-            nc.sync.dma_start(bias_rows[row : row + 1, :], bias.unsqueeze(0))
-        load_state(0)
-        load_state(1)
-        nc.sync.dma_start(weight_rows[0 : J // P, :], wgo[0].rearrange("(b p) -> b p", p=P))
-        load_state(2)
-        bias_bank = psum.tile([P, PACK, P], F32, name="bias_bank", tag="turned")
+        load_w_scales(HOLD, nc.sync)
+        x_first = [load_x("x_first%d" % a, a, 0, HALF) for a in range(2)]
+        for t in ORDER[:3]:
+            load_state(t, "state%d" % t)
+            if t == ORDER[1]:
+                nc.sync.dma_start(weight_rows[0 : J // P, :], wgo[0].rearrange("(b p) -> b p", p=P))
+
+        bias_bank = bank(4, [PACK, P])
         for t in range(PACK):
             nc.tensor.transpose(bias_bank[:, t, :], bias_rows[:, t:N:PACK], ident[:])
         nc.scalar.copy(bias_n[:], bias_bank[:, :, 0])
         nc.scalar.mul(neg_bz[:], bias_bank[:, :, 1], -1.0)
-        weight_bank = psum.tile([P, P], F32, name="weight_bank", tag="back", bufs=1)
+        weight_bank = bank(6, [P])
         nc.tensor.transpose(weight_bank[:], weight_rows[:], ident[:])
         nc.scalar.copy(weight_t[:], weight_bank[:, 0 : J // P])
 
-        w_q = [keep.tile([P, 2, 2 * N], U8, name="w_q%d" % w, align_bytes=64) for w in range(2)]
-        w_s = [keep.tile([P, 2, N], U8, name="w_s%d" % w, align_bytes=64) for w in range(2)]
+        picked_w = own("picked_w", [J], U32)
+        picked_s = own("picked_s", [J], U8)
+        nc.vector.tensor_copy(picked_w[:], tab_w[:].indirect(offsets[:]))
+        nc.vector.tensor_copy(picked_s[:], tab_s[:].indirect(offsets[:]))
 
-        def deal(w):
+        w_q = [own("w_q%d" % w, [2, 2 * N], U8) for w in range(2)]
+        w_s = [own("w_s%d" % w, [2, N], U8) for w in range(2)]
+
+        def deal_words(w):
             nc.vector.tensor_copy(
                 w_q[w][:].bitcast(U16).rearrange("p a (t m) -> p a t m", t=PACK),
                 w_raw[w][:].bitcast(U16).rearrange("p a (m t) -> p a t m", t=PACK),
             )
+
+        def deal_scales(w):
             nc.vector.tensor_copy(
                 w_s[w][:].rearrange("p a (t m) -> p a t m", t=PACK),
                 w_s_raw[w][:].rearrange("p a (m t) -> p a t m", t=PACK),
             )
 
-        picked_w = keep.tile([P, J], U32, name="picked_w", align_bytes=64)
-        picked_s = keep.tile([P, J], U8, name="picked_s", align_bytes=64)
-
-        def quantize(grouped, tag, scale_name):
-            codes = keep.tile([P, HALF], U32, name=tag, tag=tag, align_bytes=64)
-            scales = keep.tile([P, HALF], U8, name=scale_name, align_bytes=64)
+        def quantize(grouped, name, width=HALF):
+            codes = own(name + "_q", [width], U32)
+            scales = own(name + "_s", [width], U8)
             nc.vector.quantize_mx(codes[:].bitcast(FP8X4), scales[:], grouped[:])
             return codes, scales
 
-        def round_u(copy, raw):
-            grouped = ring.tile([P, PACK * HALF], BF16, name="grouped", tag="grouped", align_bytes=64, bufs=3)
-            copy(
+        def gpsimd_round(dst, src):
+            nc.gpsimd.tensor_scalar(dst, src, 1.0, 0.0, ALU.mult, ALU.add)
+
+        def grouped_tile():
+            return ring.tile([P, PACK * HALF], BF16, name="grouped", tag="grouped", align_bytes=64)
+
+        def round_u(w):
+            grouped = grouped_tile()
+            nc.scalar.copy(
                 grouped[:].rearrange("p (t m i) -> p m t i", t=PACK, i=PACK),
-                raw[:].rearrange("p i (m t) -> p m t i", t=PACK),
+                u_raw[w][:].rearrange("p i (m t) -> p m t i", t=PACK),
             )
             return grouped
 
+        def round_x(copy, grouped, at, raw, c0, c1):
+            copy(
+                grouped[:, PACK * (at + c0) : PACK * (at + c1)].rearrange("p (c e i) -> p c i e", e=4, i=PACK),
+                raw[:, :, c0:c1].rearrange("p i (c e) -> p c i e", e=4),
+            )
+
         x_q = {}
 
-        def quantize_x(copies, a, lo, pool=ring, tag="grouped", bufs=3, code_tag=None, split=HALF // 2):
-            raw = x_raw[a, lo]
-            grouped = pool.tile([P, PACK * HALF], BF16, name="grouped", tag=tag, align_bytes=64, bufs=bufs)
-            parts = raw if isinstance(raw, list) else [raw[:, :, 0:split], raw[:, :, split:HALF]]
-            for copy, part, (c0, c1) in zip(copies, parts, ((0, split), (split, HALF))):
-                copy(
-                    grouped[:, PACK * c0 : PACK * c1].rearrange("p (c e i) -> p c i e", e=4, i=PACK),
-                    part.rearrange("p i (c e) -> p c i e", e=4),
-                )
-            half = lo // HALF
-            x_q[a, half] = quantize(grouped, code_tag or "xq%d" % (2 * half + a), "x_scales%d" % (2 * half + a))
+        def quantize_half(raw, a, lo, split):
+            name = "x%d_%d" % (a, lo)
+            grouped = own(name + "_grouped", [PACK * HALF], BF16)
+            round_x(nc.scalar.copy, grouped, 0, raw, 0, split)
+            round_x(nc.vector.tensor_copy, grouped, 0, raw, split, HALF)
+            x_q[a, lo] = quantize(grouped, name) + (0,)
 
-        nc.vector.tensor_copy(picked_w[:], tab_w[:].indirect(offsets[:]))
-        nc.vector.tensor_copy(picked_s[:], tab_s[:].indirect(offsets[:]))
-        u_q = {1: quantize(round_u(nc.scalar.copy, u_raw[1]), "un_q", "un_s")}
-        deal(1)
-        u_q[0] = quantize(round_u(nc.scalar.copy, u_raw[0]), "uz_q", "uz_s")
-        load_x("raw1", 0, HALF, J)
-        quantize_x((nc.scalar.copy, nc.vector.tensor_copy), 0, 0)
-        state.append(keep.tile([P, T], F32, name="state3", tag="raw2", align_bytes=64))
-        load_state(3)
-        deal(0)
-        quantize_x((nc.scalar.copy, nc.vector.tensor_copy), 1, 0, keep, "page1", 1, split=160)
-        clear_page(1)
-        last_raw = keep.tile([P, 2, PACK, QUARTER], F32, name="last_raw", tag="raw3", align_bytes=64)
-        x_raw[1, HALF] = [last_raw[:, k] for k in range(2)]
+        def quantize_late():
+            grouped = own("x_late_grouped", [PACK * J], BF16)
+            round_x(nc.scalar.copy, grouped, 0, x_late, 0, HALF - P)
+            round_x(gpsimd_round, grouped, 0, x_late, HALF - P, HALF)
+            for k in range(2):
+                round_x(nc.scalar.copy, grouped, HALF + k * QUARTER, x_last[:, k], 0, QUARTER)
+            codes, scales = quantize(grouped, "x_late", J)
+            for a in range(2):
+                x_q[a, HALF] = (codes, scales, a * HALF)
+
+        u_q = {CAND: quantize(round_u(CAND), "un")}
+        deal_words(CAND)
+        deal_scales(CAND)
+        u_q[HOLD] = quantize(round_u(HOLD), "uz")
+        x_late = load_x("u_raw1", 0, HALF, J)
+        x_last = own("u_raw0", [2, PACK, QUARTER])
         for k in range(2):
-            lo = HALF + k * QUARTER
-            nc.sync.dma_start(last_raw[:, k], x[KP : 2 * KP, lo : lo + QUARTER].rearrange("(p i) c -> p i c", i=PACK))
+            load_rows(x_last[:, k], x[KP : 2 * KP, HALF + k * QUARTER : HALF + (k + 1) * QUARTER])
+        deal_words(HOLD)
+        deal_scales(HOLD)
+        quantize_half(x_first[0], 0, 0, 256)
+        quantize_half(x_first[1], 1, 0, 160)
+        clear_page(0, "x1_0_grouped")
+        load_state(3, "x_first0")
+        gate_banks = []
 
-        def gate(w, step):
-            t, lo, hi = STEPS[step]
-            half, first = divmod(lo, HALF)
-            width = hi - lo
-            bank = psum.tile([P, width], F32, name="bank", tag="bank", bufs=4)
+        def gate(w, step, into=None):
+            t, lo, hi = step
+            gate_banks.append(len(gate_banks) % 4)
+            sums = bank(gate_banks[-1], [hi - lo])
             cols = slice(t * P, (t + 1) * P)
             nc.tensor.matmul_mx(
-                bank[:], lhsT=u_q[w][0][:, cols].bitcast(FP8X4), lhsT_scale=u_q[w][1][:, cols],
+                sums[:], lhsT=u_q[w][0][:, cols].bitcast(FP8X4), lhsT_scale=u_q[w][1][:, cols],
                 rhs=picked_w[:, lo:hi].bitcast(FP8X4), rhs_scale=picked_s[TAB_ROW:P, lo:hi],
                 start=True, stop=False,
             )
-            n = HALF if width == HALF else P
+            n = HALF
             for a in range(2):
-                codes, scales = x_q[a, half]
-                for c in range(0, width, n):
+                for c in range(lo, hi, n):
+                    codes, scales, first = x_q[a, c]
                     nc.tensor.matmul_mx(
-                        bank[:, c : c + n], lhsT=w_q[w][:, a, 2 * t * P : 2 * (t + 1) * P].bitcast(FP4X4),
+                        sums[:, c - lo : c - lo + n], lhsT=w_q[w][:, a, 2 * t * P : 2 * (t + 1) * P].bitcast(FP4X4),
                         lhsT_scale=w_s[w][:, a, cols],
-                        rhs=codes[:, first + c : first + c + n].bitcast(FP8X4), rhs_scale=scales[:, first + c : first + c + n],
-                        start=False, stop=(a == 1 and c + n == width),
+                        rhs=codes[:, first : first + n].bitcast(FP8X4), rhs_scale=scales[:, first : first + n],
+                        start=False, stop=(a == 1 and c + n == hi),
                     )
-            if w == 1:
-                res = ring.tile([P, width], F32, name="cand", tag="cand", bufs=4)
-                nc.scalar.activation(res[:], bank[:], ACT.Tanh, bias=bias_n[:, t : t + 1])
+            res = own("gate%d_%d_%d" % (w, t, lo), [hi - lo]) if into is None else into
+            if w == CAND:
+                nc.scalar.activation(res[:], sums[:], ACT.Tanh, bias=bias_n[:, t : t + 1])
             else:
-                if step in hold_tags:
-                    res = keep.tile([P, width], F32, name="hold", tag=hold_tags[step], align_bytes=64)
-                else:
-                    res = ring.tile([P, width], F32, name="hold", tag="hold", bufs=3)
-                nc.scalar.activation(res[:], bank[:], ACT.Sigmoid, bias=neg_bz[:, t : t + 1], scale=-1.0)
+                nc.scalar.activation(res[:], sums[:], ACT.Sigmoid, bias=neg_bz[:, t : t + 1], scale=-1.0)
             return res
 
-        cands, holds = {}, {}
-        last = len(STEPS) - 1
+        cands, holds, diffs, mixes = {}, {}, {}, {}
 
-        hold_tags = {0: "page2", 1: "hold1", 2: "hold2", last: "last_hold"}
-        term_tags = {1: "state2", 3: "late1"}
-        weighted_tags = {1: "raw1", last: "last_weighted"}
-        diffs, terms, mixes = {}, {}, {}
+        def gates(step):
+            cands[step] = gate(CAND, step)
+            holds[step] = gate(HOLD, step)
 
-        def window(step):
-            t, lo, hi = STEPS[step]
-            return state[t][:].indirect(offsets[:, lo // 16 : hi // 16])
+        def listed(tile, lo, hi):
+            return tile[:].indirect(offsets[:, lo // 16 : hi // 16])
 
-        def own(tag, width=HALF):
-            return keep.tile([P, width], F32, name="diff", tag=tag, align_bytes=64)
+        def fetch(step, into):
+            t, lo, hi = step
+            diffs[step] = into
+            nc.vector.tensor_copy(diffs[step], listed(state[t], lo, hi))
 
-        def fetch_diff(step, diff):
-            diffs[step] = diff
-            nc.vector.tensor_tensor(diff, window(step), cands[step][:], ALU.subtract)
+        def fetch_diff(step, into=None):
+            t, lo, hi = step
+            diffs[step] = own("diff%d_%d" % (t, lo), [hi - lo])[:] if into is None else into
+            nc.vector.tensor_tensor(diffs[step], listed(state[t], lo, hi), cands[step][:], ALU.subtract)
 
-        def fetch(step, diff):
-            diffs[step] = diff
-            nc.vector.tensor_copy(diff, window(step))
+        def subtract(step):
+            nc.gpsimd.tensor_tensor(diffs[step], diffs[step], cands[step][:], ALU.subtract)
 
-        def product(step, engine):
-            term = diffs[step]
-            if step in term_tags:
-                term = keep.tile([P, HALF], F32, name="term", tag=term_tags[step], align_bytes=64)[:]
-            engine.tensor_tensor(term, diffs[step], holds[step][:], ALU.mult)
-            terms[step] = term
+        def product(step, engine, into=None):
+            diff = diffs[step]
+            if into is not None:
+                diffs[step] = into
+            engine.tensor_tensor(diffs[step], diff, holds[step][:], ALU.mult)
 
-        def turn(step):
-            t, lo, hi = STEPS[step]
-            cand, term, mix = cands[step], terms[step], diffs[step]
-            if step == 1:
-                mix = behind_rounding[:, 0:HALF]
-            mixes[step] = mix
+        turns = []
+
+        def turn(step, mix=None, back_bank=None, weighted=None):
+            t, lo, hi = step
             blocks = [slice(b, b + P) for b in range(0, hi - lo, P)]
-            turned = psum.tile([P, hi - lo], F32, name="turned", tag="turned")
-            for second, src in enumerate((cand, term)):
+            turns.append(step)
+            turned = bank(4 + len(turns) % 2, [hi - lo])
+            for second, src in enumerate((cands[step][:], diffs[step])):
                 for b, cols in enumerate(blocks):
                     nc.tensor.matmul(
                         turned[:, cols], lhsT=src[:, cols], rhs=ident[:], is_transpose=True,
                         start=(second == 0 and b == 0), stop=(second == 1 and b == len(blocks) - 1),
                     )
-            if step == 2:
-                weighted = behind_rounding[:, HALF:J]
-            elif step in weighted_tags:
-                weighted = keep.tile([P, hi - lo], F32, name="weighted", tag=weighted_tags[step], align_bytes=64)
-            else:
-                weighted = ring.tile([P, hi - lo], F32, name="weighted", tag="weighted")
+            if weighted is None:
+                weighted = ring.tile([P, hi - lo], F32, name="weighted", tag="weighted")[:]
+                weighted = [weighted[:, cols] for cols in blocks]
             for b, cols in enumerate(blocks):
                 block = lo // P + b
-                nc.scalar.activation(weighted[:, cols], turned[:, cols], ACT.Copy, scale=weight_t[:, block : block + 1])
-            back = psum.tile([P, hi - lo], F32, name="back", tag="back", bufs=1)
-            for cols in blocks:
-                nc.tensor.transpose(back[:, cols], weighted[:, cols], ident[:])
-            nc.scalar.copy(mix, back[:])
-
-        spare = ["raw2", "raw3", "state0", "state1", "state2", "raw0"]
-
-        y_s = keep.tile([P, T], U8, name="y_s", align_bytes=64)
-        words_out = out_1[0].rearrange("p t i -> p (t i)").bitcast(I32)
-
-        def emit(lo, hi):
-            c, first = divmod(lo, HALF)
-            cols = slice(first, first + hi - lo)
-            copy, word = (nc.scalar.copy, U32) if c < 2 else (nc.vector.tensor_copy, I32)
-            both = pairs[c // 2][:, c % 2].rearrange("p u c e -> p u (c e)").bitcast(word).rearrange("p u c -> p c u")
-            rounded = keep.tile([P, hi - lo, PACK], BF16, name="rounded%d" % lo, tag=spare.pop(), align_bytes=64)
-            copy(rounded[:].bitcast(word), both[:, cols])
-            y_w = keep.tile([P, hi - lo], U32, name="y_w%d" % lo, align_bytes=64)
-            nc.vector.quantize_mx(y_w[:].bitcast(FP8X4), y_s[:, lo:hi], rounded[:].rearrange("p c t -> p (c t)"))
-            nc.sync.dma_start(words_out[:, lo:hi], y_w[:].bitcast(I32))
+                nc.scalar.activation(weighted[b], turned[:, cols], ACT.Copy, scale=weight_t[:, block : block + 1])
+            back = bank(back_bank, [hi - lo])
+            for b, cols in enumerate(blocks):
+                nc.tensor.transpose(back[:, cols], weighted[b], ident[:])
+            mixes[step] = diffs[step] if mix is None else mix
+            nc.scalar.copy(mixes[step], back[:])
 
         def place(step):
-            t, lo, hi = STEPS[step]
-            nc.vector.tensor_copy(page[t][:].indirect(offsets[:, lo // 16 : hi // 16]), mixes[step])
+            t, lo, hi = step
+            nc.vector.tensor_copy(listed(page[t], lo, hi), mixes[step])
             if hi == J:
                 nc.sync.dma_start(out_0.rearrange("(p t) c -> t p c", t=PACK)[t], page[t][:])
 
-        def round_page(t):
-            u, e = divmod(t, 2)
-            for c in (2, 3, 0, 1):
-                src = page[t][:, c * HALF : (c + 1) * HALF]
-                dst = pairs[c // 2][:, c % 2, u]
-                if c < 2:
-                    nc.scalar.copy(dst[:, :, e], src)
-                elif t == 3:
-                    nc.vector.tensor_copy(dst[:, :, e], src)
-                elif t == 2:
-                    nc.gpsimd.tensor_scalar(dst, src.unsqueeze(2).to_broadcast([P, HALF, 2]), 1.0, 0.0, ALU.mult, ALU.add)
-                else:
-                    nc.gpsimd.tensor_scalar(dst[:, :, e], src, 1.0, 0.0, ALU.mult, ALU.add)
+        early = [(t, 0, HALF) for t in ORDER]
+        late = [(t, HALF, J) for t in ORDER]
 
-        def gates(step):
-            cands[step] = gate(1, step)
-            holds[step] = gate(0, step)
+        for k in range(3):
+            gates(early[k])
+            fetch(late[k], own("late%d" % k, [HALF])[:])
+            fetch_diff(early[k])
+            if k == 0:
+                product(early[0], nc.vector)
+                clear_page(1, "gate0_2_0")
+                turn(early[0], None, 7)
+        place(early[0])
+        clear_page(3, "state0")
+        cands[early[3]] = gate(CAND, early[3])
+        quantize_late()
+        product(early[1], nc.gpsimd, own("state1", [HALF])[:])
+        product(early[2], nc.gpsimd)
+        pairs = own("pairs", [PACK * 2 * HALF * 2], BF16)[:].rearrange("p (c u j e) -> p c u j e", c=PACK, u=2, e=2)
 
-        gates(0)
-        fetch(4, own("diff4")[:])
-        gates(1)
-        fetch_diff(0, own("diff0")[:])
-        product(0, nc.vector)
-        clear_page(2)
-        turn(0)
-        gates(2)
-        fetch(5, own("diff5")[:])
-        fetch_diff(1, own("diff1")[:])
-        gates(3)
-        fetch(6, own("diff6")[:])
-        fetch_diff(2, own("diff2")[:])
-        product(1, nc.gpsimd)
-        quantize_x((nc.scalar.copy, nc.scalar.copy), 0, HALF, keep, "late0", 1)
-        quantize_x((nc.scalar.copy, nc.scalar.copy), 1, HALF, keep, "late1", 1)
-        behind_rounding = own("raw3", J)
-        turn(1)
-        product(2, nc.gpsimd)
-        turn(2)
-        both = own("hold2", J)
-        fetch(7, both[:, HALF:J])
-        fetch_diff(3, both[:, 0:HALF])
-        gates(4)
-        product(3, nc.gpsimd)
-        turn(3)
-        for step in range(PACK, len(STEPS)):
-            if step < last:
-                gates(step + 1)
-            nc.gpsimd.tensor_tensor(diffs[step], diffs[step], cands[step][:], ALU.subtract)
-            product(step, nc.gpsimd)
-            turn(step)
-        for step in range(len(STEPS)):
+        def room(c, u):
+            return pairs[:, c, u].rearrange("p c e -> p (c e)").bitcast(F32)
+
+        behind = own("u_raw0", [7, HALF])
+        fetch(late[3], behind[:, 1])
+        fetch_diff(early[3], behind[:, 0])
+        turn(early[1], behind[:, 2], 6, [behind[:, 4, b * P : (b + 1) * P] for b in range(PACK)])
+        cands[late[0]] = gate(CAND, late[0])
+        holds[late[0]] = gate(HOLD, late[0], room(0, 1))
+        holds[early[3]] = gate(HOLD, early[3], behind[:, 6])
+        turn(early[2], behind[:, 3], 7, [behind[:, 5, b * P : (b + 1) * P] for b in range(PACK)])
+        for k in range(3):
+            if k < 2:
+                gates(late[k + 1])
+            else:
+                cands[late[3]] = gate(CAND, late[3], room(3, 1))
+                holds[late[3]] = gate(HOLD, late[3], room(2, 1))
+            subtract(late[k])
+            product(late[k], nc.gpsimd)
+            turn(late[k], None, 6 + k % 2)
+        product(early[3], nc.gpsimd, room(0, 1))
+        subtract(late[3])
+        product(late[3], nc.gpsimd, room(1, 1))
+        turn(early[3], behind[:, 0], 7)
+        turn(late[3], behind[:, 1], 6, [room(b, 0)[:, 0:P] for b in range(PACK)])
+        mixes[3, 0, J] = behind[:, 0:2].rearrange("p h c -> p (h c)")
+        for step in early[1:3] + late[:3] + [(3, 0, J)]:
             place(step)
-        pairs = [keep.tile([P, 2, 2, HALF, 2], BF16, name="pairs", tag=tag, align_bytes=64) for tag in ("last_weighted", "last_hold")]
-        for t in range(PACK):
-            round_page(t)
-        for lo, hi in ((J, J + QUARTER), (J + QUARTER, J + HALF), (J + HALF, T), (0, HALF), (HALF, HALF + QUARTER), (HALF + QUARTER, 2 * HALF)):
-            emit(lo, hi)
 
-        for r in range(4):
-            nc.scalar.dma_start(out_2[0, r:16:4, :].bitcast(I32), y_s[r:P:32, :].bitcast(I32))
+        woven = [own(tag, [2, HALF, PACK], BF16) for tag in ("state2", "tab_w")]
+
+        def block(t, c):
+            return page[t][:, c * HALF : (c + 1) * HALF]
+
+        for t in ORDER[:3]:
+            u, e = divmod(t, 2)
+            for c in range(PACK):
+                if c == 0 and t < 2:
+                    nc.scalar.copy(pairs[:, c, u, :, e], block(t, c))
+                else:
+                    gpsimd_round(pairs[:, c, u, :, e], block(t, c))
+        for h in range(2):
+            nc.scalar.copy(
+                woven[h][:].bitcast(U32),
+                pairs[:, 2 * h : 2 * h + 2].rearrange("p g u c e -> p g u (c e)").bitcast(U32).rearrange("p g u c -> p g c u"),
+            )
+
+        y_s = own("y_s", [2, HALF], U8)
+        words_out = out_1[0].rearrange("p t i -> p (t i)").bitcast(I32)
+        for c in range(PACK):
+            copy = nc.vector.tensor_copy if c < 2 else nc.scalar.copy
+            copy(woven[c // 2][:, c % 2, :, 3], block(3, c))
+        for c in range(PACK):
+            h, g = divmod(c, 2)
+            y_w = own("y_w%d" % c, [HALF], U32)
+            nc.vector.quantize_mx(y_w[:].bitcast(FP8X4), y_s[4 * h : P, g], woven[h][:, g].rearrange("p c t -> p (c t)"))
+            nc.sync.dma_start(words_out[:, c * HALF : (c + 1) * HALF], y_w[:].bitcast(I32))
+        for q in range(4):
+            nc.scalar.dma_start(
+                out_2[0, 4 * q : 4 * q + 4, :].rearrange("r (h j) -> h r j", h=2).bitcast(I32),
+                y_s[32 * q : 32 * q + 8].rearrange("p g j -> p (g j)").bitcast(I32),
+            )

@@ -25,6 +25,7 @@ QUARTER = 256
 TAB_ROW = 4
 CAND, HOLD = 1, 0
 ORDER = (2, 0, 1, 3)
+OWN = 768
 
 
 def tile_list_tgn_emaP_kernel(
@@ -54,14 +55,15 @@ def tile_list_tgn_emaP_kernel(
         weight_t = own("weight_t", [J // P])
         weight_rows = own("weight_rows", [P])
         ident = own("ident", [P])
-        page = {2: own("page2", [T])}
+        page = {t: own("page%d" % t, [T]) for t in ORDER[:2]}
 
         nc.gpsimd.memset(tab_s[:].bitcast(I32), 0)
         for w in (CAND, HOLD):
             nc.vector.memset(w_s_raw[w][:].rearrange("p a n -> p (a n)").bitcast(I32), 0)
         nc.vector.memset(bias_rows[:], 0.0)
         nc.vector.memset(weight_rows[:], 0.0)
-        nc.vector.memset(page[2][:].bitcast(I32), 0)
+        for t in ORDER[:2]:
+            nc.vector.memset(page[t][:].bitcast(I32), 0)
 
         def clear_page(t, tag):
             page[t] = own(tag, [T])
@@ -174,29 +176,31 @@ def tile_list_tgn_emaP_kernel(
             x_q[a, lo] = quantize(grouped, name) + (0,)
 
         def quantize_late():
-            grouped = own("x_late_grouped", [PACK * J], BF16)
-            round_x(nc.scalar.copy, grouped, 0, x_late, 0, HALF - P)
-            round_x(gpsimd_round, grouped, 0, x_late, HALF - P, HALF)
+            grouped = own("x_late_grouped", [PACK * HALF], BF16)
+            round_x(nc.scalar.copy, grouped, 0, x_late, 0, HALF)
+            x_q[0, HALF] = quantize(grouped, "x_late") + (0,)
+
+        def quantize_last():
+            grouped = own("x_last_grouped", [PACK * HALF], BF16)
             for k in range(2):
-                round_x(nc.scalar.copy, grouped, HALF + k * QUARTER, x_last[:, k], 0, QUARTER)
-            codes, scales = quantize(grouped, "x_late", J)
-            for a in range(2):
-                x_q[a, HALF] = (codes, scales, a * HALF)
+                round_x(nc.scalar.copy, grouped, k * QUARTER, x_last[:, k], 0, QUARTER)
+            x_q[1, HALF] = quantize(grouped, "x_last") + (0,)
 
         u_q = {CAND: quantize(round_u(CAND), "un")}
         deal_words(CAND)
         deal_scales(CAND)
         u_q[HOLD] = quantize(round_u(HOLD), "uz")
         x_late = load_x("u_raw1", 0, HALF, J)
-        x_last = own("u_raw0", [2, PACK, QUARTER])
-        for k in range(2):
-            load_rows(x_last[:, k], x[KP : 2 * KP, HALF + k * QUARTER : HALF + (k + 1) * QUARTER])
+
         deal_words(HOLD)
         deal_scales(HOLD)
         quantize_half(x_first[0], 0, 0, 256)
-        quantize_half(x_first[1], 1, 0, 160)
-        clear_page(0, "x1_0_grouped")
         load_state(3, "x_first0")
+        quantize_half(x_first[1], 1, 0, 160)
+        clear_page(1, "x1_0_grouped")
+        x_last = own("x_first1", [2, PACK, QUARTER])
+        for k in range(2):
+            load_rows(x_last[:, k], x[KP : 2 * KP, HALF + k * QUARTER : HALF + (k + 1) * QUARTER])
         gate_banks = []
 
         def gate(w, step, into=None):
@@ -223,7 +227,8 @@ def tile_list_tgn_emaP_kernel(
             if w == CAND:
                 nc.scalar.activation(res[:], sums[:], ACT.Tanh, bias=bias_n[:, t : t + 1])
             else:
-                nc.scalar.activation(res[:], sums[:], ACT.Sigmoid, bias=neg_bz[:, t : t + 1], scale=-1.0)
+                src = sums[:] if len(res.shape) == 2 else sums[:].rearrange("p (r j) -> p r j", r=res.shape[1])
+                nc.scalar.activation(res[:], src, ACT.Sigmoid, bias=neg_bz[:, t : t + 1], scale=-1.0)
             return res
 
         cands, holds, diffs, mixes = {}, {}, {}, {}
@@ -245,8 +250,11 @@ def tile_list_tgn_emaP_kernel(
             diffs[step] = own("diff%d_%d" % (t, lo), [hi - lo])[:] if into is None else into
             nc.vector.tensor_tensor(diffs[step], listed(state[t], lo, hi), cands[step][:], ALU.subtract)
 
-        def subtract(step):
-            nc.gpsimd.tensor_tensor(diffs[step], diffs[step], cands[step][:], ALU.subtract)
+        def subtract(step, into=None):
+            values = diffs[step]
+            if into is not None:
+                diffs[step] = into
+            nc.gpsimd.tensor_tensor(diffs[step], values, cands[step][:], ALU.subtract)
 
         def product(step, engine, into=None):
             diff = diffs[step]
@@ -256,7 +264,9 @@ def tile_list_tgn_emaP_kernel(
 
         turns = []
 
-        def turn(step, mix=None, back_bank=None, weighted=None):
+        scaled = {}
+
+        def turn_in(step, weighted=None):
             t, lo, hi = step
             blocks = [slice(b, b + P) for b in range(0, hi - lo, P)]
             turns.append(step)
@@ -273,9 +283,12 @@ def tile_list_tgn_emaP_kernel(
             for b, cols in enumerate(blocks):
                 block = lo // P + b
                 nc.scalar.activation(weighted[b], turned[:, cols], ACT.Copy, scale=weight_t[:, block : block + 1])
-            back = bank(back_bank, [hi - lo])
-            for b, cols in enumerate(blocks):
-                nc.tensor.transpose(back[:, cols], weighted[b], ident[:])
+            scaled[step] = weighted
+
+        def turn_out(step, back_bank, mix=None):
+            back = bank(back_bank, [step[2] - step[1]])
+            for b, block in enumerate(scaled[step]):
+                nc.tensor.transpose(back[:, b * P : (b + 1) * P], block, ident[:])
             mixes[step] = diffs[step] if mix is None else mix
             nc.scalar.copy(mixes[step], back[:])
 
@@ -288,79 +301,112 @@ def tile_list_tgn_emaP_kernel(
         early = [(t, 0, HALF) for t in ORDER]
         late = [(t, HALF, J) for t in ORDER]
 
+        pairs = own("pairs", [2 * T * 2], BF16)[:].rearrange("p (u j e) -> p u j e", u=2, e=2)
+
+        def room(c, u):
+            return pairs[:, u, c * HALF : (c + 1) * HALF].rearrange("p j e -> p (j e)").bitcast(F32)
+
+        def quarters(tile):
+            return [tile[:, b * P : (b + 1) * P] for b in range(PACK)]
+
         for k in range(3):
-            gates(early[k])
+            cands[early[k]] = gate(CAND, early[k], room(k, 1))
+            holds[early[k]] = gate(HOLD, early[k], room(3, 1) if k == 2 else None)
             fetch(late[k], own("late%d" % k, [HALF])[:])
             fetch_diff(early[k])
             if k == 0:
                 product(early[0], nc.vector)
-                clear_page(1, "gate0_2_0")
-                turn(early[0], None, 7)
+                clear_page(3, "gate0_2_0")
+                turn_in(early[0])
+                turn_out(early[0], 7)
         place(early[0])
-        clear_page(3, "state0")
         cands[early[3]] = gate(CAND, early[3])
         quantize_late()
         product(early[1], nc.gpsimd, own("state1", [HALF])[:])
         product(early[2], nc.gpsimd)
-        pairs = own("pairs", [PACK * 2 * HALF * 2], BF16)[:].rearrange("p (c u j e) -> p c u j e", c=PACK, u=2, e=2)
-
-        def room(c, u):
-            return pairs[:, c, u].rearrange("p c e -> p (c e)").bitcast(F32)
-
-        behind = own("u_raw0", [7, HALF])
-        fetch(late[3], behind[:, 1])
-        fetch_diff(early[3], behind[:, 0])
-        turn(early[1], behind[:, 2], 6, [behind[:, 4, b * P : (b + 1) * P] for b in range(PACK)])
-        cands[late[0]] = gate(CAND, late[0])
-        holds[late[0]] = gate(HOLD, late[0], room(0, 1))
-        holds[early[3]] = gate(HOLD, early[3], behind[:, 6])
-        turn(early[2], behind[:, 3], 7, [behind[:, 5, b * P : (b + 1) * P] for b in range(PACK)])
-        for k in range(3):
-            if k < 2:
-                gates(late[k + 1])
-            else:
-                cands[late[3]] = gate(CAND, late[3], room(3, 1))
-                holds[late[3]] = gate(HOLD, late[3], room(2, 1))
-            subtract(late[k])
-            product(late[k], nc.gpsimd)
-            turn(late[k], None, 6 + k % 2)
-        product(early[3], nc.gpsimd, room(0, 1))
-        subtract(late[3])
-        product(late[3], nc.gpsimd, room(1, 1))
-        turn(early[3], behind[:, 0], 7)
-        turn(late[3], behind[:, 1], 6, [room(b, 0)[:, 0:P] for b in range(PACK)])
-        mixes[3, 0, J] = behind[:, 0:2].rearrange("p h c -> p (h c)")
-        for step in early[1:3] + late[:3] + [(3, 0, J)]:
+        holds[early[3]] = gate(HOLD, early[3])
+        fetched = own("u_raw1", [3, HALF])
+        fetch_diff(early[3], fetched[:, 0])
+        fetch(late[3], fetched[:, 1])
+        turn_in(early[1], quarters(fetched[:, 2]))
+        quantize_last()
+        behind = own("x_first1", [3, HALF])
+        last_mix = own("last_mix", [J])
+        product(early[3], nc.gpsimd, own("x_last_grouped", [HALF])[:])
+        turn_out(early[1], 6, behind[:, 0])
+        turn_in(early[2], quarters(behind[:, 2]))
+        gates(late[0])
+        subtract(late[0])
+        product(late[0], nc.gpsimd)
+        turn_out(early[2], 7, behind[:, 1])
+        turn_in(early[3])
+        gates(late[1])
+        subtract(late[1])
+        product(late[1], nc.gpsimd)
+        turn_out(early[3], 6, last_mix[:, 0:HALF])
+        turn_in(late[0])
+        gates(late[2])
+        subtract(late[2], holds[late[1]][:])
+        product(late[2], nc.gpsimd)
+        turn_out(late[0], 7)
+        turn_in(late[1])
+        spread = pairs.rearrange("p u (c j) e -> p (u c) (j e)", c=PACK).bitcast(F32)[:, :, 0 : HALF // 8]
+        cands[late[3]] = gate(CAND, late[3])
+        holds[late[3]] = gate(HOLD, late[3], spread)
+        subtract(late[3], holds[late[2]][:])
+        eighths = diffs[late[3]].rearrange("p (r j) -> p r j", r=8)
+        nc.gpsimd.tensor_tensor(eighths, eighths, spread, ALU.mult)
+        turn_out(late[1], 6)
+        turn_in(late[2], quarters(room(0, 1))[1:] + quarters(room(1, 1))[1:2])
+        turn_out(late[2], 7)
+        turn_in(late[3], quarters(room(0, 0)))
+        turn_out(late[3], 6, last_mix[:, HALF:J])
+        mixes[3, 0, QUARTER] = last_mix[:, 0:QUARTER]
+        mixes[3, QUARTER, J] = last_mix[:, QUARTER:J]
+        for step in early[1:3] + [(3, 0, QUARTER)] + late[:3] + [(3, QUARTER, J)]:
             place(step)
 
-        woven = [own(tag, [2, HALF, PACK], BF16) for tag in ("state2", "tab_w")]
+        woven = own("state2", [T * PACK], BF16)[:].rearrange("p (j i) -> p j i", i=PACK)
 
-        def block(t, c):
-            return page[t][:, c * HALF : (c + 1) * HALF]
+        def round_plane(copy, t, lo, hi):
+            copy(pairs[:, t // 2, lo:hi, t % 2], page[t][:, lo:hi])
 
-        for t in ORDER[:3]:
-            u, e = divmod(t, 2)
-            for c in range(PACK):
-                if c == 0 and t < 2:
-                    nc.scalar.copy(pairs[:, c, u, :, e], block(t, c))
-                else:
-                    gpsimd_round(pairs[:, c, u, :, e], block(t, c))
-        for h in range(2):
-            nc.scalar.copy(
-                woven[h][:].bitcast(U32),
-                pairs[:, 2 * h : 2 * h + 2].rearrange("p g u c e -> p g u (c e)").bitcast(U32).rearrange("p g u c -> p g c u"),
-            )
+        def weave(copy, word, lo, hi):
+            both = pairs.rearrange("p u j e -> p u (j e)").bitcast(word).rearrange("p u j -> p j u")
+            copy(woven.bitcast(word)[:, lo:hi], both[:, lo:hi])
+
+        ahead = ((OWN, J), (J, J + HALF), (J + HALF, T))
+        round_plane(nc.scalar.copy, 2, 0, J)
+        for lo, hi in ahead[1:]:
+            round_plane(gpsimd_round, 2, lo, hi)
+        for t in (0, 1):
+            round_plane(nc.scalar.copy, t, 0, HALF)
+            for lo in (HALF, J, J + HALF):
+                round_plane(gpsimd_round, t, lo, lo + HALF)
+        for lo, hi in ahead:
+            weave(nc.scalar.copy, U32, lo, hi)
 
         y_s = own("y_s", [2, HALF], U8)
         words_out = out_1[0].rearrange("p t i -> p (t i)").bitcast(I32)
-        for c in range(PACK):
-            copy = nc.vector.tensor_copy if c < 2 else nc.scalar.copy
-            copy(woven[c // 2][:, c % 2, :, 3], block(3, c))
-        for c in range(PACK):
+
+        def emit(lo, hi):
+            c, start = divmod(lo, HALF)
             h, g = divmod(c, 2)
-            y_w = own("y_w%d" % c, [HALF], U32)
-            nc.vector.quantize_mx(y_w[:].bitcast(FP8X4), y_s[4 * h : P, g], woven[h][:, g].rearrange("p c t -> p (c t)"))
-            nc.sync.dma_start(words_out[:, c * HALF : (c + 1) * HALF], y_w[:].bitcast(I32))
+            y_w = own("y_w%d" % lo, [hi - lo], U32)
+            nc.vector.quantize_mx(
+                y_w[:].bitcast(FP8X4), y_s[4 * h : P, g, start : start + hi - lo], woven[:, lo:hi].rearrange("p j i -> p (j i)")
+            )
+            nc.sync.dma_start(words_out[:, lo:hi], y_w[:].bitcast(I32))
+
+        own_pieces = ((0, OWN // 2), (OWN // 2, OWN))
+        for lo, hi in own_pieces:
+            round_plane(nc.vector.tensor_copy, 3, lo, hi)
+        for lo, hi in own_pieces:
+            weave(nc.vector.tensor_copy, I32, lo, hi)
+        for lo, hi in ahead[:2] + ((J + HALF, T - QUARTER), (T - QUARTER, T)):
+            nc.scalar.copy(woven[:, lo:hi, 3], page[3][:, lo:hi])
+        for lo, hi in ((0, QUARTER), (QUARTER, HALF), (HALF, J), (J, J + HALF), (J + HALF, T - QUARTER), (T - QUARTER, T)):
+            emit(lo, hi)
         for q in range(4):
             nc.scalar.dma_start(
                 out_2[0, 4 * q : 4 * q + 4, :].rearrange("r (h j) -> h r j", h=2).bitcast(I32),

@@ -25,7 +25,7 @@ QUARTER = 256
 TAB_ROW = 4
 CAND, HOLD = 1, 0
 ORDER = (2, 0, 1, 3)
-OWN = 768
+OWN = 896
 
 
 def tile_list_tgn_emaP_kernel(
@@ -250,11 +250,8 @@ def tile_list_tgn_emaP_kernel(
             diffs[step] = own("diff%d_%d" % (t, lo), [hi - lo])[:] if into is None else into
             nc.vector.tensor_tensor(diffs[step], listed(state[t], lo, hi), cands[step][:], ALU.subtract)
 
-        def subtract(step, into=None):
-            values = diffs[step]
-            if into is not None:
-                diffs[step] = into
-            nc.gpsimd.tensor_tensor(diffs[step], values, cands[step][:], ALU.subtract)
+        def subtract(step):
+            nc.gpsimd.tensor_tensor(diffs[step], diffs[step], cands[step][:], ALU.subtract)
 
         def product(step, engine, into=None):
             diff = diffs[step]
@@ -331,7 +328,6 @@ def tile_list_tgn_emaP_kernel(
         turn_in(early[1], quarters(fetched[:, 2]))
         quantize_last()
         behind = own("x_first1", [3, HALF])
-        last_mix = own("last_mix", [J])
         product(early[3], nc.gpsimd, own("x_last_grouped", [HALF])[:])
         turn_out(early[1], 6, behind[:, 0])
         turn_in(early[2], quarters(behind[:, 2]))
@@ -343,27 +339,25 @@ def tile_list_tgn_emaP_kernel(
         gates(late[1])
         subtract(late[1])
         product(late[1], nc.gpsimd)
-        turn_out(early[3], 6, last_mix[:, 0:HALF])
+        turn_out(early[3], 6)
         turn_in(late[0])
         gates(late[2])
-        subtract(late[2], holds[late[1]][:])
+        subtract(late[2])
         product(late[2], nc.gpsimd)
         turn_out(late[0], 7)
         turn_in(late[1])
         spread = pairs.rearrange("p u (c j) e -> p (u c) (j e)", c=PACK).bitcast(F32)[:, :, 0 : HALF // 8]
         cands[late[3]] = gate(CAND, late[3])
         holds[late[3]] = gate(HOLD, late[3], spread)
-        subtract(late[3], holds[late[2]][:])
+        subtract(late[3])
         eighths = diffs[late[3]].rearrange("p (r j) -> p r j", r=8)
         nc.gpsimd.tensor_tensor(eighths, eighths, spread, ALU.mult)
         turn_out(late[1], 6)
-        turn_in(late[2], quarters(room(0, 1))[1:] + quarters(room(1, 1))[1:2])
+        turn_in(late[2])
         turn_out(late[2], 7)
-        turn_in(late[3], quarters(room(0, 0)))
-        turn_out(late[3], 6, last_mix[:, HALF:J])
-        mixes[3, 0, QUARTER] = last_mix[:, 0:QUARTER]
-        mixes[3, QUARTER, J] = last_mix[:, QUARTER:J]
-        for step in early[1:3] + [(3, 0, QUARTER)] + late[:3] + [(3, QUARTER, J)]:
+        turn_in(late[3], [quarters(room(c, u))[1] for c, u in ((0, 1), (3, 0), (2, 0), (2, 1))])
+        turn_out(late[3], 6)
+        for step in early[1:] + late:
             place(step)
 
         woven = own("state2", [T * PACK], BF16)[:].rearrange("p (j i) -> p j i", i=PACK)
@@ -375,16 +369,13 @@ def tile_list_tgn_emaP_kernel(
             both = pairs.rearrange("p u j e -> p u (j e)").bitcast(word).rearrange("p u j -> p j u")
             copy(woven.bitcast(word)[:, lo:hi], both[:, lo:hi])
 
-        ahead = ((OWN, J), (J, J + HALF), (J + HALF, T))
-        round_plane(nc.scalar.copy, 2, 0, J)
-        for lo, hi in ahead[1:]:
-            round_plane(gpsimd_round, 2, lo, hi)
+        own_pieces = ((0, OWN // 2), (OWN // 2, OWN))
+        other_pieces = ((OWN, J + QUARTER), (J + QUARTER, T - QUARTER), (T - QUARTER, T))
+        round_plane(nc.scalar.copy, 2, 0, OWN)
+        round_plane(nc.scalar.copy, 2, OWN, T)
         for t in (0, 1):
-            round_plane(nc.scalar.copy, t, 0, HALF)
-            for lo in (HALF, J, J + HALF):
-                round_plane(gpsimd_round, t, lo, lo + HALF)
-        for lo, hi in ahead:
-            weave(nc.scalar.copy, U32, lo, hi)
+            round_plane(gpsimd_round, t, 0, OWN)
+            round_plane(nc.scalar.copy, t, OWN, T)
 
         y_s = own("y_s", [2, HALF], U8)
         words_out = out_1[0].rearrange("p t i -> p (t i)").bitcast(I32)
@@ -398,14 +389,16 @@ def tile_list_tgn_emaP_kernel(
             )
             nc.sync.dma_start(words_out[:, lo:hi], y_w[:].bitcast(I32))
 
-        own_pieces = ((0, OWN // 2), (OWN // 2, OWN))
         for lo, hi in own_pieces:
             round_plane(nc.vector.tensor_copy, 3, lo, hi)
         for lo, hi in own_pieces:
             weave(nc.vector.tensor_copy, I32, lo, hi)
-        for lo, hi in ahead[:2] + ((J + HALF, T - QUARTER), (T - QUARTER, T)):
-            nc.scalar.copy(woven[:, lo:hi, 3], page[3][:, lo:hi])
-        for lo, hi in ((0, QUARTER), (QUARTER, HALF), (HALF, J), (J, J + HALF), (J + HALF, T - QUARTER), (T - QUARTER, T)):
+        round_plane(nc.scalar.copy, 3, *other_pieces[0])
+        for k, piece in enumerate(other_pieces):
+            if k + 1 < len(other_pieces):
+                round_plane(nc.scalar.copy, 3, *other_pieces[k + 1])
+            weave(nc.scalar.copy, U32, *piece)
+        for lo, hi in ((0, QUARTER), (QUARTER, HALF), (HALF, J), (J, J + QUARTER), (J + QUARTER, J + HALF), (J + HALF, T - QUARTER), (T - QUARTER, T)):
             emit(lo, hi)
         for q in range(4):
             nc.scalar.dma_start(

@@ -25,7 +25,9 @@ QUARTER = 256
 TAB_ROW = 4
 CAND, HOLD = 1, 0
 ORDER = (2, 0, 1, 3)
-OWN = 896
+OWN = 960
+SHARE = 832
+FILLED = 1408
 
 
 def tile_list_tgn_emaP_kernel(
@@ -355,7 +357,7 @@ def tile_list_tgn_emaP_kernel(
         turn_out(late[1], 6)
         turn_in(late[2])
         turn_out(late[2], 7)
-        turn_in(late[3], [quarters(room(c, u))[1] for c, u in ((0, 1), (3, 0), (2, 0), (2, 1))])
+        turn_in(late[3], [quarters(room(c, u))[1] for c, u in ((3, 1), (3, 0), (2, 0))] + quarters(room(2, 0))[2:3])
         turn_out(late[3], 6)
         for step in early[1:] + late:
             place(step)
@@ -365,29 +367,35 @@ def tile_list_tgn_emaP_kernel(
         def round_plane(copy, t, lo, hi):
             copy(pairs[:, t // 2, lo:hi, t % 2], page[t][:, lo:hi])
 
+        def fill_words(copy, t, lo, hi):
+            copy(pairs[:, t // 2, lo:hi], page[t][:, lo:hi].unsqueeze(2).to_broadcast([P, hi - lo, 2]))
+
         def weave(copy, word, lo, hi):
             both = pairs.rearrange("p u j e -> p u (j e)").bitcast(word).rearrange("p u j -> p j u")
             copy(woven.bitcast(word)[:, lo:hi], both[:, lo:hi])
 
         own_pieces = ((0, OWN // 2), (OWN // 2, OWN))
         other_pieces = ((OWN, J + QUARTER), (J + QUARTER, T - QUARTER), (T - QUARTER, T))
-        round_plane(nc.scalar.copy, 2, 0, OWN)
-        round_plane(nc.scalar.copy, 2, OWN, T)
+        fill_words(gpsimd_round, 2, 0, FILLED)
+        round_plane(nc.scalar.copy, 2, FILLED, T)
+        fill_words(gpsimd_round, 0, 0, SHARE)
+        round_plane(gpsimd_round, 1, 0, SHARE)
         for t in (0, 1):
-            round_plane(gpsimd_round, t, 0, OWN)
-            round_plane(nc.scalar.copy, t, OWN, T)
+            round_plane(nc.scalar.copy, t, SHARE, T)
 
         y_s = own("y_s", [2, HALF], U8)
+        y_w = own("y_w", [T], U32)
         words_out = out_1[0].rearrange("p t i -> p (t i)").bitcast(I32)
 
         def emit(lo, hi):
             c, start = divmod(lo, HALF)
             h, g = divmod(c, 2)
-            y_w = own("y_w%d" % lo, [hi - lo], U32)
             nc.vector.quantize_mx(
-                y_w[:].bitcast(FP8X4), y_s[4 * h : P, g, start : start + hi - lo], woven[:, lo:hi].rearrange("p j i -> p (j i)")
+                y_w[:, lo:hi].bitcast(FP8X4), y_s[4 * h : P, g, start : start + hi - lo], woven[:, lo:hi].rearrange("p j i -> p (j i)")
             )
-            nc.sync.dma_start(words_out[:, lo:hi], y_w[:].bitcast(I32))
+            if hi % HALF == 0 or hi == T - QUARTER:
+                lo = hi - HALF if hi <= J + HALF else lo
+                nc.sync.dma_start(words_out[:, lo:hi], y_w[:, lo:hi].bitcast(I32))
 
         for lo, hi in own_pieces:
             round_plane(nc.vector.tensor_copy, 3, lo, hi)

@@ -25,9 +25,8 @@ QUARTER = 256
 TAB_ROW = 4
 CAND, HOLD = 1, 0
 ORDER = (2, 0, 1, 3)
-OWN = 960
-SHARE = 832
-FILLED = 1408
+SHARE = 1216
+FILLED = 1536
 
 
 def tile_list_tgn_emaP_kernel(
@@ -357,7 +356,7 @@ def tile_list_tgn_emaP_kernel(
         turn_out(late[1], 6)
         turn_in(late[2])
         turn_out(late[2], 7)
-        turn_in(late[3], [quarters(room(c, u))[1] for c, u in ((3, 1), (3, 0), (2, 0))] + quarters(room(2, 0))[2:3])
+        turn_in(late[3], quarters(room(3, 1))[1:2] + quarters(room(0, 0))[1:])
         turn_out(late[3], 6)
         for step in early[1:] + late:
             place(step)
@@ -374,42 +373,42 @@ def tile_list_tgn_emaP_kernel(
             both = pairs.rearrange("p u j e -> p u (j e)").bitcast(word).rearrange("p u j -> p j u")
             copy(woven.bitcast(word)[:, lo:hi], both[:, lo:hi])
 
-        own_pieces = ((0, OWN // 2), (OWN // 2, OWN))
-        other_pieces = ((OWN, J + QUARTER), (J + QUARTER, T - QUARTER), (T - QUARTER, T))
+        other_pieces = [(lo, lo + QUARTER) for c in (1, 3) for lo in (c * HALF, c * HALF + QUARTER)]
         fill_words(gpsimd_round, 2, 0, FILLED)
         round_plane(nc.scalar.copy, 2, FILLED, T)
-        fill_words(gpsimd_round, 0, 0, SHARE)
-        round_plane(gpsimd_round, 1, 0, SHARE)
+        fill_words(gpsimd_round, 0, SHARE, T)
+        round_plane(gpsimd_round, 1, SHARE, T)
         for t in (0, 1):
-            round_plane(nc.scalar.copy, t, SHARE, T)
+            round_plane(nc.scalar.copy, t, 0, SHARE)
 
-        y_s = own("y_s", [2, HALF], U8)
+        y_s = own("y_s", [HALF], U8)
         y_w = own("y_w", [T], U32)
         words_out = out_1[0].rearrange("p t i -> p (t i)").bitcast(I32)
 
         def emit(lo, hi):
             c, start = divmod(lo, HALF)
-            h, g = divmod(c, 2)
             nc.vector.quantize_mx(
-                y_w[:, lo:hi].bitcast(FP8X4), y_s[4 * h : P, g, start : start + hi - lo], woven[:, lo:hi].rearrange("p j i -> p (j i)")
+                y_w[:, lo:hi].bitcast(FP8X4), y_s[4 * c : P, start : start + hi - lo], woven[:, lo:hi].rearrange("p j i -> p (j i)")
             )
-            if hi % HALF == 0 or hi == T - QUARTER:
-                lo = hi - HALF if hi <= J + HALF else lo
-                nc.sync.dma_start(words_out[:, lo:hi], y_w[:, lo:hi].bitcast(I32))
+            if hi % HALF == 0:
+                nc.sync.dma_start(words_out[:, hi - HALF : hi], y_w[:, hi - HALF : hi].bitcast(I32))
 
-        for lo, hi in own_pieces:
-            round_plane(nc.vector.tensor_copy, 3, lo, hi)
-        for lo, hi in own_pieces:
-            weave(nc.vector.tensor_copy, I32, lo, hi)
         round_plane(nc.scalar.copy, 3, *other_pieces[0])
         for k, piece in enumerate(other_pieces):
             if k + 1 < len(other_pieces):
                 round_plane(nc.scalar.copy, 3, *other_pieces[k + 1])
             weave(nc.scalar.copy, U32, *piece)
-        for lo, hi in ((0, QUARTER), (QUARTER, HALF), (HALF, J), (J, J + QUARTER), (J + QUARTER, J + HALF), (J + HALF, T - QUARTER), (T - QUARTER, T)):
-            emit(lo, hi)
+        for lo in (0, J):
+            round_plane(nc.vector.tensor_copy, 3, lo, lo + HALF)
+        for lo in (0, QUARTER):
+            weave(nc.vector.tensor_copy, I32, lo, lo + QUARTER)
+        for lo in (0, QUARTER):
+            emit(lo, lo + QUARTER)
+        weave(nc.vector.tensor_copy, I32, J, J + HALF)
+        for lo in range(HALF, T, QUARTER):
+            emit(lo, lo + QUARTER)
         for q in range(4):
             nc.scalar.dma_start(
-                out_2[0, 4 * q : 4 * q + 4, :].rearrange("r (h j) -> h r j", h=2).bitcast(I32),
-                y_s[32 * q : 32 * q + 8].rearrange("p g j -> p (g j)").bitcast(I32),
+                out_2[0, 4 * q : 4 * q + 4, :].rearrange("r (c j) -> c r j", c=PACK).bitcast(I32),
+                y_s[32 * q : 32 * q + 16].bitcast(I32),
             )

@@ -153,12 +153,13 @@ def tile_list_tgn_emaP_kernel(
         def grouped_tile():
             return ring.tile([P, PACK * HALF], BF16, name="grouped", tag="grouped", align_bytes=64)
 
-        def round_u(w):
+        def round_u(w, split):
             grouped = grouped_tile()
-            nc.scalar.copy(
-                grouped[:].rearrange("p (t m i) -> p m t i", t=PACK, i=PACK),
-                u_raw[w][:].rearrange("p i (m t) -> p m t i", t=PACK),
-            )
+            dealt = grouped[:].rearrange("p (t m i) -> p m t i", t=PACK, i=PACK)
+            raw = u_raw[w][:].rearrange("p i (m t) -> p m t i", t=PACK)
+            nc.scalar.copy(dealt[:, :split], raw[:, :split])
+            if split < P:
+                nc.vector.tensor_copy(dealt[:, split:], raw[:, split:])
             return grouped
 
         def round_x(copy, grouped, at, raw, c0, c1):
@@ -187,10 +188,10 @@ def tile_list_tgn_emaP_kernel(
                 round_x(nc.scalar.copy, grouped, k * QUARTER, x_last[:, k], 0, QUARTER)
             x_q[1, HALF] = quantize(grouped, "x_last") + (0,)
 
-        u_q = {CAND: quantize(round_u(CAND), "un")}
+        u_q = {CAND: quantize(round_u(CAND, P), "un")}
         deal_words(CAND)
         deal_scales(CAND)
-        u_q[HOLD] = quantize(round_u(HOLD), "uz")
+        u_q[HOLD] = quantize(round_u(HOLD, 80), "uz")
         x_late = load_x("u_raw1", 0, HALF, J)
 
         deal_words(HOLD)

from contextlib import ExitStack

import concourse.mybir as mybir
from concourse.masks import make_identity

K, M, N, T, J = 1024, 512, 512, 2048, 1024
FLOPS = 2 * 2 * (K + M) * N * J

F32 = mybir.dt.float32
BF16 = mybir.dt.bfloat16
I32 = mybir.dt.int32
U32 = mybir.dt.uint32
U16 = mybir.dt.uint16
U8 = mybir.dt.uint8
FP8X4 = mybir.dt.float8_e4m3fn_x4
FP4X4 = mybir.dt.float4_e2m1fn_x4
ACT = mybir.ActivationFunctionType
ALU = mybir.AluOpType

P = 128
PACK = 4
KP = P * PACK
HALF = 512
QUARTER = 256
TAB_ROW = 4
CAND, HOLD = 1, 0
ORDER = (2, 0, 1, 3)
SHARE = 1216
FILLED = 1536


def tile_list_tgn_emaP_kernel(
    tc, x, tab_words, tab_scales, wz_words, wz_scales, uz, wn_words, wn_scales, un, bz, bn, hT, wgo, offs,
    out_0, out_1, out_2,
):
    nc = tc.nc
    with ExitStack() as ctx:
        keep = ctx.enter_context(tc.tile_pool(name="keep", bufs=1))
        ring = ctx.enter_context(tc.tile_pool(name="ring", bufs=2))
        psum = ctx.enter_context(tc.psum_pool(name="psum", bufs=1))

        def own(tag, shape, dtype=F32):
            return keep.tile([P] + shape, dtype, name=tag, tag=tag, align_bytes=64)

        def bank(k, shape):
            return psum.tile([P] + shape, F32, name="bank%d" % k, tag="bank%d" % k)

        offsets = keep.tile([P, J // 16], U16, name="offsets")
        tab_s = own("tab_s", [T], U8)
        tab_w = own("tab_w", [T], U32)
        w_s_raw = [own("w_s_raw%d" % w, [2, N], U8) for w in range(2)]
        w_raw = [own("w_raw%d" % w, [2, 2 * N], U8) for w in range(2)]
        bias_n = own("bias_n", [PACK])
        neg_bz = own("neg_bz", [PACK])
        bias_rows = own("bias_rows", [N])
        weight_t = own("weight_t", [J // P])
        weight_rows = own("weight_rows", [P])
        ident = own("ident", [P])
        page = {t: own("page%d" % t, [T]) for t in ORDER[:2]}

        nc.gpsimd.memset(tab_s[:].bitcast(I32), 0)
        for w in (CAND, HOLD):
            nc.vector.memset(w_s_raw[w][:].rearrange("p a n -> p (a n)").bitcast(I32), 0)
        nc.vector.memset(bias_rows[:], 0.0)
        nc.vector.memset(weight_rows[:], 0.0)
        for t in ORDER[:2]:
            nc.vector.memset(page[t][:].bitcast(I32), 0)

        def clear_page(t, tag):
            page[t] = own(tag, [T])
            nc.gpsimd.memset(page[t][:], 0.0)

        make_identity(nc, ident[:])
        warm = own("warm", [1])
        nc.scalar.activation(warm[:], ident[:, 0:1], ACT.Sigmoid)

        def load_rows(dst, rows):
            nc.sync.dma_start(dst, rows.rearrange("(p i) c -> p i c", i=PACK))

        state = {}

        def load_state(t, tag):
            state[t] = own(tag, [T])
            nc.sync.dma_start(state[t][:], hT.rearrange("(p t) c -> t p c", t=PACK)[t])

        def load_x(tag, a, lo, hi):
            raw = own(tag, [PACK, hi - lo])
            load_rows(raw[:], x[a * KP : (a + 1) * KP, lo:hi])
            return raw

        def load_w_scales(w, queue):
            for q in range(4):
                queue.dma_start(
                    w_s_raw[w][q:P:32].bitcast(I32),
                    (wz_scales, wn_scales)[w][:, q:16:4, :].rearrange("a r n -> r a n").bitcast(I32),
                )

        nc.sync.dma_start(offsets[:], offs)
        nc.sync.dma_start(tab_w[:].bitcast(I32), tab_words[0].rearrange("p t i -> p (t i)").bitcast(I32))
        for q in range(4):
            nc.sync.dma_start(tab_s[TAB_ROW + q : P : 32, :].bitcast(I32), tab_scales[0, q:16:4, :].bitcast(I32))
        u_raw = {w: own("u_raw%d" % w, [PACK, N]) for w in (CAND, HOLD)}
        load_w_scales(CAND, nc.gpsimd)
        for w in (CAND, HOLD):
            load_rows(u_raw[w][:], (uz, un)[w])
            nc.sync.dma_start(bias_rows[1 - w : 2 - w, :], (bz, bn)[w].unsqueeze(0))
            nc.sync.dma_start(w_raw[w][:].bitcast(I32), (wz_words, wn_words)[w].rearrange("a p b -> p a b").bitcast(I32))
        load_w_scales(HOLD, nc.sync)
        x_first = [load_x("x_first%d" % a, a, 0, HALF) for a in range(2)]
        for t in ORDER[:3]:
            load_state(t, "state%d" % t)
            if t == ORDER[1]:
                nc.sync.dma_start(weight_rows[0 : J // P, :], wgo[0].rearrange("(b p) -> b p", p=P))

        bias_bank = bank(4, [PACK, P])
        for t in range(PACK):
            nc.tensor.transpose(bias_bank[:, t, :], bias_rows[:, t:N:PACK], ident[:])
        nc.scalar.copy(bias_n[:], bias_bank[:, :, 0])
        nc.scalar.mul(neg_bz[:], bias_bank[:, :, 1], -1.0)
        weight_bank = bank(6, [P])
        nc.tensor.transpose(weight_bank[:], weight_rows[:], ident[:])
        nc.scalar.copy(weight_t[:], weight_bank[:, 0 : J // P])

        picked_w = own("picked_w", [J], U32)
        picked_s = own("picked_s", [J], U8)
        nc.vector.tensor_copy(picked_w[:], tab_w[:].indirect(offsets[:]))
        nc.vector.tensor_copy(picked_s[:], tab_s[:].indirect(offsets[:]))

        w_q = [own("w_q%d" % w, [2, 2 * N], U8) for w in range(2)]
        w_s = [own("w_s%d" % w, [2, N], U8) for w in range(2)]

        def deal_words(w):
            nc.vector.tensor_copy(
                w_q[w][:].bitcast(U16).rearrange("p a (t m) -> p a t m", t=PACK),
                w_raw[w][:].bitcast(U16).rearrange("p a (m t) -> p a t m", t=PACK),
            )

        def deal_scales(w):
            nc.vector.tensor_copy(
                w_s[w][:].rearrange("p a (t m) -> p a t m", t=PACK),
                w_s_raw[w][:].rearrange("p a (m t) -> p a t m", t=PACK),
            )

        def quantize(grouped, name, width=HALF):
            codes = own(name + "_q", [width], U32)
            scales = own(name + "_s", [width], U8)
            nc.vector.quantize_mx(codes[:].bitcast(FP8X4), scales[:], grouped[:])
            return codes, scales

        def gpsimd_round(dst, src):
            nc.gpsimd.tensor_scalar(dst, src, 1.0, 0.0, ALU.mult, ALU.add)

        def grouped_tile():
            return ring.tile([P, PACK * HALF], BF16, name="grouped", tag="grouped", align_bytes=64)

        def round_u(w, split):
            grouped = grouped_tile()
            dealt = grouped[:].rearrange("p (t m i) -> p m t i", t=PACK, i=PACK)
            raw = u_raw[w][:].rearrange("p i (m t) -> p m t i", t=PACK)
            nc.scalar.copy(dealt[:, :split], raw[:, :split])
            if split < P:
                nc.vector.tensor_copy(dealt[:, split:], raw[:, split:])
            return grouped

        def round_x(copy, grouped, at, raw, c0, c1):
            copy(
                grouped[:, PACK * (at + c0) : PACK * (at + c1)].rearrange("p (c e i) -> p c i e", e=4, i=PACK),
                raw[:, :, c0:c1].rearrange("p i (c e) -> p c i e", e=4),
            )

        x_q = {}

        def quantize_half(raw, a, lo, split):
            name = "x%d_%d" % (a, lo)
            grouped = own(name + "_grouped", [PACK * HALF], BF16)
            round_x(nc.scalar.copy, grouped, 0, raw, 0, split)
            round_x(nc.vector.tensor_copy, grouped, 0, raw, split, HALF)
            x_q[a, lo] = quantize(grouped, name) + (0,)

        def quantize_late():
            grouped = own("x_late_grouped", [PACK * HALF], BF16)
            round_x(nc.scalar.copy, grouped, 0, x_late, 0, HALF)
            x_q[0, HALF] = quantize(grouped, "x_late") + (0,)

        def quantize_last():
            grouped = own("x_last_grouped", [PACK * HALF], BF16)
            for k in range(2):
                round_x(nc.scalar.copy, grouped, k * QUARTER, x_last[:, k], 0, QUARTER)
            x_q[1, HALF] = quantize(grouped, "x_last") + (0,)

        u_q = {CAND: quantize(round_u(CAND, P), "un")}
        deal_words(CAND)
        deal_scales(CAND)
        u_q[HOLD] = quantize(round_u(HOLD, 80), "uz")
        x_late = load_x("u_raw1", 0, HALF, J)

        deal_words(HOLD)
        deal_scales(HOLD)
        quantize_half(x_first[0], 0, 0, 256)
        load_state(3, "x_first0")
        quantize_half(x_first[1], 1, 0, 160)
        clear_page(1, "x1_0_grouped")
        x_last = own("x_first1", [2, PACK, QUARTER])
        for k in range(2):
            load_rows(x_last[:, k], x[KP : 2 * KP, HALF + k * QUARTER : HALF + (k + 1) * QUARTER])
        gate_banks = []

        def gate(w, step, into=None):
            t, lo, hi = step
            gate_banks.append(len(gate_banks) % 4)
            sums = bank(gate_banks[-1], [hi - lo])
            cols = slice(t * P, (t + 1) * P)
            nc.tensor.matmul_mx(
                sums[:], lhsT=u_q[w][0][:, cols].bitcast(FP8X4), lhsT_scale=u_q[w][1][:, cols],
                rhs=picked_w[:, lo:hi].bitcast(FP8X4), rhs_scale=picked_s[TAB_ROW:P, lo:hi],
                start=True, stop=False,
            )
            n = HALF
            for a in range(2):
                for c in range(lo, hi, n):
                    codes, scales, first = x_q[a, c]
                    nc.tensor.matmul_mx(
                        sums[:, c - lo : c - lo + n], lhsT=w_q[w][:, a, 2 * t * P : 2 * (t + 1) * P].bitcast(FP4X4),
                        lhsT_scale=w_s[w][:, a, cols],
                        rhs=codes[:, first : first + n].bitcast(FP8X4), rhs_scale=scales[:, first : first + n],
                        start=False, stop=(a == 1 and c + n == hi),
                    )
            res = own("gate%d_%d_%d" % (w, t, lo), [hi - lo]) if into is None else into
            if w == CAND:
                nc.scalar.activation(res[:], sums[:], ACT.Tanh, bias=bias_n[:, t : t + 1])
            else:
                src = sums[:] if len(res.shape) == 2 else sums[:].rearrange("p (r j) -> p r j", r=res.shape[1])
                nc.scalar.activation(res[:], src, ACT.Sigmoid, bias=neg_bz[:, t : t + 1], scale=-1.0)
            return res

        cands, holds, diffs, mixes = {}, {}, {}, {}

        def gates(step):
            cands[step] = gate(CAND, step)
            holds[step] = gate(HOLD, step)

        def listed(tile, lo, hi):
            return tile[:].indirect(offsets[:, lo // 16 : hi // 16])

        def fetch(step, into):
            t, lo, hi = step
            diffs[step] = into
            nc.vector.tensor_copy(diffs[step], listed(state[t], lo, hi))

        def fetch_diff(step, into=None):
            t, lo, hi = step
            diffs[step] = own("diff%d_%d" % (t, lo), [hi - lo])[:] if into is None else into
            nc.vector.tensor_tensor(diffs[step], listed(state[t], lo, hi), cands[step][:], ALU.subtract)

        def subtract(step):
            nc.gpsimd.tensor_tensor(diffs[step], diffs[step], cands[step][:], ALU.subtract)

        def product(step, engine, into=None):
            diff = diffs[step]
            if into is not None:
                diffs[step] = into
            engine.tensor_tensor(diffs[step], diff, holds[step][:], ALU.mult)

        turns = []

        scaled = {}

        def turn_in(step, weighted=None):
            t, lo, hi = step
            blocks = [slice(b, b + P) for b in range(0, hi - lo, P)]
            turns.append(step)
            turned = bank(4 + len(turns) % 2, [hi - lo])
            for second, src in enumerate((cands[step][:], diffs[step])):
                for b, cols in enumerate(blocks):
                    nc.tensor.matmul(
                        turned[:, cols], lhsT=src[:, cols], rhs=ident[:], is_transpose=True,
                        start=(second == 0 and b == 0), stop=(second == 1 and b == len(blocks) - 1),
                    )
            if weighted is None:
                weighted = ring.tile([P, hi - lo], F32, name="weighted", tag="weighted")[:]
                weighted = [weighted[:, cols] for cols in blocks]
            for b, cols in enumerate(blocks):
                block = lo // P + b
                nc.scalar.activation(weighted[b], turned[:, cols], ACT.Copy, scale=weight_t[:, block : block + 1])
            scaled[step] = weighted

        def turn_out(step, back_bank, mix=None):
            back = bank(back_bank, [step[2] - step[1]])
            for b, block in enumerate(scaled[step]):
                nc.tensor.transpose(back[:, b * P : (b + 1) * P], block, ident[:])
            mixes[step] = diffs[step] if mix is None else mix
            nc.scalar.copy(mixes[step], back[:])

        def place(step):
            t, lo, hi = step
            nc.vector.tensor_copy(listed(page[t], lo, hi), mixes[step])
            if hi == J:
                nc.sync.dma_start(out_0.rearrange("(p t) c -> t p c", t=PACK)[t], page[t][:])

        early = [(t, 0, HALF) for t in ORDER]
        late = [(t, HALF, J) for t in ORDER]

        pairs = own("pairs", [2 * T * 2], BF16)[:].rearrange("p (u j e) -> p u j e", u=2, e=2)

        def room(c, u):
            return pairs[:, u, c * HALF : (c + 1) * HALF].rearrange("p j e -> p (j e)").bitcast(F32)

        def quarters(tile):
            return [tile[:, b * P : (b + 1) * P] for b in range(PACK)]

        for k in range(3):
            cands[early[k]] = gate(CAND, early[k], room(k, 1))
            holds[early[k]] = gate(HOLD, early[k], room(3, 1) if k == 2 else None)
            fetch(late[k], own("late%d" % k, [HALF])[:])
            fetch_diff(early[k])
            if k == 0:
                product(early[0], nc.vector)
                clear_page(3, "gate0_2_0")
                turn_in(early[0])
                turn_out(early[0], 7)
        place(early[0])
        cands[early[3]] = gate(CAND, early[3])
        quantize_late()
        product(early[1], nc.gpsimd, own("state1", [HALF])[:])
        product(early[2], nc.gpsimd)
        holds[early[3]] = gate(HOLD, early[3])
        fetched = own("u_raw1", [3, HALF])
        fetch_diff(early[3], fetched[:, 0])
        fetch(late[3], fetched[:, 1])
        turn_in(early[1], quarters(fetched[:, 2]))
        quantize_last()
        behind = own("x_first1", [3, HALF])
        product(early[3], nc.gpsimd, own("x_last_grouped", [HALF])[:])
        turn_out(early[1], 6, behind[:, 0])
        turn_in(early[2], quarters(behind[:, 2]))
        gates(late[0])
        subtract(late[0])
        product(late[0], nc.gpsimd)
        turn_out(early[2], 7, behind[:, 1])
        turn_in(early[3])
        gates(late[1])
        subtract(late[1])
        product(late[1], nc.gpsimd)
        turn_out(early[3], 6)
        turn_in(late[0])
        gates(late[2])
        subtract(late[2])
        product(late[2], nc.gpsimd)
        turn_out(late[0], 7)
        turn_in(late[1])
        spread = pairs.rearrange("p u (c j) e -> p (u c) (j e)", c=PACK).bitcast(F32)[:, :, 0 : HALF // 8]
        cands[late[3]] = gate(CAND, late[3])
        holds[late[3]] = gate(HOLD, late[3], spread)
        subtract(late[3])
        eighths = diffs[late[3]].rearrange("p (r j) -> p r j", r=8)
        nc.gpsimd.tensor_tensor(eighths, eighths, spread, ALU.mult)
        turn_out(late[1], 6)
        turn_in(late[2])
        turn_out(late[2], 7)
        turn_in(late[3], quarters(room(3, 1))[1:2] + quarters(room(0, 0))[1:])
        turn_out(late[3], 6)
        for step in early[1:] + late:
            place(step)

        woven = own("state2", [T * PACK], BF16)[:].rearrange("p (j i) -> p j i", i=PACK)

        def round_plane(copy, t, lo, hi):
            copy(pairs[:, t // 2, lo:hi, t % 2], page[t][:, lo:hi])

        def fill_words(copy, t, lo, hi):
            copy(pairs[:, t // 2, lo:hi], page[t][:, lo:hi].unsqueeze(2).to_broadcast([P, hi - lo, 2]))

        def weave(copy, word, lo, hi):
            both = pairs.rearrange("p u j e -> p u (j e)").bitcast(word).rearrange("p u j -> p j u")
            copy(woven.bitcast(word)[:, lo:hi], both[:, lo:hi])

        other_pieces = [(lo, lo + QUARTER) for c in (1, 3) for lo in (c * HALF, c * HALF + QUARTER)]
        fill_words(gpsimd_round, 2, 0, FILLED)
        round_plane(nc.scalar.copy, 2, FILLED, T)
        fill_words(gpsimd_round, 0, SHARE, T)
        round_plane(gpsimd_round, 1, SHARE, T)
        for t in (0, 1):
            round_plane(nc.scalar.copy, t, 0, SHARE)

        y_s = own("y_s", [HALF], U8)
        y_w = own("y_w", [T], U32)
        words_out = out_1[0].rearrange("p t i -> p (t i)").bitcast(I32)

        def emit(lo, hi):
            c, start = divmod(lo, HALF)
            nc.vector.quantize_mx(
                y_w[:, lo:hi].bitcast(FP8X4), y_s[4 * c : P, start : start + hi - lo], woven[:, lo:hi].rearrange("p j i -> p (j i)")
            )
            if hi % HALF == 0:
                nc.sync.dma_start(words_out[:, hi - HALF : hi], y_w[:, hi - HALF : hi].bitcast(I32))

        round_plane(nc.scalar.copy, 3, *other_pieces[0])
        for k, piece in enumerate(other_pieces):
            if k + 1 < len(other_pieces):
                round_plane(nc.scalar.copy, 3, *other_pieces[k + 1])
            weave(nc.scalar.copy, U32, *piece)
        for lo in (0, J):
            round_plane(nc.vector.tensor_copy, 3, lo, lo + HALF)
        for lo in (0, QUARTER):
            weave(nc.vector.tensor_copy, I32, lo, lo + QUARTER)
        for lo in (0, QUARTER):
            emit(lo, lo + QUARTER)
        weave(nc.vector.tensor_copy, I32, J, J + HALF)
        for lo in range(HALF, T, QUARTER):
            emit(lo, lo + QUARTER)
        for q in range(4):
            nc.scalar.dma_start(
                out_2[0, 4 * q : 4 * q + 4, :].rearrange("r (c j) -> c r j", c=PACK).bitcast(I32),
                y_s[32 * q : 32 * q + 16].bitcast(I32),
            )
